import numpy as np, ml_dtypes
CORES = [6,15,38,47]
N = 4
BF = ml_dtypes.bfloat16
def gentries(a):
    return np.ascontiguousarray(a.reshape(8, 16, -1).transpose(0, 2, 1)).reshape(8, -1)
def gtable(e):
    e = np.asarray(e); return np.ascontiguousarray(e.reshape(8, -1, 16).transpose(0, 2, 1)).reshape(128, -1).astype(np.int32)
W, LN, RO, BL, LG = 4096, 64, 4, 16, 12
SZ = W // LN
DIST = 1 + (np.arange(LN) // BL) % (N - 1)
ROT = (np.arange(16)[:, None] + np.arange(16)[None, :]) % 16
PAT = 255 * np.array([0, 0, 0, 0, 1, 0, 0, 1, 1, 0, 1, 0, 1, 1, 1, 1])
def parts(rng):
    x = rng.integers(0, 256, (N, 8, 16, W)); L = rng.integers(0, W, (N, 8, LN, 16)); c = rng.integers(0, W, (N, 8, LN))
    s = rng.choice(np.array([1.0, 1.3, 1.6]), (N, 8, LN, 1))
    z = np.minimum(np.maximum(np.rint(127.5 + s * (255 * rng.random((N, 8, LN, 16)) - 127.5)), 0), 255).astype(np.int64)
    return x, L, c, z
def mid(rng, x, z, q):
    a = rng.integers(0, W, 512); b = rng.integers(0, LN, 512)
    zz = np.roll(z[:, :, b, :], 5, axis=3).transpose(0, 1, 3, 2)
    d = np.sort(np.sum(np.abs(x[:, :, :, a] - zz), axis=2), axis=2)
    return np.minimum(np.maximum(np.take_along_axis(d, (q * 512).astype(np.int64)[:, :, None], 2)[:, :, 0], 1275), 2295)
def pack(x, L, c, z, t):
    return {"x": x.reshape(N, 128, W).astype(np.float32).astype(BF), "ls": np.stack([gtable(a) for a in L]), "an": c.astype(np.int32),
            "z": np.ascontiguousarray(z.transpose(0, 1, 3, 2)).reshape(N, 128, LN).astype(np.float32).astype(BF), "th": t.reshape(N, 8, 1).astype(np.int32)}
def setup_inputs(rng):
    x, L, c, z = parts(rng)
    return pack(x, L, c, z, mid(rng, x, z, rng.choice(np.array([0.15, 0.22, 0.3, 0.4]), (N, 8))))
def rough(rng, shape, share):
    e = np.minimum(np.exp2(8.1 * rng.random(shape)).astype(np.int64) - 1, 255)
    return np.where(rng.random(shape) < share, 255 - e, e)
def setup_inputs_spread(rng):
    sh = np.array([0.2, 0.5, 0.8])
    x = rough(rng, (N, 8, 16, W), rng.choice(sh, (N, 8, 1, W))); z = rough(rng, (N, 8, LN, 16), rng.choice(sh, (N, 8, LN, 1)))
    e = np.exp2(LG * rng.random((N, 8, LN, 17))).astype(np.int64) - 1
    e = np.where(rng.random(e.shape) < 0.5, W - 1 - e, e)
    return pack(x, e[..., :16], e[..., 16], z, mid(rng, x, z, 0.05 + 0.9 * rng.random((N, 8))))
def setup_inputs_ends(rng):
    sh = np.array([0.3, 0.5, 0.7])
    x = 255 * (rng.random((N, 8, 16, W)) < rng.choice(sh, (N, 8, 1, W))).astype(np.int64)
    z = 255 * (rng.random((N, 8, LN, 16)) < rng.choice(sh, (N, 8, LN, 1))).astype(np.int64)
    L = (W - 1) * (rng.random((N, 8, LN, 16)) < rng.choice(np.array([0.25, 0.5, 0.75]), (N, 8, LN, 1))).astype(np.int64)
    c = (W - 1) * rng.integers(0, 2, (N, 8, LN))
    t = np.where(rng.random((N, 8)) < 0.5, 1275, 2295); t[:, 2] = 1275; t[:, 5] = 2295
    x[:, 1::2, :, 0] = 255; x[:, 1::2, :, W - 1] = 0
    for l, a, b in ((0, 0, 0), (1, W - 1, 0), (2, 0, 255), (3, W - 1, 255), (LN - 4, 0, 0), (LN - 3, W - 1, 255), (LN - 2, W - 1, 0), (LN - 1, 0, 255)):
        L[:, 1::2, l] = 0; c[:, 1::2, l] = a; z[:, 1::2, l] = b
    return pack(x, L, c, z, t)
def setup_inputs_corners(rng):
    x, L, c, z = parts(rng); t = rng.choice(np.array([1275, 1400, 1600, 1800]), (N, 8))
    cnt = np.minimum(np.array([0, 1, 31, 32, 33, LN - 1, LN, 9]), LN)
    for q in range(N):
        order = np.arange(8) if q == 0 else rng.permutation(8)
        for g in range(8):
            hot = rng.permutation(LN) < cnt[order[g]]
            for l in range(LN):
                m = int(rng.choice(np.array([16, 16, 15, 9, 17]))) if hot[l] else int(rng.choice(np.array([8, 8, 1, 0])))
                col = SZ * l + 8 + int(rng.integers(0, 16)); kk = int(rng.choice(np.array([0, 15, int(rng.integers(0, 16))]))) if m == 16 else 0
                zz = np.full(16, 255) if m == 17 else np.roll(PAT, int(rng.integers(0, 16)))
                x[q, g][:, [col - 6, col + 1, col + 6]] = rng.integers(120, 136, (16, 3))
                x[q, g, :, col] = rng.integers(120, 136, 16) if m == 0 else np.roll(zz, -kk)
                c[q, g, l] = col; z[q, g, l] = zz
                L[q, g, l] = 0 if m in (0, 16, 17) else np.where(rng.permutation(16) < m, 0, 6)
    return pack(x, L, c, z, t)
def setup_inputs_ties(rng):
    x, L, c, z = parts(rng); t = mid(rng, x, z, rng.choice(np.array([0.2, 0.3, 0.4]), (N, 8)))
    t[:, ::2] = rng.integers(1275, 2296, (N, 4)); t[0, 0] = 1275; t[N - 1, 6] = 2295
    s = t[:, ::2, None] + rng.integers(-1, 2, (N, 4, LN)); up = rng.random((N, 4, LN)) < 0.5; m = rng.random((N, 4, LN)) < 0.6
    v = (s // 16)[:, :, None, :] + (np.arange(16)[:, None] < (s % 16)[:, :, None, :])
    v = np.where(up[:, :, None, :], 255 - v, v); col = SZ * np.arange(LN) + rng.integers(0, SZ, (N, 4, LN))
    xe = x[:, ::2]; np.put_along_axis(xe, np.repeat(col[:, :, None, :], 16, axis=2), v, 3)
    L[:, ::2] = np.where(m[..., None], 0, L[:, ::2]); c[:, ::2] = np.where(m, col, c[:, ::2]); z[:, ::2] = np.where(m[..., None], 255 * up[..., None], z[:, ::2])
    L[:, 1] = L[:, 1, :1].copy(); c[:, 1] = c[:, 1, :1].copy(); z[:, 1] = z[:, 1][:, np.arange(LN) % 2]
    L[:, 3] = 0; c[:, 3] = W - 1; c[1::2, 3, LN - 1] = 0
    L[:, 5] = rng.choice(np.array([0, 3, W // 2, W - 1]), (N, LN, 16))
    x[:, 7, :, 1::2] = x[:, 7, :, ::2].copy(); L[:, 7, 1::2] = L[:, 7, ::2].copy(); c[:, 7, 1::2] = c[:, 7, ::2].copy()
    return pack(x, L, c, z, t)
def check_inputs(d):
    bad = []
    for k, lo, hi in (("x", 0, 255), ("ls", 0, W - 1), ("an", 0, W - 1), ("z", 0, 255), ("th", 1275, 2295)):
        v = np.asarray(d[k]).astype(np.float64)
        if not (np.min(v) >= lo and np.max(v) <= hi): bad.append("range of " + k)
        elif np.any(v != np.floor(v)): bad.append("whole numbers in " + k)
    return bad
def reference(x, ls, an, z, th):
    X = x.astype(np.float32).astype(np.int64).reshape(N, 8, 16, W)
    L = np.stack([gentries(a) for a in ls]).astype(np.int64).reshape(N, 8, LN, 16)
    c = an.astype(np.int64)
    Z = z.astype(np.float32).astype(np.int64).reshape(N, 8, 16, LN).transpose(0, 1, 3, 2)
    t = th.astype(np.int64).reshape(N, 8); A = np.zeros((N, 8), np.int64)
    src = ((np.arange(N)[:, None] - DIST[None, :]) % N)[:, None, :]; gg = np.arange(8)[None, :, None]; sl = np.arange(LN)[None, None, :]
    k16 = np.arange(16)
    for rnd in range(RO):
        La = L[:, :, :, ROT]; Li = L[:, :, :, None, :]
        E = (((La * Li) >> 5) + La - Li + c[:, :, :, None, None]) & (W - 1)
        ix = E.reshape(N, 8, LN * 256); D = np.zeros(E.shape, np.int64)
        for f in range(16):
            D = D + np.abs(np.take_along_axis(X[:, :, f], ix, 2).reshape(E.shape) - Z[:, :, :, (f + k16) % 16][..., None])
        C = np.sum(D < (t + (A & 31))[:, :, None, None, None], axis=4)
        kt = np.argmax(C, axis=3); kb = np.argmin(C, axis=3)
        win = np.take_along_axis(E, kt[..., None, None], 3)[:, :, :, 0]
        v = np.take_along_axis(np.take_along_axis(E, kb[..., None, None], 3)[:, :, :, 0], kt[..., None], 3)
        M = np.max(np.take_along_axis(X, np.repeat(win.reshape(N, 8, 1, LN * 16), 16, axis=2), 3).reshape(N, 8, 16, LN, 16), axis=4).transpose(0, 1, 3, 2)
        Y = (M + Z) >> 1
        u = np.sum(Y * (2 * k16 + 1), axis=3) & (W - 1)
        A = np.sum(np.max(C, axis=3) >= 9, axis=2)
        place = SZ * np.arange(LN) + (u & (SZ - 1))
        np.put_along_axis(X, np.repeat(place[:, :, None, :], 16, axis=2), Y.transpose(0, 1, 3, 2), 3)
        c = (((u * u) >> 5) + 37 * u + A[:, :, None]) & (W - 1)
        Z = np.abs(Z - M)
        L = np.where(np.roll(k16 == kb[..., None], 1, axis=0), np.roll(v, 1, axis=0), win)
        L = L[src, gg, sl]; c = c[src, gg, sl]; Z = Z[src, gg, sl]
    return {"yx": X.reshape(N, 128, W).astype(np.float32).astype(BF), "yl": np.stack([gtable(a) for a in L]).astype(np.float32), "ya": c.astype(np.float32),
            "yz": np.ascontiguousarray(Z.transpose(0, 1, 3, 2)).reshape(N, 128, LN).astype(np.float32).astype(BF)}

@@ -1,0 +1,563 @@
+from concourse.bass import DstId, RemoteDMATransfer
+from concourse.mybir import AluOpType as Op, ActivationFunctionType as Act
+
+RO = 4
+ORD = [2, 0, 3, 1]
+NT = 8
+S_T, V_T = 0.224, 0.262
+V_LATE = [2.0, 3.5, 3.5, 3.5]
+NH = [40, 5, 5, 5]
+NV = [14, 0, 0, 0]
+S_BEST = 58
+DMA_TABS = [1, 2, 4, 5, 6]
+TURN_S, TURN_V = 3, 7
+
+SCRATCH = {
+    "tab": ("sbuf", [128, NT * 4096], "bfloat16"),
+    "sd": ("sbuf", [128, 112 * 128], "bfloat16"),
+    "vd": ("sbuf", [128, 96 * 128], "bfloat16"),
+    "vr": ("sbuf", [128, 96 * 128], "bfloat16"),
+    "W": ("sbuf", [128, 1024], "int32"), "E": ("sbuf", [128, 1024], "int32"),
+    "off0": ("sbuf", [128, 512], "uint16"), "off1": ("sbuf", [128, 512], "uint16"),
+    "L16": ("sbuf", [128, 64], "float16"), "B": ("sbuf", [128, 64], "float32"),
+    "C0": ("sbuf", [128, 64], "float32"),
+    "zb": ("sbuf", [128, 64], "bfloat16"), "z8": ("sbuf", [128, 64], "bfloat16"), "zh": ("sbuf", [128, 64], "float32"),
+    "thr": ("sbuf", [128, 512], "float16"), "nT": ("sbuf", [128, 1], "float32"), "ncol": ("sbuf", [128, 1], "float32"),
+    "kA": ("sbuf", [128, 1], "float32"), "Ai": ("sbuf", [128, 1], "int32"), "Aj": ("sbuf", [128, 1], "int32"),
+    "cmp0": ("sbuf", [128, 512], "bfloat16"), "cmp1": ("sbuf", [128, 512], "bfloat16"),
+    "En": ("sbuf", [128, 128], "float32"), "Sc": ("sbuf", [128, 128], "float32"),
+    "hot": ("sbuf", [128, 4], "bfloat16"),
+    "KI": ("sbuf", [128, 8], "int32"), "KJ": ("sbuf", [128, 8], "int32"), "koff": ("sbuf", [128, 8], "uint16"),
+    "EtU": ("sbuf", [128, 64], "uint16"), "OO": ("sbuf", [128, 128], "bfloat16"),
+    "Eb": ("sbuf", [128, 64], "float32"), "Q": ("sbuf", [128, 64], "float16"),
+    "G": ("sbuf", [128, 1024], "bfloat16"), "Ms": ("sbuf", [128, 1024], "bfloat16"),
+    "Yi": ("sbuf", [128, 64], "int32"), "Yb": ("sbuf", [128, 64], "bfloat16"), "Yr": ("sbuf", [128, 512], "bfloat16"),
+    "si": ("sbuf", [128, 64], "int32"), "ui": ("sbuf", [128, 64], "int32"), "u1": ("sbuf", [128, 64], "float32"),
+    "u2": ("sbuf", [128, 64], "float32"), "Wc": ("sbuf", [128, 64], "int32"), "Wd": ("sbuf", [128, 64], "int32"),
+    "w6": ("sbuf", [128, 64], "int32"), "wv": ("sbuf", [128, 64], "float32"), "ws": ("sbuf", [128, 64], "float32"),
+    "woff": ("sbuf", [128, 4], "uint16"),
+    "tm": ("sbuf", [128, 64], "float16"),
+    "Lc": ("sbuf", [128, 32], "float16"),
+    "J": ("sbuf", [128, 16], "int32"), "J2": ("sbuf", [128, 16], "int32"), "tg": ("sbuf", [128, 16], "float32"),
+    "mh": ("sbuf", [128, 128], "bfloat16"), "ms": ("sbuf", [128, 128], "bfloat16"), "lm": ("sbuf", [128, 64], "bfloat16"),
+    "pi": ("sbuf", [128, 1], "int32"), "pj": ("sbuf", [128, 1], "int32"), "pk": ("sbuf", [128, 1], "int32"),
+    "pl": ("sbuf", [128, 1], "int32"),
+    "pif": ("sbuf", [128, 1], "float32"), "pgf": ("sbuf", [128, 1], "float32"), "pff": ("sbuf", [128, 1], "float32"),
+    "pbf": ("sbuf", [128, 1], "float32"), "pwf": ("sbuf", [128, 1], "float32"),
+    "PH": ("sbuf", [128, 16 * 128], "float16"), "PB": ("sbuf", [128, 8 * 128], "bfloat16"),
+    "BDh": ("sbuf", [128, 128], "float16"), "BDb": ("sbuf", [128, 128], "bfloat16"), "WU": ("sbuf", [128, 128], "bfloat16"),
+    "I2": ("sbuf", [128, 128], "bfloat16"), "In": ("sbuf", [128, 128], "bfloat16"),
+    "o8": ("sbuf", [128, 32], "bfloat16"), "sel": ("sbuf", [128, 128], "float32"),
+    "oneh": ("sbuf", [128, 128], "float16"), "c16": ("sbuf", [128, 512], "float16"),
+    "tmi": ("sbuf", [128, 512], "bfloat16"), "tmask": ("sbuf", [128, 512], "float16"),
+    "kmi": ("sbuf", [128, 64], "int32"), "Km": ("sbuf", [128, 64], "float32"), "Kb": ("sbuf", [128, 64], "float32"),
+    "rmask": ("sbuf", [128, 1024], "bfloat16"),
+    "eyi": ("sbuf", [128, 1024], "bfloat16"), "eye": ("sbuf", [128, 1024], "bfloat16"),
+    "lbi": ("sbuf", [128, 64], "int32"), "lb1": ("sbuf", [128, 64], "float32"), "lb": ("sbuf", [128, 64], "float32"),
+    "lsi": ("sbuf", [128, 64], "int32"), "ani": ("sbuf", [128, 64], "int32"), "thi": ("sbuf", [128, 1], "int32"),
+    "anf": ("sbuf", [128, 65], "float32"),
+    "ylf": ("sbuf", [128, 64], "float32"), "yaf": ("sbuf", [128, 64], "float32"), "yzf": ("sbuf", [128, 64], "bfloat16"),
+}
+PS = ["pA0", "pA1", "pD0", "pD1", "pC", "pV", "pU", "pY"]
+for _n in PS:
+    SCRATCH[_n] = ("psum", [128, 512], "float32")
+for _r in range(RO):
+    SCRATCH["SA%d" % _r] = ("sbuf", [128, 160], "float16")
+    SCRATCH["LA%d" % _r] = ("sbuf", [128, 192], "float16")
+    SCRATCH["SB%d" % _r] = ("sbuf", [128, 128], "float32")
+    SCRATCH["LB%d" % _r] = ("sbuf", [128, 128], "float32")
+DM = ["d_ls", "d_an", "d_z", "d_th"] + ["d_x%d" % j for j in range(4)] + ["d_t%d" % k for k in DMA_TABS] + ["d_out"]
+SEMAPHORES = ["sV", "sS", "sP", "sG", "lo"] + DM + ["ra%d" % r for r in range(RO)] + ["rb%d" % r for r in range(RO)]
+MSGA = [(0, 0, 48, 3), (48, 48, 48, 1), (80, 96, 48, 2), (112, 144, 48, 2)]
+MSGB = [(0, 0, 32, 3), (32, 32, 32, 1), (64, 64, 32, 2), (96, 96, 32, 1)]
+
+
+def rank_program(g, core, T, topo):
+    rank = T.rank_of(core)
+    if rank is None:
+        return
+    ENG = {"V": g.vector, "S": g.scalar, "P": g.tensor, "G": g, "Y": g.sync}
+    known = {q: {} for q in ENG}
+    clock = {}
+    total = {}
+    acc = {}
+
+    def t(name, lo=0, hi=None, st=1, p0=0, p1=128, ps=1):
+        if hi is None:
+            hi = SCRATCH[name][1][1]
+        if p0 == 0 and p1 == 128 and ps == 1:
+            ap = T[name][:, lo:hi] if st == 1 else T[name][:, lo:hi:st]
+        else:
+            ap = T[name][p0:p1, lo:hi] if ps == 1 else T[name][p0:p1:ps, lo:hi]
+        return (ap, [(name, lo, hi)])
+
+    def ind(win, off):
+        return (win[0].indirect(off[0]), win[1] + off[1])
+
+    def outside(ap):
+        return (ap, [])
+
+    def need(q, regs, isw):
+        own = "s" + q
+        out = {}
+        for name, lo, hi in regs:
+            ps = name in PS
+            for a, b, sem, val, w in acc.get(name, []):
+                over = a < hi and lo < b
+                if sem == own:
+                    hit = over and w and not isw
+                elif ps:
+                    hit = True
+                else:
+                    hit = over and (w or isw)
+                if hit and known[q].get(sem, 0) < val:
+                    out[sem] = max(out.get(sem, 0), val)
+        return out
+
+    def note(regs, sem, val, isw):
+        for name, lo, hi in regs:
+            lst = [e for e in acc.get(name, []) if not (e[0] >= lo and e[1] <= hi and e[2] == sem and (e[4] == isw))]
+            lst.append((lo, hi, sem, val, isw))
+            acc[name] = lst
+
+    def prepare(q, reads, writes):
+        w = {}
+        for regs, isw in ((reads, False), (writes, True)):
+            for s, v in need(q, regs, isw).items():
+                w[s] = max(w.get(s, 0), v)
+        for s in sorted(w):
+            if any(o != s and clock.get((o, w[o]), {}).get(s, 0) >= w[s] and known[q].get(o, 0) < w[o] for o in w):
+                continue
+            if known[q].get(s, 0) >= w[s]:
+                continue
+            ENG[q].wait_ge(T.sem[s], w[s])
+            k = known[q]
+            for a, b in clock.get((s, w[s]), {}).items():
+                k[a] = max(k.get(a, 0), b)
+            k[s] = max(k.get(s, 0), w[s])
+
+    def finish(q, ins, sem, n, reads, writes):
+        total[sem] = total.get(sem, 0) + n
+        ins.then_inc(T.sem[sem], n)
+        clock[(sem, total[sem])] = dict(known[q])
+        note(reads, sem, total[sem], False)
+        note(writes, sem, total[sem], True)
+
+    def op(q, fn, out, ins, *rest, **kw):
+        reads = []
+        for a in ins:
+            if isinstance(a, tuple):
+                reads = reads + a[1]
+        if "bias" in kw and isinstance(kw["bias"], tuple):
+            reads = reads + kw["bias"][1]
+            kw["bias"] = kw["bias"][0]
+        wr = out[1]
+        if len(wr) > 1:
+            reads = reads + wr[1:]
+            wr = wr[:1]
+        prepare(q, reads, wr)
+        i = fn(out[0], *([a[0] if isinstance(a, tuple) else a for a in ins] + list(rest)), **kw)
+        finish(q, i, "s" + q, 1, reads, wr)
+
+    def tt(out, a, b, o):
+        op("V", g.vector.tensor_tensor, out, [a, b, o])
+
+    def ts(out, a, s1, o1, s2=None, o2=None):
+        if o2 is None:
+            op("V", g.vector.tensor_scalar, out, [a, s1, None, o1])
+        else:
+            op("V", g.vector.tensor_scalar, out, [a, s1, s2, o1, o2])
+
+    def cp(out, a):
+        op("V", g.vector.tensor_copy, out, [a])
+
+    def segmax(out, mask, a):
+        op("V", g.vector.tensor_tensor_scan, out, [mask, a, 0.0, Op.min, Op.max])
+
+    def act(out, a, f, **kw):
+        op("S", g.scalar.activation, out, [a, f], **kw)
+
+    def mm(out, l, r, start=True, stop=True):
+        op("P", g.tensor.matmul, out, [l, r, start, stop])
+
+    def dma(q, sem, out, a, fresh=False):
+        prepare(q, a[1], [] if fresh else out[1])
+        i = ENG[q].dma_start(out[0], a[0])
+        finish(q, i, sem, 16, a[1], out[1])
+
+    for b in range(4):
+        s = 16 * ORD[b]
+        dma("S", "d_ls", t("lsi", 16 * b, 16 * b + 16), outside(T.ls[:, s:s + 16]))
+    for b in range(4):
+        s = 16 * ORD[b]
+        dma("S", "d_an", t("ani", 16 * b, 16 * b + 16, p1=8), outside(T.an[:, s:s + 16]))
+    dma("S", "d_th", t("thi", p1=8), outside(T.th[:, 0:1]))
+    for b in range(4):
+        s = 16 * ORD[b]
+        dma("S", "d_z", t("zb", 16 * b, 16 * b + 16), outside(T.z[:, s:s + 16]))
+    for j in range(4):
+        dma("Y", "d_x%d" % j, t("tab", 1024 * j, 1024 * j + 1024), outside(T.x[:, 1024 * j:1024 * j + 1024]))
+    for k in DMA_TABS:
+        lo, hi = 4096 * k, 4096 * k + 4096
+        for gg in range(8):
+            dma("Y", "d_t%d" % k, t("tab", lo, hi, p0=16 * gg + k, p1=16 * gg + 16), outside(T.x[16 * gg:16 * gg + 16 - k, :]), True)
+        for f in range(k):
+            dma("Y", "d_t%d" % k, t("tab", lo, hi, p0=f, p1=128, ps=16), outside(T.x[16 + f - k::16, :]), True)
+
+    def iota(out, pattern, base, cm, **kw):
+        op("G", g.iota, out, [], pattern, base, cm, **kw)
+
+    SM = {"allow_small_or_imprecise_dtypes": True}
+    iota(t("pi"), [[0, 1]], 0, 1)
+    iota(t("J"), [[-1, 16]], 16, 1)
+    iota(t("mh"), [[1, 128]], 0, 0, **SM)
+    iota(t("ms"), [[1, 8], [0, 16]], 0, 0, **SM)
+    iota(t("tmi"), [[0, 4], [16, 8], [0, 16]], 0, 0, **SM)
+    iota(t("kmi"), [[16, 4], [-64, 16]], 960, 0)
+    iota(t("lm"), [[0, 4], [1, 16]], 0, 0, **SM)
+    iota(t("eyi"), [[-1, 16], [0, 64]], 15, 0, **SM)
+    iota(t("rmask"), [[0, 64], [32767, 16]], 0, 0, **SM)
+    for b in range(4):
+        iota(t("lbi", 16 * b, 16 * b + 16), [[64, 16]], 1024 * ORD[b] - 100000, 0)
+    SH, AND = Op.arith_shift_right, Op.bitwise_and
+    ts(t("pj"), t("pi"), 15, AND)
+    ts(t("pk"), t("pi"), 4, SH)
+    ts(t("pl"), t("pi"), 112, AND)
+    ts(t("J2"), t("J"), 15, AND)
+    cp(t("pif"), t("pi"))
+    cp(t("pff"), t("pj"))
+    cp(t("pgf"), t("pk"))
+    cp(t("pbf"), t("pl"))
+    ts(t("tg"), t("J2"), t("pbf"), Op.add)
+    ts(t("sel", p1=8), t("ms", p1=8), t("pif", p1=8), Op.is_equal)
+    for k in range(16):
+        ts(t("PH", 128 * k, 128 * k + 128), t("mh"), t("tg", k, k + 1), Op.is_equal)
+    ts(t("oneh"), t("mh"), 0.0, Op.mult, 1.0, Op.add)
+    ts(t("c16", p1=32), t("tmi", p1=32), 0.0, Op.mult, 2016.0, Op.add)
+    ts(t("L16"), t("lsi"), -2048.0, Op.add)
+    ts(t("B"), t("lsi"), 32.0, Op.add)
+    cp(t("anf", 0, 64, p1=8), t("ani", p1=8))
+    cp(t("anf", 64, 65, p1=8), t("thi", p1=8))
+    mm(t("pU", 0, 65), t("sel", p1=8), t("anf", p1=8))
+    ts(t("C0"), t("pU", 0, 64), 32.0, Op.mult, 1024.0 - 8388608.0, Op.add)
+    ts(t("nT"), t("pU", 64, 65), -1.0, Op.mult, 1785.0, Op.add)
+    for k in range(8, 16):
+        ts(t("PB", 128 * (k - 8), 128 * (k - 8) + 128), t("mh"), t("tg", k, k + 1), Op.is_equal)
+
+    def perm_b(k):
+        return t("PB", 128 * (k - 8), 128 * (k - 8) + 128)
+
+    def names_pe(h):
+        pa = "pA%d" % h
+        mm(t(pa), t("oneh", p1=1), t("c16", p1=1), True, False)
+        for k in range(8):
+            mm(t(pa, 64 * k, 64 * k + 64), t("PH", 128 * (8 * h + k), 128 * (8 * h + k) + 128), t("L16"), False, k == 7)
+
+    def names_mul(h):
+        for k in range(8):
+            sl = t("pA%d" % h, 64 * k, 64 * k + 64)
+            tt(sl, sl, t("B"), Op.mult)
+
+    def off_w(h, k):
+        return (T["off%d" % h][:, k:512:8], [("off%d#%d" % (h, k // 4), 0, 512)])
+
+    def off_r(h, a, b):
+        return (T["off%d" % h][:, a:b], [("off%d#%d" % (h, p), 0, 512) for p in range(2) if a % 8 // 4 <= p <= (b - 1) % 8 // 4])
+
+    def names_v(h, C, ks=range(8)):
+        pa = "pA%d" % h
+        for k in ks:
+            c = (15 - 8 * h - k) * 64
+            tt(t("W", c, c + 64), t(pa, 64 * k, 64 * k + 64), C, Op.add)
+        c, w = (15 - 8 * h - ks[-1]) * 64, 64 * len(ks)
+        ts(t("E", c, c + w), t("W", c, c + w), 5, SH, 4095, AND)
+        for k in ks:
+            c = (15 - 8 * h - k) * 64
+            ts(off_w(h, k), t("E", c, c + 64), 4096.0 * k, Op.add)
+
+    names_pe(0)
+    names_pe(1)
+
+    def turn(k, j, bank, q):
+        mm(t(bank), perm_b(16 - k), t("tab", 512 * j, 512 * j + 512))
+        o = t("tab", 4096 * k + 512 * j, 4096 * k + 512 * j + 512)
+        if q == "S":
+            act(o, t(bank), Act.Copy)
+        else:
+            cp(o, t(bank))
+    names_mul(0)
+    names_mul(1)
+    names_v(0, t("C0"))
+    names_v(1, t("C0"))
+    mm(t("pV", 64, 128), perm_b(8), t("zb"))
+    act(t("z8"), t("pV", 64, 128), Act.Copy)
+    act(t("zh"), t("zb"), Act.Copy, scale=0.5, bias=-0.25)
+    ts(t("o8", 0, 8), t("mh", 0, 8), t("pgf"), Op.is_equal)
+    ts(t("o8", 8, 16), t("mh", 0, 8), t("pgf"), Op.is_equal, 2.0, Op.mult)
+    ts(t("o8", 16, 24), t("mh", 0, 8), t("pgf"), Op.is_equal, -1.0, Op.mult)
+    ts(t("o8", 24, 32), t("mh", 0, 8), t("pgf"), Op.is_equal, 1024.0, Op.mult)
+    ts(t("tmask"), t("tmi"), t("pif"), Op.is_equal)
+    ts(t("thr"), t("tmask"), t("nT"), Op.mult)
+    for j in range(8):
+        turn(TURN_S, j, ("pD0", "pD1")[j % 2], "S")
+    for j in range(8):
+        turn(TURN_V, j, ("pY", "pU")[j % 2], "V")
+
+    def late_constants():
+        ts(t("I2"), t("mh"), t("pif"), Op.is_equal, 2.0, Op.mult)
+        ts(t("In"), t("mh"), t("pif"), Op.is_equal, -1.0, Op.mult)
+        ts(t("BDh"), t("ms"), t("pgf"), Op.is_equal)
+        ts(t("BDb"), t("ms"), t("pgf"), Op.is_equal)
+        ts(t("pwf"), t("pff"), 2.0, Op.mult, 1.0, Op.add)
+        ts(t("Km"), t("kmi"), t("pff"), Op.add)
+        ts(t("WU"), t("ms"), t("pgf"), Op.is_equal, t("pwf"), Op.mult)
+        ts(t("lb1"), t("lm"), t("pff"), Op.is_equal, 100000.0, Op.mult)
+        ts(t("Kb"), t("Km"), 16384.0, Op.add)
+        ts(t("eye"), t("eyi"), t("pff"), Op.is_equal)
+        tt(t("lb"), t("lb1"), t("lbi"), Op.add)
+
+    def send(name, land, msg, sem):
+        prepare("G", t(name)[1], [])
+        tr = []
+        for j, (lo, at, w, d) in enumerate(msg):
+            dst = T.cores[(rank + d) % 4]
+            rid, pid, _ = topo.addr(dst)
+            e = topo.engines(core, dst)
+            n = 8 // len(msg)
+            m = 0
+            for x in e[n * j:n * j + n]:
+                m |= 1 << x
+            tr.append(RemoteDMATransfer(dst_ids=[DstId(rid=rid, pnc=pid)], dma_engine_mask=m, remote_sem=T.sem[sem],
+                                        src=T[name][:, lo:lo + w], dst=T[land][:, at:at + w]))
+        g.remote_dma_fused(tr, local_sem=T.sem.lo)
+        total["lo"] = total.get("lo", 0) + 8
+        total[sem] = 8
+        note([(land, 0, 4 * msg[0][2])], sem, 8, True)
+
+    def dbank(k1, q):
+        b, l = q // 16, q % 16
+        if k1 == 0:
+            return "pD0", 128 * b + l
+        if b < 3:
+            return "pD1", 128 * b + l
+        return "pA0", l
+
+    def begin(r):
+        for q in range(NH[r]):
+            act(t("sd", 128 * q, 128 * q + 64), ind(t("tab", 0, 4 * 4096), off_r(0, 8 * q, 8 * q + 4)), Act.Abs,
+                bias=t("zb", q, q + 1), scale=-1.0)
+
+    def gathers(r):
+        chunks = [(k1, q) for k1 in range(2) for q in range(64)]
+        ts_, tv_ = 0.0, V_LATE[r]
+        plan = []
+        for c in chunks:
+            if len(plan) < NH[r]:
+                ts_ += 0.145
+                plan.append("S")
+            elif len(plan) < NH[r] + NV[r]:
+                tv_ += 0.18
+                plan.append("V")
+            elif ts_ + S_T <= tv_ + V_T:
+                ts_ += S_T
+                plan.append("S")
+            else:
+                tv_ += V_T
+                plan.append("V")
+        left = {"pD0": 0, "pD1": 0, "pA0": 0}
+        for c, e in zip(chunks, plan):
+            left[dbank(*c)[0]] += 1 if e == "S" else 2
+        for bank, w in (("pD0", 512), ("pD1", 384), ("pA0", 128)):
+            mm(t(bank, 0, w), t("oneh"), t("thr", 0, w), True, False)
+
+        def dist(c, src, lo, w):
+            bank, col = dbank(*c)
+            left[bank] -= 1
+            mm(t(bank, col, col + 113, 16), t(src, lo, lo + 128), t("o8", w, w + 8), False, left[bank] == 0)
+
+        ns, nv = [0], [0]
+        pend_s, pend_v = [], []
+
+        def flush_s():
+            for c, lo in reversed(pend_s):
+                dist(c, "sd", lo, 0)
+            pend_s.clear()
+
+        def flush_v(keep=0):
+            now = pend_v[:len(pend_v) - keep]
+            if not now:
+                return
+            a, b = now[0][1], now[-1][1] + 128
+            ts(t("vr", a, b), t("vd", a, b), 0.0, Op.max)
+            for c, lo in reversed(now):
+                dist(c, "vr", lo, 8)
+                dist(c, "vd", lo, 16)
+            del pend_v[:len(now)]
+
+        def compare(bank, w, out, lo):
+            ts(t(out, lo, lo + w), t(bank, 0, w), 1785.0, Op.is_lt)
+
+        def count(k1, b):
+            mm(t("pC", 16 * b + 8 * k1, 16 * b + 8 * k1 + 8), t("cmp%d" % k1, 128 * b, 128 * b + 128), t("o8", 24, 32))
+
+        todo = {"pD0": ("pD0", 512, "cmp0", 0), "pD1": ("pD1", 384, "cmp1", 0), "pA0": ("pA0", 128, "cmp1", 384)}
+        lag = []
+        for i, (c, e) in enumerate(zip(chunks, plan)):
+            k1, q = c
+            src = ind(t("tab"), off_r(k1, 8 * q, 8 * q + 8))
+            src2 = ind(t("tab"), off_r(k1, 8 * q + 4, 8 * q + 8))
+            zc = t("z8" if k1 else "zb", q, q + 1)
+            if e == "S":
+                lo = 128 * ns[0]
+                ns[0] += 1
+                if i < NH[r]:
+                    act(t("sd", lo + 64, lo + 128), src2, Act.Abs, bias=zc, scale=-1.0)
+                else:
+                    act(t("sd", lo, lo + 128), src, Act.Abs, bias=zc, scale=-1.0)
+                pend_s.append((c, lo))
+            else:
+                lo = 128 * nv[0]
+                nv[0] += 1
+                if i < NH[r] + NV[r]:
+                    ts(t("vd", lo + 64, lo + 128), src2, zc, Op.subtract)
+                else:
+                    ts(t("vd", lo, lo + 128), src, zc, Op.subtract)
+                pend_v.append((c, lo))
+            last = i + 1 == len(chunks) or dbank(*chunks[i + 1])[0] != dbank(*c)[0]
+            near = len(chunks) - i <= 16
+            if last:
+                flush_v()
+                flush_s()
+                lag.append((dbank(*c)[0], i + (24 if k1 == 0 else 12)))
+            else:
+                if len(pend_s) >= (2 if near else 4):
+                    flush_s()
+                if len(pend_v) >= (4 if near else 9):
+                    flush_v(1)
+            while lag and (lag[0][1] <= i and e == "V" or i + 1 == len(chunks)):
+                compare(*todo[lag.pop(0)[0]])
+        for b in range(4):
+            count(0, b)
+            count(1, b)
+
+    PIECES = (("Lc", 0, 16, 32, 16, 0), ("A", 112, 160, 48, 32, 16), ("A", 16, 0, 96, 16, 48))
+
+    def merge(r):
+        la = "LA%d" % r
+        for src, nm, rm, l, n, q in PIECES:
+            tt(t("tm", q, q + n), t(la, l, l + n), t(la if src == "A" else src, nm, nm + n), Op.mult)
+        for src, nm, rm, l, n, q in PIECES:
+            tt(t("L16", q, q + n), t("tm", q, q + n), t(la if src == "A" else src, rm, rm + n), Op.add)
+        if r + 1 < RO:
+            ts(t("B"), t("L16"), 2080.0, Op.add)
+            names_pe(0)
+            names_pe(1)
+
+    def tail(r):
+        sa, sb = "SA%d" % r, "SB%d" % r
+        tt(t("En", 0, 64), t("pC", 0, 64), t("Km"), Op.add)
+        tt(t("En", 64, 128), t("Kb"), t("pC", 0, 64), Op.subtract)
+        segmax(t("Sc"), t("rmask", 0, 128), t("En"))
+        cp(t("KI"), t("Sc", 15, 128, 16))
+        ts(t("KJ"), t("KI"), 1023, AND)
+        cp(t("koff"), t("KJ"))
+        act(t("OO", 0, 64), ind(t("eye"), t("koff", 0, 4)), Act.Copy)
+        cp(t("EtU"), ind(t("E"), t("koff", 0, 4)))
+        c = S_BEST
+        for lo, hi in ((0, 32), (32, c)):
+            act(t("G", 16 * lo, 16 * hi), ind(t("tab", 0, 4096), t("EtU", lo, hi)), Act.Copy, scale=0.5)
+        ts(t("hot"), t("Sc", 15, 64, 16), 9216.0, Op.is_ge)
+        for b in range(4):
+            mm(t("pU", 64, 65), t("BDb"), t("hot", b, b + 1), b == 0, b == 3)
+        if c < 64:
+            ts(t("G", 16 * c, 1024), ind(t("tab", 0, 4096), t("EtU", c, 64)), 0.5, Op.mult)
+        ts(t("Eb"), ind(t("E"), t("koff", 4, 8)), -2048.0, Op.add)
+        cp(t("OO", 64, 128), ind(t("eye"), t("koff", 4, 8)))
+        tt(t("Q"), t("Eb"), t("OO", 0, 64), Op.mult)
+        mm(t("pV", 0, 64), t("BDh"), t("Q"))
+        ts(t(sa, 32, 96), t("EtU"), -2048.0, Op.add)
+        for dst, lo, q, n in (("Lc", 0, 0, 16), (sa, 96, 16, 32), (sa, 16, 48, 16)):
+            ts(t(dst, lo, lo + n), t("OO", 64 + q, 64 + q + n), -1.0, Op.mult, 1.0, Op.add)
+        segmax(t("Ms", 0, 512), t("rmask", 0, 512), t("G", 0, 512))
+        for dst, lo, q, n in (("Lc", 16, 0, 16), (sa, 128, 16, 32), (sa, 0, 48, 16)):
+            tt(t(dst, lo, lo + n), t("pV", q, q + n), t("OO", 64 + q, 64 + q + n), Op.mult)
+        send(sa, "LA%d" % r, MSGA, "ra%d" % r)
+        act(t("kA"), t("pU", 64, 65), Act.Copy, scale=32.0, bias=65536.0 + 1024.0 - 8388608.0)
+        segmax(t("Ms", 512, 1024), t("rmask", 512, 1024), t("G", 512, 1024))
+        tt(t("Yi"), t("Ms", 15, 1024, 16), t("zh"), Op.add)
+        cp(t("Yb"), t("Yi"))
+        mm(t("pU", 0, 64), t("WU"), t("Yb"))
+        mm(t("pV", 128, 192), t("I2"), t("Ms", 15, 1024, 16), True, False)
+        mm(t("pV", 128, 192), t("In"), t("zb"), False, True)
+        for lo, q, n in ((0, 0, 16), (96, 16, 32), (80, 48, 16)):
+            act(t(sb, lo, lo + n), t("pV", 128 + q, 128 + q + n), Act.Abs)
+        cp(t("si"), t("pU", 0, 64))
+        ts(t("ui"), t("si"), 4095, AND)
+        ts(t("w6"), t("si"), 63, AND)
+        ts(t("u1"), t("ui"), -2048.0, Op.add)
+        ts(t("u2"), t("ui"), 3232.0, Op.add)
+        tt(t("wv"), t("w6"), t("lb"), Op.add)
+        tt(t("Wc"), t("u1"), t("u2"), Op.mult)
+        segmax(t("ws"), t("rmask", 0, 64), t("wv"))
+        ts(t("Wd"), t("Wc"), 0x1FFE0, AND)
+        cp(t("woff"), t("ws", 15, 64, 16))
+        ts(t(sb, 16, 80), t("Wd"), t("kA"), Op.add)
+        send(sb, "LB%d" % r, MSGB, "rb%d" % r)
+        if r + 1 < RO:
+            for k in range(1, NT):
+                mm(t("pY", 64 * k, 64 * k + 64), perm_b(16 - k), t("Yb"))
+            act(t("Yr", 64, 512), t("pY", 64, 512), Act.Copy)
+        cp(ind(t("tab", 0, 4096), t("woff")), t("Yb"))
+        if r + 1 < RO:
+            for k in range(1, NT):
+                cp(ind(t("tab", 4096 * k, 4096 * k + 4096), t("woff")), t("Yr", 64 * k, 64 * k + 64))
+            merge(r)
+            names_mul(0)
+        else:
+            merge(r)
+            dma("Y", "d_out", outside(T.yx[:, :]), t("tab", 0, 4096))
+
+    def receive(r):
+        lb = "LB%d" % r
+        if r + 1 < RO:
+            for lo, q, n in ((0, 0, 16), (96, 16, 32), (80, 48, 16)):
+                act(t("zb", q, q + n), t(lb, lo, lo + n), Act.Copy)
+            mm(t("pV", 64, 128), perm_b(8), t("zb"))
+            act(t("z8"), t("pV", 64, 128), Act.Copy)
+            act(t("zh"), t("zb"), Act.Copy, scale=0.5, bias=-0.25)
+            names_v(0, t(lb, 16, 80), range(4))
+            begin(r + 1)
+            cp(t("Ai"), t("pU", 64, 65))
+            names_v(0, t(lb, 16, 80), range(4, 8))
+            ts(t("Aj"), t("Ai"), 31, AND)
+            names_mul(1)
+            ts(t("ncol"), t("Aj"), -1.0, Op.mult, t("nT"), Op.add)
+            names_v(1, t(lb, 16, 80))
+            ts(t("thr"), t("tmask"), t("ncol"), Op.mult)
+        else:
+            for b in range(4):
+                s = 16 * ORD[b]
+                ts(t("ylf", s, s + 16), t("L16", 16 * b, 16 * b + 16), 2048.0, Op.add)
+            dma("Y", "d_out", outside(T.yl[:, :]), t("ylf"))
+            for lo, b in ((0, 0), (96, 1), (112, 2), (80, 3)):
+                s = 16 * ORD[b]
+                act(t("yzf", s, s + 16), t(lb, lo, lo + 16), Act.Copy)
+            dma("S", "d_out", outside(T.yz[:, :]), t("yzf"))
+            ts(t("Wc"), t(lb, 16, 80), 8388608.0 - 1024.0, Op.add)
+            ts(t("Wd"), t("Wc"), 5, SH, 4095, AND)
+            for b in range(4):
+                s = 16 * ORD[b]
+                cp(t("yaf", s, s + 16), t("Wd", 16 * b, 16 * b + 16))
+            dma("Y", "d_out", outside(T.ya[:, :]), t("yaf", p0=0, p1=128, ps=16))
+
+    begin(0)
+    late_constants()
+    for j in range(NV[0]):
+        q = NH[0] + j
+        ts(t("vd", 128 * j, 128 * j + 64), ind(t("tab", 0, 4 * 4096), off_r(0, 8 * q, 8 * q + 4)), t("zb", q, q + 1), Op.subtract)
+    for r in range(RO):
+        gathers(r)
+        tail(r)
+        receive(r)
+    for s in sorted(total):
+        g.wait_ge(T.sem[s], total[s])

@@ -1,75 +1,76 @@
+import math
 from concourse.bass import DstId, RemoteDMATransfer
 from concourse.mybir import AluOpType as Op, ActivationFunctionType as Act
 
 RO = 4
-ORD = [2, 0, 3, 1]
 NT = 8
-S_T, V_T = 0.224, 0.262
-V_LATE = [2.0, 3.5, 3.5, 3.5]
-NH = [40, 5, 5, 5]
-NV = [14, 0, 0, 0]
-S_BEST = 58
-DMA_TABS = [1, 2, 4, 5, 6]
-TURN_S, TURN_V = 3, 7
+TW = 4160
+RUNS = ((0, 0, 16), (16, 48, 16), (32, 16, 32))
+SLOT0 = (0, 48, 16, 32)
+FIX, CYC, GAT, SCA, LAT, FAR = 0.05, 0.00083, 0.00125, 0.003, 0.1, 3.6
+T_SMALL, T_X, T_TAB = 2.4, 5.2, 3.2
+WAIT, SLACK = 0.03, 0.12
+EARLY = False
+RAW = ((0, 256), (256, 384))
 
 SCRATCH = {
-    "tab": ("sbuf", [128, NT * 4096], "bfloat16"),
-    "sd": ("sbuf", [128, 112 * 128], "bfloat16"),
-    "vd": ("sbuf", [128, 96 * 128], "bfloat16"),
-    "vr": ("sbuf", [128, 96 * 128], "bfloat16"),
-    "W": ("sbuf", [128, 1024], "int32"), "E": ("sbuf", [128, 1024], "int32"),
-    "off0": ("sbuf", [128, 512], "uint16"), "off1": ("sbuf", [128, 512], "uint16"),
-    "L16": ("sbuf", [128, 64], "float16"), "B": ("sbuf", [128, 64], "float32"),
-    "C0": ("sbuf", [128, 64], "float32"),
-    "zb": ("sbuf", [128, 64], "bfloat16"), "z8": ("sbuf", [128, 64], "bfloat16"), "zh": ("sbuf", [128, 64], "float32"),
+    "tab": ("sbuf", [128, NT * TW + 16], "bfloat16"), "spare": ("sbuf", [128, 4096], "bfloat16"),
+    "sd": ("sbuf", [128, 64 * 128], "bfloat16"),
+    "vd": ("sbuf", [128, 48 * 128], "bfloat16"),
+    "vr": ("sbuf", [128, 48 * 128], "bfloat16"),
+    "rx": ("sbuf", [128, 8192], "bfloat16"), "rm": ("sbuf", [128, 8192], "bfloat16"),
+    "W": ("sbuf", [128, 512], "int32"), "E": ("sbuf", [128, 1024], "int32"), "off": ("sbuf", [128, 1024], "uint16"),
+    "L16": ("sbuf", [128, 64], "float16"), "B2": ("sbuf", [128, 128], "float32"), "C2": ("sbuf", [128, 128], "float32"),
+    "zr": ("sbuf", [128, 256], "bfloat16"), "zh": ("sbuf", [128, 64], "float32"), "zn": ("sbuf", [128, 32], "bfloat16"),
+    "zi": ("sbuf", [128, 64], "bfloat16"), "zm": ("sbuf", [128, 512], "bfloat16"),
     "thr": ("sbuf", [128, 512], "float16"), "nT": ("sbuf", [128, 1], "float32"), "ncol": ("sbuf", [128, 1], "float32"),
     "kA": ("sbuf", [128, 1], "float32"), "Ai": ("sbuf", [128, 1], "int32"), "Aj": ("sbuf", [128, 1], "int32"),
-    "cmp0": ("sbuf", [128, 512], "bfloat16"), "cmp1": ("sbuf", [128, 512], "bfloat16"),
-    "En": ("sbuf", [128, 128], "float32"), "Sc": ("sbuf", [128, 128], "float32"),
-    "hot": ("sbuf", [128, 4], "bfloat16"),
+    "cmp": ("sbuf", [128, 1024], "bfloat16"), "Sc": ("sbuf", [128, 128], "float32"), "hot": ("sbuf", [128, 4], "bfloat16"),
     "KI": ("sbuf", [128, 8], "int32"), "KJ": ("sbuf", [128, 8], "int32"), "koff": ("sbuf", [128, 8], "uint16"),
+    "Ei": ("sbuf", [128, 64], "int32"), "Em": ("sbuf", [128, 64], "int32"),
     "EtU": ("sbuf", [128, 64], "uint16"), "OO": ("sbuf", [128, 128], "bfloat16"),
     "Eb": ("sbuf", [128, 64], "float32"), "Q": ("sbuf", [128, 64], "float16"),
-    "G": ("sbuf", [128, 1024], "bfloat16"), "Ms": ("sbuf", [128, 1024], "bfloat16"),
-    "Yi": ("sbuf", [128, 64], "int32"), "Yb": ("sbuf", [128, 64], "bfloat16"), "Yr": ("sbuf", [128, 512], "bfloat16"),
+    "G": ("sbuf", [128, 512], "bfloat16"), "Ms": ("sbuf", [128, 1024], "bfloat16"),
+    "Y16": ("sbuf", [128, 64], "float16"), "Yr0": ("sbuf", [128, 240], "bfloat16"), "Yr1": ("sbuf", [128, 288], "bfloat16"),
     "si": ("sbuf", [128, 64], "int32"), "ui": ("sbuf", [128, 64], "int32"), "u1": ("sbuf", [128, 64], "float32"),
     "u2": ("sbuf", [128, 64], "float32"), "Wc": ("sbuf", [128, 64], "int32"), "Wd": ("sbuf", [128, 64], "int32"),
-    "w6": ("sbuf", [128, 64], "int32"), "wv": ("sbuf", [128, 64], "float32"), "ws": ("sbuf", [128, 64], "float32"),
-    "woff": ("sbuf", [128, 4], "uint16"),
-    "tm": ("sbuf", [128, 64], "float16"),
-    "Lc": ("sbuf", [128, 32], "float16"),
+    "w6": ("sbuf", [128, 1], "int32"), "ws": ("sbuf", [128, 64], "float32"), "wr": ("sbuf", [128, 4], "float32"),
+    "wo0": ("sbuf", [128, 16], "uint16"), "wo1": ("sbuf", [128, 18], "uint16"),
+    "tm": ("sbuf", [128, 64], "float32"),
+    "ST": ("sbuf", [128, RO * 320], "float32"), "LA": ("sbuf", [128, RO * 384], "float32"),
+    "SA": ("sbuf", [128, RO * 4], "float32"), "LB": ("sbuf", [128, RO * 4], "float32"),
     "J": ("sbuf", [128, 16], "int32"), "J2": ("sbuf", [128, 16], "int32"), "tg": ("sbuf", [128, 16], "float32"),
-    "mh": ("sbuf", [128, 128], "bfloat16"), "ms": ("sbuf", [128, 128], "bfloat16"), "lm": ("sbuf", [128, 64], "bfloat16"),
+    "mh": ("sbuf", [128, 128], "bfloat16"), "ms": ("sbuf", [128, 128], "bfloat16"), "lm": ("sbuf", [128, 32], "bfloat16"),
     "pi": ("sbuf", [128, 1], "int32"), "pj": ("sbuf", [128, 1], "int32"), "pk": ("sbuf", [128, 1], "int32"),
-    "pl": ("sbuf", [128, 1], "int32"),
+    "pl": ("sbuf", [128, 1], "int32"), "pm": ("sbuf", [128, 1], "int32"),
     "pif": ("sbuf", [128, 1], "float32"), "pgf": ("sbuf", [128, 1], "float32"), "pff": ("sbuf", [128, 1], "float32"),
-    "pbf": ("sbuf", [128, 1], "float32"), "pwf": ("sbuf", [128, 1], "float32"),
-    "PH": ("sbuf", [128, 16 * 128], "float16"), "PB": ("sbuf", [128, 8 * 128], "bfloat16"),
-    "BDh": ("sbuf", [128, 128], "float16"), "BDb": ("sbuf", [128, 128], "bfloat16"), "WU": ("sbuf", [128, 128], "bfloat16"),
-    "I2": ("sbuf", [128, 128], "bfloat16"), "In": ("sbuf", [128, 128], "bfloat16"),
-    "o8": ("sbuf", [128, 32], "bfloat16"), "sel": ("sbuf", [128, 128], "float32"),
-    "oneh": ("sbuf", [128, 128], "float16"), "c16": ("sbuf", [128, 512], "float16"),
-    "tmi": ("sbuf", [128, 512], "bfloat16"), "tmask": ("sbuf", [128, 512], "float16"),
-    "kmi": ("sbuf", [128, 64], "int32"), "Km": ("sbuf", [128, 64], "float32"), "Kb": ("sbuf", [128, 64], "float32"),
-    "rmask": ("sbuf", [128, 1024], "bfloat16"),
-    "eyi": ("sbuf", [128, 1024], "bfloat16"), "eye": ("sbuf", [128, 1024], "bfloat16"),
-    "lbi": ("sbuf", [128, 64], "int32"), "lb1": ("sbuf", [128, 64], "float32"), "lb": ("sbuf", [128, 64], "float32"),
+    "pbf": ("sbuf", [128, 1], "float32"), "pwf": ("sbuf", [128, 1], "float32"), "p8f": ("sbuf", [128, 1], "float32"),
+    "p64": ("sbuf", [128, 1], "float32"), "podd": ("sbuf", [128, 1], "float32"), "pev": ("sbuf", [128, 1], "float32"),
+    "pad1": ("sbuf", [128, 1], "float32"), "padb": ("sbuf", [128, 1], "float32"),
+    "PH": ("sbuf", [128, 16 * 128], "float16"),
+    "BD": ("sbuf", [128, 128], "float16"), "WU": ("sbuf", [128, 128], "float16"), "In": ("sbuf", [128, 128], "float16"),
+    "o8": ("sbuf", [128, 56], "bfloat16"), "sel": ("sbuf", [128, 128], "float32"),
+    "oneh": ("sbuf", [128, 128], "bfloat16"), "c16": ("sbuf", [128, 512], "bfloat16"), "c2k": ("sbuf", [128, 32], "bfloat16"),
+    "gmi": ("sbuf", [128, 512], "bfloat16"), "gm": ("sbuf", [128, 512], "float16"),
+    "kmi": ("sbuf", [128, 64], "int32"), "Km": ("sbuf", [128, 64], "float16"),
+    "cfi": ("sbuf", [128, 32], "int32"), "coff": ("sbuf", [128, 32], "uint16"),
+    "rmask": ("sbuf", [128, 256], "bfloat16"), "rmi": ("sbuf", [128, 256], "bfloat16"), "dm": ("sbuf", [128, 32], "bfloat16"), "dm1": ("sbuf", [128, 32], "bfloat16"),
+    "eyi": ("sbuf", [128, 512], "bfloat16"), "eye": ("sbuf", [128, 512], "bfloat16"),
+    "tci": ("sbuf", [128, 48], "int32"), "tc": ("sbuf", [128, 48], "float32"),
     "lsi": ("sbuf", [128, 64], "int32"), "ani": ("sbuf", [128, 64], "int32"), "thi": ("sbuf", [128, 1], "int32"),
     "anf": ("sbuf", [128, 65], "float32"),
     "ylf": ("sbuf", [128, 64], "float32"), "yaf": ("sbuf", [128, 64], "float32"), "yzf": ("sbuf", [128, 64], "bfloat16"),
 }
-PS = ["pA0", "pA1", "pD0", "pD1", "pC", "pV", "pU", "pY"]
+PS = ["pA", "pZ", "pD0", "pD1", "pC", "pV", "pU", "pY"]
 for _n in PS:
     SCRATCH[_n] = ("psum", [128, 512], "float32")
-for _r in range(RO):
-    SCRATCH["SA%d" % _r] = ("sbuf", [128, 160], "float16")
-    SCRATCH["LA%d" % _r] = ("sbuf", [128, 192], "float16")
-    SCRATCH["SB%d" % _r] = ("sbuf", [128, 128], "float32")
-    SCRATCH["LB%d" % _r] = ("sbuf", [128, 128], "float32")
-DM = ["d_ls", "d_an", "d_z", "d_th"] + ["d_x%d" % j for j in range(4)] + ["d_t%d" % k for k in DMA_TABS] + ["d_out"]
-SEMAPHORES = ["sV", "sS", "sP", "sG", "lo"] + DM + ["ra%d" % r for r in range(RO)] + ["rb%d" % r for r in range(RO)]
-MSGA = [(0, 0, 48, 3), (48, 48, 48, 1), (80, 96, 48, 2), (112, 144, 48, 2)]
-MSGB = [(0, 0, 32, 3), (32, 32, 32, 1), (64, 64, 32, 2), (96, 96, 32, 1)]
+DM = ["d_ls", "d_an", "d_z", "d_th", "d_x", "d_sp", "d_o1", "d_o2"] + ["d_t%d" % k for k in range(1, NT)]
+SEMAPHORES = ["sV", "sS", "sP", "sG", "lo"] + DM + ["r%s%d" % (a, r) for a in "abc" for r in range(RO)]
+MSG = (((0, 0, 96, 1), (64, 96, 96, 2)), ((128, 192, 80, 2), (208, 272, 80, 3)))
+LANES = ((0, 0), (160, 224))
+PAIRS = ((96, 128), (256, 320))
+MAGIC = 1.5 * 2 ** 29
+CC = 65536.0 + 1024.0 - 8388608.0
 
 
 def rank_program(g, core, T, topo):
@@ -78,9 +79,8 @@ def rank_program(g, core, T, topo):
         return
     ENG = {"V": g.vector, "S": g.scalar, "P": g.tensor, "G": g, "Y": g.sync}
     known = {q: {} for q in ENG}
-    clock = {}
-    total = {}
-    acc = {}
+    clock, total, acc, plan = {}, {}, {}, {}
+    clk = {q: 0.0 for q in ENG}
 
     def t(name, lo=0, hi=None, st=1, p0=0, p1=128, ps=1):
         if hi is None:
@@ -89,21 +89,22 @@ def rank_program(g, core, T, topo):
             ap = T[name][:, lo:hi] if st == 1 else T[name][:, lo:hi:st]
         else:
             ap = T[name][p0:p1, lo:hi] if ps == 1 else T[name][p0:p1:ps, lo:hi]
-        return (ap, [(name, lo, hi)])
+        regs = [(name, lo, hi, st)]
+        return (ap, regs, (hi - lo + st - 1) // st, SCRATCH[name][2].endswith("16"), "")
 
     def ind(win, off):
-        return (win[0].indirect(off[0]), win[1] + off[1])
+        return (win[0].indirect(off[0]), win[1] + off[1], 16 * off[2], win[3], "ind")
 
     def outside(ap):
-        return (ap, [])
+        return (ap, [], 0, False, "")
 
     def need(q, regs, isw):
         own = "s" + q
         out = {}
-        for name, lo, hi in regs:
+        for name, lo, hi, st in regs:
             ps = name in PS
-            for a, b, sem, val, w in acc.get(name, []):
-                over = a < hi and lo < b
+            for a, b, sem, val, w, s2 in acc.get(name, []):
+                over = a < hi and lo < b and (lo - a) % math.gcd(st, s2) == 0
                 if sem == own:
                     hit = over and w and not isw
                 elif ps:
@@ -115,16 +116,22 @@ def rank_program(g, core, T, topo):
         return out
 
     def note(regs, sem, val, isw):
-        for name, lo, hi in regs:
-            lst = [e for e in acc.get(name, []) if not (e[0] >= lo and e[1] <= hi and e[2] == sem and (e[4] == isw))]
-            lst.append((lo, hi, sem, val, isw))
+        for name, lo, hi, st in regs:
+            lst = [e for e in acc.get(name, []) if not (e[0] >= lo and e[1] <= hi and e[2] == sem and e[4] == isw
+                                                        and e[5] % st == 0 and (e[0] - lo) % st == 0)]
+            lst.append((lo, hi, sem, val, isw, st))
             acc[name] = lst
 
-    def prepare(q, reads, writes):
+    def waits(q, reads, writes):
         w = {}
         for regs, isw in ((reads, False), (writes, True)):
             for s, v in need(q, regs, isw).items():
                 w[s] = max(w.get(s, 0), v)
+        return w
+
+    def prepare(q, reads, writes):
+        w = waits(q, reads, writes)
+        clk[q] = max([clk[q]] + [plan[e] for e in w.items()])
         for s in sorted(w):
             if any(o != s and clock.get((o, w[o]), {}).get(s, 0) >= w[s] and known[q].get(o, 0) < w[o] for o in w):
                 continue
@@ -136,28 +143,55 @@ def rank_program(g, core, T, topo):
                 k[a] = max(k.get(a, 0), b)
             k[s] = max(k.get(s, 0), w[s])
 
-    def finish(q, ins, sem, n, reads, writes):
+    def finish(q, ins, sem, n, reads, writes, when):
         total[sem] = total.get(sem, 0) + n
         ins.then_inc(T.sem[sem], n)
         clock[(sem, total[sem])] = dict(known[q])
+        plan[(sem, total[sem])] = when
         note(reads, sem, total[sem], False)
         note(writes, sem, total[sem], True)
 
+    rec = [None]
+
+    def put(step):
+        if rec[0] is None:
+            step[4]()
+        else:
+            rec[0].append(step)
+
+    def stream(fn, *a):
+        keep, rec[0] = rec[0], []
+        fn(*a)
+        s, rec[0] = rec[0], keep
+        return s
+
     def op(q, fn, out, ins, *rest, **kw):
-        reads = []
-        for a in ins:
-            if isinstance(a, tuple):
-                reads = reads + a[1]
-        if "bias" in kw and isinstance(kw["bias"], tuple):
+        aps = [a for a in ins if isinstance(a, tuple)]
+        reads = [r for a in aps for r in a[1]]
+        if isinstance(kw.get("bias"), tuple):
             reads = reads + kw["bias"][1]
             kw["bias"] = kw["bias"][0]
         wr = out[1]
-        if len(wr) > 1:
-            reads = reads + wr[1:]
-            wr = wr[:1]
-        prepare(q, reads, wr)
-        i = fn(out[0], *([a[0] if isinstance(a, tuple) else a for a in ins] + list(rest)), **kw)
-        finish(q, i, "s" + q, 1, reads, wr)
+        if out[4]:
+            reads, wr, c = reads + wr[1:], wr[:1], FIX + SCA * out[2]
+        elif q == "P":
+            c = 0.0005 * max(64, out[2])
+        elif aps and aps[0][4]:
+            c = (FIX if q == "V" else 0.065) + GAT * out[2]
+        elif q == "G":
+            c = 0.13 + 2 * CYC * out[2]
+        else:
+            c = FIX + CYC * out[2] * (0.5 if q == "V" and all(a[3] or a[2] == 1 for a in aps + [out]) else 1)
+
+        def go():
+            prepare(q, reads, wr)
+            i = fn(out[0], *([a[0] if isinstance(a, tuple) else a for a in ins] + list(rest)), **kw)
+            clk[q] += c
+            finish(q, i, "s" + q, 1, reads, wr, clk[q] + LAT)
+        put((q, reads, wr, c, go))
+
+    def call(fn):
+        put(("", [], [], 0, fn))
 
     def tt(out, a, b, o):
         op("V", g.vector.tensor_tensor, out, [a, b, o])
@@ -171,38 +205,55 @@ def rank_program(g, core, T, topo):
     def cp(out, a):
         op("V", g.vector.tensor_copy, out, [a])
 
-    def segmax(out, mask, a):
-        op("V", g.vector.tensor_tensor_scan, out, [mask, a, 0.0, Op.min, Op.max])
+    def segmax(out, a):
+        op("V", g.vector.tensor_tensor_scan, out, [t("rmask", 0, out[2]), a, 0.0, Op.min, Op.max])
 
-    def act(out, a, f, **kw):
+    def act(out, a, f=Act.Copy, **kw):
         op("S", g.scalar.activation, out, [a, f], **kw)
 
     def mm(out, l, r, start=True, stop=True):
         op("P", g.tensor.matmul, out, [l, r, start, stop])
 
-    def dma(q, sem, out, a, fresh=False):
-        prepare(q, a[1], [] if fresh else out[1])
-        i = ENG[q].dma_start(out[0], a[0])
-        finish(q, i, sem, 16, a[1], out[1])
+    def dma(q, sem, out, a, when=2.0, fresh=False):
+        def go():
+            prepare(q, a[1], [] if fresh else out[1])
+            i = ENG[q].dma_start(out[0], a[0])
+            finish(q, i, sem, 16, a[1], out[1], clk[q] + when)
+        put((q if q == "S" else "Y", a[1], [] if fresh else out[1], 0.05, go))
 
-    for b in range(4):
-        s = 16 * ORD[b]
-        dma("S", "d_ls", t("lsi", 16 * b, 16 * b + 16), outside(T.ls[:, s:s + 16]))
-    for b in range(4):
-        s = 16 * ORD[b]
-        dma("S", "d_an", t("ani", 16 * b, 16 * b + 16, p1=8), outside(T.an[:, s:s + 16]))
-    dma("S", "d_th", t("thi", p1=8), outside(T.th[:, 0:1]))
-    for b in range(4):
-        s = 16 * ORD[b]
-        dma("S", "d_z", t("zb", 16 * b, 16 * b + 16), outside(T.z[:, s:s + 16]))
-    for j in range(4):
-        dma("Y", "d_x%d" % j, t("tab", 1024 * j, 1024 * j + 1024), outside(T.x[:, 1024 * j:1024 * j + 1024]))
-    for k in DMA_TABS:
-        lo, hi = 4096 * k, 4096 * k + 4096
+    def send(src, land, c0, l0, msg, sem):
+        def go():
+            prepare("G", [(src, c0 + lo, c0 + lo + w, 1) for lo, at, w, d in msg], [])
+            tr = []
+            for j, (lo, at, w, d) in enumerate(msg):
+                dst = T.cores[(rank + d) % 4]
+                rid, pid, _ = topo.addr(dst)
+                e = topo.engines(core, dst)
+                n = len(e) // len(msg)
+                m = 0
+                for x in e[n * j:n * j + n]:
+                    m |= 1 << x
+                tr.append(RemoteDMATransfer(dst_ids=[DstId(rid=rid, pnc=pid)], dma_engine_mask=m, remote_sem=T.sem[sem],
+                                            src=T[src][:, c0 + lo:c0 + lo + w], dst=T[land][:, l0 + at:l0 + at + w]))
+                total["lo"] = total.get("lo", 0) + n
+                total[sem] = total.get(sem, 0) + n
+            g.remote_dma_fused(tr, local_sem=T.sem.lo)
+            plan[(sem, total[sem])] = clk["G"] + FAR
+            clk["G"] += 0.6
+            note([(land, l0 + at, l0 + at + w, 1) for lo, at, w, d in msg], sem, total[sem], True)
+        put(("G", [], [], 0, go))
+
+    dma("Y", "d_ls", t("lsi"), outside(T.ls[:, :]), T_SMALL)
+    dma("S", "d_an", t("ani", p1=8), outside(T.an[:, :]), T_SMALL)
+    dma("S", "d_th", t("thi", p1=8), outside(T.th[:, 0:1]), T_SMALL)
+    dma("Y", "d_z", t("zi"), outside(T.z[:, :]), T_SMALL)
+    dma("Y", "d_x", t("tab", 0, 4096), outside(T.x[:, :]), T_X)
+    for k in range(1, NT):
+        lo, hi, when = TW * k, TW * k + 4096, T_X + T_TAB * k
         for gg in range(8):
-            dma("Y", "d_t%d" % k, t("tab", lo, hi, p0=16 * gg + k, p1=16 * gg + 16), outside(T.x[16 * gg:16 * gg + 16 - k, :]), True)
+            dma("Y", "d_t%d" % k, t("tab", lo, hi, p0=16 * gg + k, p1=16 * gg + 16), outside(T.x[16 * gg:16 * gg + 16 - k, :]), when, True)
         for f in range(k):
-            dma("Y", "d_t%d" % k, t("tab", lo, hi, p0=f, p1=128, ps=16), outside(T.x[16 + f - k::16, :]), True)
+            dma("Y", "d_t%d" % k, t("tab", lo, hi, p0=f, p1=128, ps=16), outside(T.x[16 + f - k::16, :]), when, True)
 
     def iota(out, pattern, base, cm, **kw):
         op("G", g.iota, out, [], pattern, base, cm, **kw)
@@ -212,352 +263,504 @@ def rank_program(g, core, T, topo):
     iota(t("J"), [[-1, 16]], 16, 1)
     iota(t("mh"), [[1, 128]], 0, 0, **SM)
     iota(t("ms"), [[1, 8], [0, 16]], 0, 0, **SM)
-    iota(t("tmi"), [[0, 4], [16, 8], [0, 16]], 0, 0, **SM)
-    iota(t("kmi"), [[16, 4], [-64, 16]], 960, 0)
-    iota(t("lm"), [[0, 4], [1, 16]], 0, 0, **SM)
-    iota(t("eyi"), [[-1, 16], [0, 64]], 15, 0, **SM)
-    iota(t("rmask"), [[0, 64], [32767, 16]], 0, 0, **SM)
-    for b in range(4):
-        iota(t("lbi", 16 * b, 16 * b + 16), [[64, 16]], 1024 * ORD[b] - 100000, 0)
+    iota(t("gmi"), [[0, 4], [16, 8], [0, 16]], 0, 0, **SM)
+    iota(t("cfi"), [[16, 2], [0, 16]], 0, 0)
+    for s in range(2):
+        iota(t("kmi", 32 * s, 32 * s + 32), [[128, 2], [256, 2], [1, 8]], 0, 0)
+    iota(t("lm"), [[0, 2], [1, 16]], 0, 0, **SM)
+    iota(t("eyi"), [[-8, 2], [0, 32], [-1, 8]], 15, 0, **SM)
+    iota(t("rmi"), [[0, 16], [32767, 16]], -16384, 0, **SM)
+    for c, h, base in ((0, 0, 0), (16, 1, 0), (32, 0, TW - 4096)):
+        iota(t("tci", c, c + 16), [[TW, NT], [64 * (SLOT0[2 * h + 1] - SLOT0[2 * h]), 2]], base + 64 * SLOT0[2 * h], 0)
     SH, AND = Op.arith_shift_right, Op.bitwise_and
+    op("V", g.vector.memset, t("oneh"), [], 1.0)
+    op("V", g.vector.memset, t("c16", p1=32), [], 2016.0)
     ts(t("pj"), t("pi"), 15, AND)
-    ts(t("pk"), t("pi"), 4, SH)
     ts(t("pl"), t("pi"), 112, AND)
+    ts(t("pk"), t("pi"), 4, SH)
     ts(t("J2"), t("J"), 15, AND)
+    cp(t("pbf"), t("pl"))
     cp(t("pif"), t("pi"))
+    ts(t("tg"), t("J2"), t("pbf"), Op.add)
     cp(t("pff"), t("pj"))
     cp(t("pgf"), t("pk"))
-    cp(t("pbf"), t("pl"))
-    ts(t("tg"), t("J2"), t("pbf"), Op.add)
-    ts(t("sel", p1=8), t("ms", p1=8), t("pif", p1=8), Op.is_equal)
     for k in range(16):
         ts(t("PH", 128 * k, 128 * k + 128), t("mh"), t("tg", k, k + 1), Op.is_equal)
-    ts(t("oneh"), t("mh"), 0.0, Op.mult, 1.0, Op.add)
-    ts(t("c16", p1=32), t("tmi", p1=32), 0.0, Op.mult, 2016.0, Op.add)
-    ts(t("L16"), t("lsi"), -2048.0, Op.add)
-    ts(t("B"), t("lsi"), 32.0, Op.add)
-    cp(t("anf", 0, 64, p1=8), t("ani", p1=8))
-    cp(t("anf", 64, 65, p1=8), t("thi", p1=8))
-    mm(t("pU", 0, 65), t("sel", p1=8), t("anf", p1=8))
-    ts(t("C0"), t("pU", 0, 64), 32.0, Op.mult, 1024.0 - 8388608.0, Op.add)
-    ts(t("nT"), t("pU", 64, 65), -1.0, Op.mult, 1785.0, Op.add)
-    for k in range(8, 16):
-        ts(t("PB", 128 * (k - 8), 128 * (k - 8) + 128), t("mh"), t("tg", k, k + 1), Op.is_equal)
+    ts(t("sel", p1=8), t("ms", p1=8), t("pif", p1=8), Op.is_equal)
 
-    def perm_b(k):
-        return t("PB", 128 * (k - 8), 128 * (k - 8) + 128)
-
-    def names_pe(h):
-        pa = "pA%d" % h
-        mm(t(pa), t("oneh", p1=1), t("c16", p1=1), True, False)
-        for k in range(8):
-            mm(t(pa, 64 * k, 64 * k + 64), t("PH", 128 * (8 * h + k), 128 * (8 * h + k) + 128), t("L16"), False, k == 7)
-
-    def names_mul(h):
-        for k in range(8):
-            sl = t("pA%d" % h, 64 * k, 64 * k + 64)
-            tt(sl, sl, t("B"), Op.mult)
-
-    def off_w(h, k):
-        return (T["off%d" % h][:, k:512:8], [("off%d#%d" % (h, k // 4), 0, 512)])
-
-    def off_r(h, a, b):
-        return (T["off%d" % h][:, a:b], [("off%d#%d" % (h, p), 0, 512) for p in range(2) if a % 8 // 4 <= p <= (b - 1) % 8 // 4])
-
-    def names_v(h, C, ks=range(8)):
-        pa = "pA%d" % h
-        for k in ks:
-            c = (15 - 8 * h - k) * 64
-            tt(t("W", c, c + 64), t(pa, 64 * k, 64 * k + 64), C, Op.add)
-        c, w = (15 - 8 * h - ks[-1]) * 64, 64 * len(ks)
-        ts(t("E", c, c + w), t("W", c, c + w), 5, SH, 4095, AND)
-        for k in ks:
-            c = (15 - 8 * h - k) * 64
-            ts(off_w(h, k), t("E", c, c + 64), 4096.0 * k, Op.add)
-
-    names_pe(0)
-    names_pe(1)
-
-    def turn(k, j, bank, q):
-        mm(t(bank), perm_b(16 - k), t("tab", 512 * j, 512 * j + 512))
-        o = t("tab", 4096 * k + 512 * j, 4096 * k + 512 * j + 512)
-        if q == "S":
-            act(o, t(bank), Act.Copy)
-        else:
-            cp(o, t(bank))
-    names_mul(0)
-    names_mul(1)
-    names_v(0, t("C0"))
-    names_v(1, t("C0"))
-    mm(t("pV", 64, 128), perm_b(8), t("zb"))
-    act(t("z8"), t("pV", 64, 128), Act.Copy)
-    act(t("zh"), t("zb"), Act.Copy, scale=0.5, bias=-0.25)
-    ts(t("o8", 0, 8), t("mh", 0, 8), t("pgf"), Op.is_equal)
-    ts(t("o8", 8, 16), t("mh", 0, 8), t("pgf"), Op.is_equal, 2.0, Op.mult)
-    ts(t("o8", 16, 24), t("mh", 0, 8), t("pgf"), Op.is_equal, -1.0, Op.mult)
-    ts(t("o8", 24, 32), t("mh", 0, 8), t("pgf"), Op.is_equal, 1024.0, Op.mult)
-    ts(t("tmask"), t("tmi"), t("pif"), Op.is_equal)
-    ts(t("thr"), t("tmask"), t("nT"), Op.mult)
-    for j in range(8):
-        turn(TURN_S, j, ("pD0", "pD1")[j % 2], "S")
-    for j in range(8):
-        turn(TURN_V, j, ("pY", "pU")[j % 2], "V")
+    def turn(k):
+        return t("PH", 128 * (k % 16), 128 * (k % 16) + 128)
 
     def late_constants():
-        ts(t("I2"), t("mh"), t("pif"), Op.is_equal, 2.0, Op.mult)
-        ts(t("In"), t("mh"), t("pif"), Op.is_equal, -1.0, Op.mult)
-        ts(t("BDh"), t("ms"), t("pgf"), Op.is_equal)
-        ts(t("BDb"), t("ms"), t("pgf"), Op.is_equal)
+        for k in range(NT):
+            op("V", g.vector.memset, t("tab", TW * k + 4096, TW * k + TW + 16 * (k == NT - 1)), [], 0.0)
+        op("V", g.vector.memset, t("c2k"), [], 2048.0)
+        for c, w in enumerate((1.0, 2.0, -1.0, -512.0, 512.0, -1024.0, 1024.0)):
+            ts(t("o8", 8 * c, 8 * c + 8), t("mh", 0, 8), t("pgf"), Op.is_equal, w, Op.mult)
+        ts(t("gm"), t("gmi"), t("pbf"), Op.is_equal)
+        ts(t("coff"), t("cfi"), t("pff"), Op.add)
+        ts(t("nT"), t("pU", 128, 129), -1.0, Op.mult, 1785.0, Op.add)
+        ts(t("thr"), t("gm"), t("nT"), Op.mult, 0.0625, Op.mult)
+        tt(t("zm"), ind(t("zn"), t("coff")), t("gm"), Op.mult)
+
+    def tail_constants():
+        ts(t("rmask"), t("rmi"), 32.0, Op.mult)
+        ts(t("p8f"), t("pff"), 8.0, Op.mult)
+        ts(t("p64"), t("pff"), 64.0, Op.mult, 31.5, Op.add)
         ts(t("pwf"), t("pff"), 2.0, Op.mult, 1.0, Op.add)
-        ts(t("Km"), t("kmi"), t("pff"), Op.add)
+        ts(t("pm"), t("pi"), 1, AND)
+        ts(t("In"), t("mh"), t("pif"), Op.is_equal, -0.5, Op.mult)
+        ts(t("BD"), t("ms"), t("pgf"), Op.is_equal)
+        ts(t("Km"), t("kmi"), t("p8f"), Op.add)
+        cp(t("podd"), t("pm"))
         ts(t("WU"), t("ms"), t("pgf"), Op.is_equal, t("pwf"), Op.mult)
-        ts(t("lb1"), t("lm"), t("pff"), Op.is_equal, 100000.0, Op.mult)
-        ts(t("Kb"), t("Km"), 16384.0, Op.add)
+        ts(t("tc"), t("tci"), t("p64"), Op.add)
+        ts(t("dm"), t("lm"), t("pff"), Op.not_equal, -524288.0, Op.mult)
+        ts(t("dm1"), t("lm"), 0.0, Op.mult, -31.5, Op.add)
         ts(t("eye"), t("eyi"), t("pff"), Op.is_equal)
-        tt(t("lb"), t("lb1"), t("lbi"), Op.add)
+        ts(t("pev"), t("podd"), -1.0, Op.mult, 1.0, Op.add)
+        ts(t("pad1"), t("pff"), -TW / 2 + 0.5, Op.mult, NT * TW - 4096 - 0.5, Op.add)
+        ts(t("pad1"), t("pad1"), t("podd"), Op.mult)
+        ts(t("padb"), t("pff"), TW / 2, Op.mult, t("pad1"), Op.add)
 
-    def send(name, land, msg, sem):
-        prepare("G", t(name)[1], [])
-        tr = []
-        for j, (lo, at, w, d) in enumerate(msg):
-            dst = T.cores[(rank + d) % 4]
-            rid, pid, _ = topo.addr(dst)
-            e = topo.engines(core, dst)
-            n = 8 // len(msg)
-            m = 0
-            for x in e[n * j:n * j + n]:
-                m |= 1 << x
-            tr.append(RemoteDMATransfer(dst_ids=[DstId(rid=rid, pnc=pid)], dma_engine_mask=m, remote_sem=T.sem[sem],
-                                        src=T[name][:, lo:lo + w], dst=T[land][:, at:at + w]))
-        g.remote_dma_fused(tr, local_sem=T.sem.lo)
-        total["lo"] = total.get("lo", 0) + 8
-        total[sem] = 8
-        note([(land, 0, 4 * msg[0][2])], sem, 8, True)
+    def spread(bank, src, first):
+        for k in range(16):
+            a, b = (15 - k) // 8, (15 - k) % 8
+            mm(t(bank, 256 * a + b, 256 * a + 256, 8), turn(k), src, first, first or k == 15)
 
-    def dbank(k1, q):
-        b, l = q // 16, q % 16
-        if k1 == 0:
-            return "pD0", 128 * b + l
-        if b < 3:
-            return "pD1", 128 * b + l
-        return "pA0", l
+    def names(h, s=None):
+        mm(t("pA"), t("oneh", p1=1), t("c16", p1=1), True, False)
+        spread("pA", t("L16", 32 * h, 32 * h + 32), False)
+        double_b(h)
+        for b in range(8):
+            tt(t("pA", b, 512, 8), t("pA", b, 512, 8), t("B2", 64 * h, 64 * h + 64), Op.mult)
+        if s is not None:
+            join(s)
+        for b in range(8):
+            tt(t("W", b, 512, 8), t("pA", b, 512, 8), t("C2", 64 * h, 64 * h + 64), Op.add)
+        ts(t("E", 512 * h, 512 * h + 512), t("W"), 5, SH, 4095, AND)
 
-    def begin(r):
-        for q in range(NH[r]):
-            act(t("sd", 128 * q, 128 * q + 64), ind(t("tab", 0, 4 * 4096), off_r(0, 8 * q, 8 * q + 4)), Act.Abs,
-                bias=t("zb", q, q + 1), scale=-1.0)
-
-    def gathers(r):
-        chunks = [(k1, q) for k1 in range(2) for q in range(64)]
-        ts_, tv_ = 0.0, V_LATE[r]
-        plan = []
-        for c in chunks:
-            if len(plan) < NH[r]:
-                ts_ += 0.145
-                plan.append("S")
-            elif len(plan) < NH[r] + NV[r]:
-                tv_ += 0.18
-                plan.append("V")
-            elif ts_ + S_T <= tv_ + V_T:
-                ts_ += S_T
-                plan.append("S")
+    def offsets(h, n, A=None):
+        for b in range(n):
+            o, e = t("off", 512 * h + b, 512 * h + 512, n), t("E", 512 * h + b, 512 * h + 512, n)
+            if A is None:
+                ts(o, e, float(TW * (n - 1 - b)), Op.add)
             else:
-                tv_ += V_T
-                plan.append("V")
-        left = {"pD0": 0, "pD1": 0, "pA0": 0}
-        for c, e in zip(chunks, plan):
-            left[dbank(*c)[0]] += 1 if e == "S" else 2
-        for bank, w in (("pD0", 512), ("pD1", 384), ("pA0", 128)):
-            mm(t(bank, 0, w), t("oneh"), t("thr", 0, w), True, False)
+                ts(o, e, A, Op.add, float(TW * (n - 1 - b)), Op.add)
 
-        def dist(c, src, lo, w):
-            bank, col = dbank(*c)
-            left[bank] -= 1
-            mm(t(bank, col, col + 113, 16), t(src, lo, lo + 128), t("o8", w, w + 8), False, left[bank] == 0)
+    def double_b(h):
+        for c in range(2):
+            ts(t("B2", 64 * h + 32 * c, 64 * h + 32 * c + 32), t("L16", 32 * h, 32 * h + 32), 2080.0, Op.add)
 
-        ns, nv = [0], [0]
-        pend_s, pend_v = [], []
+    streams, chunks, gate = [], [], [0]
+    seen = {"pD0": True, "pD1": False}
+    ring, pend, left, after = {"S": 0, "V": 0}, {"S": [], "V": []}, {}, {}
 
-        def flush_s():
-            for c, lo in reversed(pend_s):
-                dist(c, "sd", lo, 0)
-            pend_s.clear()
+    def place(h, n):
+        return ("pD0", 128 * n) if h == 0 else ("pD1", 128 * n) if n < 3 else ("pD0", 0)
 
-        def flush_v(keep=0):
-            now = pend_v[:len(pend_v) - keep]
-            if not now:
-                return
+    def dist(c, src, lo, w):
+        h, n, l = c
+        bank, col = place(h, n)
+        key = (h, bank)
+        left[key] -= w[1]
+        mm(t(bank, col + l, col + l + 113, 16), t(src, lo, lo + 128), t("o8", w[0], w[0] + 8), False, left[key] == 0)
+        if left[key] == 0:
+            after[key]()
+
+    def flush(e, keep=0):
+        now = pend[e][:len(pend[e]) - keep]
+        del pend[e][:len(now)]
+        if e == "V" and now:
             a, b = now[0][1], now[-1][1] + 128
             ts(t("vr", a, b), t("vd", a, b), 0.0, Op.max)
-            for c, lo in reversed(now):
-                dist(c, "vr", lo, 8)
-                dist(c, "vd", lo, 16)
-            del pend_v[:len(now)]
-
-        def compare(bank, w, out, lo):
-            ts(t(out, lo, lo + w), t(bank, 0, w), 1785.0, Op.is_lt)
-
-        def count(k1, b):
-            mm(t("pC", 16 * b + 8 * k1, 16 * b + 8 * k1 + 8), t("cmp%d" % k1, 128 * b, 128 * b + 128), t("o8", 24, 32))
-
-        todo = {"pD0": ("pD0", 512, "cmp0", 0), "pD1": ("pD1", 384, "cmp1", 0), "pA0": ("pA0", 128, "cmp1", 384)}
-        lag = []
-        for i, (c, e) in enumerate(zip(chunks, plan)):
-            k1, q = c
-            src = ind(t("tab"), off_r(k1, 8 * q, 8 * q + 8))
-            src2 = ind(t("tab"), off_r(k1, 8 * q + 4, 8 * q + 8))
-            zc = t("z8" if k1 else "zb", q, q + 1)
+        for c, lo in reversed(now):
             if e == "S":
-                lo = 128 * ns[0]
-                ns[0] += 1
-                if i < NH[r]:
-                    act(t("sd", lo + 64, lo + 128), src2, Act.Abs, bias=zc, scale=-1.0)
-                else:
-                    act(t("sd", lo, lo + 128), src, Act.Abs, bias=zc, scale=-1.0)
-                pend_s.append((c, lo))
+                dist(c, "sd", lo, (0, 2))
             else:
-                lo = 128 * nv[0]
-                nv[0] += 1
-                if i < NH[r] + NV[r]:
-                    ts(t("vd", lo + 64, lo + 128), src2, zc, Op.subtract)
-                else:
-                    ts(t("vd", lo, lo + 128), src, zc, Op.subtract)
-                pend_v.append((c, lo))
-            last = i + 1 == len(chunks) or dbank(*chunks[i + 1])[0] != dbank(*c)[0]
-            near = len(chunks) - i <= 16
-            if last:
-                flush_v()
-                flush_s()
-                lag.append((dbank(*c)[0], i + (24 if k1 == 0 else 12)))
+                dist(c, "vr", lo, (8, 1))
+                dist(c, "vd", lo, (16, 1))
+
+    def gather(e, c, n_t):
+        h, n, l = c
+        q, a = 16 * (n // 2) + l, n % 2
+        bank, col = place(h, n)
+        if (h, bank) not in left or left[(h, bank)] == 0:
+            w = 128 if (h, n) == (1, 3) else 512 - 128 * h
+            assert not seen[bank]
+            left[(h, bank)] = w // 4
+            seen[bank] = True
+            mm(t(bank, 0, w), t("oneh"), t("thr", 0, w), True, False)
+        if e == "V" and ring[e] == 48:
+            flush(e)
+        ring[e] %= 64 if e == "S" else 48
+        lo = 128 * ring[e]
+        ring[e] += 1
+        for s in range(8 // n_t):
+            o = 512 * h + 256 * a + 8 * q + n_t * s
+            src = ind(t("tab", 0, n_t * TW), t("off", o, o + n_t))
+            zc = 64 * ((15 - 8 * a - n_t * s) // n_t * n_t // 4) + 32 * h + q
+            w = 16 * n_t
+            if e == "S":
+                act(t("sd", lo + w * s, lo + w * s + w), src, Act.Abs, bias=t("zr", zc, zc + 1), scale=-1.0)
             else:
-                if len(pend_s) >= (2 if near else 4):
-                    flush_s()
-                if len(pend_v) >= (4 if near else 9):
-                    flush_v(1)
-            while lag and (lag[0][1] <= i and e == "V" or i + 1 == len(chunks)):
-                compare(*todo[lag.pop(0)[0]])
-        for b in range(4):
-            count(0, b)
-            count(1, b)
+                ts(t("vd", lo + w * s, lo + w * s + w), src, t("zr", zc, zc + 1), Op.subtract)
+        pend[e].append((c, lo))
+        rest = len([1 for x in chunks if place(*x[0][:2])[0] == bank and x[0][0] == h])
+        if rest == 0:
+            flush("V")
+            flush("S")
+        elif e == "S" and len(pend[e]) >= (2 if rest <= 8 else 4):
+            flush(e)
+        elif e == "V" and len(pend[e]) >= (4 if rest <= 16 else 9):
+            flush(e, 1)
 
-    PIECES = (("Lc", 0, 16, 32, 16, 0), ("A", 112, 160, 48, 32, 16), ("A", 16, 0, 96, 16, 48))
+    def ready(step):
+        return max([0.0] + [plan[e] for e in waits(step[0], step[1], step[2]).items()])
 
-    def merge(r):
-        la = "LA%d" % r
-        for src, nm, rm, l, n, q in PIECES:
-            tt(t("tm", q, q + n), t(la, l, l + n), t(la if src == "A" else src, nm, nm + n), Op.mult)
-        for src, nm, rm, l, n, q in PIECES:
-            tt(t("L16", q, q + n), t("tm", q, q + n), t(la if src == "A" else src, rm, rm + n), Op.add)
-        if r + 1 < RO:
-            ts(t("B"), t("L16"), 2080.0, Op.add)
-            names_pe(0)
-            names_pe(1)
+    def run():
+        while chunks or any(streams):
+            streams[:] = [s for s in streams if s]
+            s = next((s for s in streams if s[0][0] not in ("S", "V")), None)
+            if s is not None:
+                step = s.pop(0)
+                if step[0] != "J":
+                    step[4]()
+                elif step[4] is not s:
+                    s[:0] = step[4]
+                    step[4].clear()
+                continue
+            open_ = [c for c in chunks if c[1] <= gate[0]]
+            can = []
+            for j, s in enumerate(streams):
+                e, at = s[0][0], max(ready(s[0]), clk[s[0][0]])
+                if j and streams[0][0][0] == e and at + s[0][3] > ready(streams[0][0]) + SLACK:
+                    continue
+                can.append((max(at - WAIT, clk[e]), j, s))
+            if open_:
+                per = 0.23 * (1.3 if open_[0][2] == 4 else 1)
+                for e in "SV":
+                    at = max(there(e, open_[0]), clk[e])
+                    if e == "S" or at + per + 0.3 < clk["S"] + per * len(chunks):
+                        can.append((at, 99, e))
+            at, j, s = min(can, key=lambda c: c[:2])
+            if j == 99:
+                take(s, open_[0])
+            else:
+                s.pop(0)[4]()
 
-    def tail(r):
-        sa, sb = "SA%d" % r, "SB%d" % r
-        tt(t("En", 0, 64), t("pC", 0, 64), t("Km"), Op.add)
-        tt(t("En", 64, 128), t("Kb"), t("pC", 0, 64), Op.subtract)
-        segmax(t("Sc"), t("rmask", 0, 128), t("En"))
-        cp(t("KI"), t("Sc", 15, 128, 16))
-        ts(t("KJ"), t("KI"), 1023, AND)
-        cp(t("koff"), t("KJ"))
-        act(t("OO", 0, 64), ind(t("eye"), t("koff", 0, 4)), Act.Copy)
-        cp(t("EtU"), ind(t("E"), t("koff", 0, 4)))
-        c = S_BEST
-        for lo, hi in ((0, 32), (32, c)):
-            act(t("G", 16 * lo, 16 * hi), ind(t("tab", 0, 4096), t("EtU", lo, hi)), Act.Copy, scale=0.5)
-        ts(t("hot"), t("Sc", 15, 64, 16), 9216.0, Op.is_ge)
-        for b in range(4):
-            mm(t("pU", 64, 65), t("BDb"), t("hot", b, b + 1), b == 0, b == 3)
-        if c < 64:
-            ts(t("G", 16 * c, 1024), ind(t("tab", 0, 4096), t("EtU", c, 64)), 0.5, Op.mult)
-        ts(t("Eb"), ind(t("E"), t("koff", 4, 8)), -2048.0, Op.add)
-        cp(t("OO", 64, 128), ind(t("eye"), t("koff", 4, 8)))
-        tt(t("Q"), t("Eb"), t("OO", 0, 64), Op.mult)
-        mm(t("pV", 0, 64), t("BDh"), t("Q"))
-        ts(t(sa, 32, 96), t("EtU"), -2048.0, Op.add)
-        for dst, lo, q, n in (("Lc", 0, 0, 16), (sa, 96, 16, 32), (sa, 16, 48, 16)):
-            ts(t(dst, lo, lo + n), t("OO", 64 + q, 64 + q + n), -1.0, Op.mult, 1.0, Op.add)
-        segmax(t("Ms", 0, 512), t("rmask", 0, 512), t("G", 0, 512))
-        for dst, lo, q, n in (("Lc", 16, 0, 16), (sa, 128, 16, 32), (sa, 0, 48, 16)):
-            tt(t(dst, lo, lo + n), t("pV", q, q + n), t("OO", 64 + q, 64 + q + n), Op.mult)
-        send(sa, "LA%d" % r, MSGA, "ra%d" % r)
-        act(t("kA"), t("pU", 64, 65), Act.Copy, scale=32.0, bias=65536.0 + 1024.0 - 8388608.0)
-        segmax(t("Ms", 512, 1024), t("rmask", 512, 1024), t("G", 512, 1024))
-        tt(t("Yi"), t("Ms", 15, 1024, 16), t("zh"), Op.add)
-        cp(t("Yb"), t("Yi"))
-        mm(t("pU", 0, 64), t("WU"), t("Yb"))
-        mm(t("pV", 128, 192), t("I2"), t("Ms", 15, 1024, 16), True, False)
-        mm(t("pV", 128, 192), t("In"), t("zb"), False, True)
-        for lo, q, n in ((0, 0, 16), (96, 16, 32), (80, 48, 16)):
-            act(t(sb, lo, lo + n), t("pV", 128 + q, 128 + q + n), Act.Abs)
-        cp(t("si"), t("pU", 0, 64))
-        ts(t("ui"), t("si"), 4095, AND)
-        ts(t("w6"), t("si"), 63, AND)
-        ts(t("u1"), t("ui"), -2048.0, Op.add)
-        ts(t("u2"), t("ui"), 3232.0, Op.add)
-        tt(t("wv"), t("w6"), t("lb"), Op.add)
-        tt(t("Wc"), t("u1"), t("u2"), Op.mult)
-        segmax(t("ws"), t("rmask", 0, 64), t("wv"))
-        ts(t("Wd"), t("Wc"), 0x1FFE0, AND)
-        cp(t("woff"), t("ws", 15, 64, 16))
-        ts(t(sb, 16, 80), t("Wd"), t("kA"), Op.add)
-        send(sb, "LB%d" % r, MSGB, "rb%d" % r)
-        if r + 1 < RO:
-            for k in range(1, NT):
-                mm(t("pY", 64 * k, 64 * k + 64), perm_b(16 - k), t("Yb"))
-            act(t("Yr", 64, 512), t("pY", 64, 512), Act.Copy)
-        cp(ind(t("tab", 0, 4096), t("woff")), t("Yb"))
-        if r + 1 < RO:
-            for k in range(1, NT):
-                cp(ind(t("tab", 4096 * k, 4096 * k + 4096), t("woff")), t("Yr", 64 * k, 64 * k + 64))
-            merge(r)
-            names_mul(0)
+    def there(e, c):
+        return ready((e, t("tab", 0, c[2] * TW)[1] + t("off", 512 * c[0][0], 512 * c[0][0] + 512)[1], []))
+
+    def take(e, c):
+        chunks.remove(c)
+        gather(e, c[0], c[2])
+
+    def open_half(h, n_t):
+        def go():
+            gate[0] += 1
+        call(go)
+
+    def fork(fn, *a, at=99):
+        s = stream(fn, *a)
+        call(lambda: streams.insert(at, s))
+        return s
+
+    def join(s):
+        put(("J", [], [], 0, s))
+
+    def compare(h, n0, n1, e):
+        bank, col = place(h, n0)
+        o, d = t("cmp", 512 * h + 128 * n0, 512 * h + 128 * n1), t(bank, col, col + 128 * (n1 - n0))
+        if e == "S":
+            act(o, d, Act.Sign, bias=-1784.5)
         else:
-            merge(r)
-            dma("Y", "d_out", outside(T.yx[:, :]), t("tab", 0, 4096))
+            ts(o, d, 1785.0, Op.is_ge, 0.5, Op.subtract)
+        call(lambda: seen.update({bank: False}))
+        if n0 == 0:
+            mm(t("pC", 0, 64), turn(0), t("Km"), True, False)
+        w = 24 if e == "S" else 40
+        for n in range(n0, n1):
+            for s in range(2):
+                c = 32 * s + 8 * n
+                mm(t("pC", c, c + 8), t("cmp", 512 * h + 128 * n, 512 * h + 128 * n + 128), t("o8", w + 8 * s, w + 8 * s + 8),
+                   False, n == 3 and s == 1)
 
-    def receive(r):
-        lb = "LB%d" % r
-        if r + 1 < RO:
-            for lo, q, n in ((0, 0, 16), (96, 16, 32), (80, 48, 16)):
-                act(t("zb", q, q + n), t(lb, lo, lo + n), Act.Copy)
-            mm(t("pV", 64, 128), perm_b(8), t("zb"))
-            act(t("z8"), t("pV", 64, 128), Act.Copy)
-            act(t("zh"), t("zb"), Act.Copy, scale=0.5, bias=-0.25)
-            names_v(0, t(lb, 16, 80), range(4))
-            begin(r + 1)
-            cp(t("Ai"), t("pU", 64, 65))
-            names_v(0, t(lb, 16, 80), range(4, 8))
-            ts(t("Aj"), t("Ai"), 31, AND)
-            names_mul(1)
-            ts(t("ncol"), t("Aj"), -1.0, Op.mult, t("nT"), Op.add)
-            names_v(1, t(lb, 16, 80))
-            ts(t("thr"), t("tmask"), t("ncol"), Op.mult)
+    def field(name, r, h, f):
+        base, st = (LANES, 3) if f < 3 else (PAIRS, 2)
+        lo = (320 * r + base[h][0] if name == "ST" else 384 * r + base[h][1]) + f % 3
+        return t(name, lo, lo + 32 * st - f % 3, st)
+
+    def choose(h):
+        c = 4 * h
+        segmax(t("Sc", 64 * h, 64 * h + 64), t("pC", 0, 64))
+        ts(t("hot", 2 * h, 2 * h + 2), t("Sc", 64 * h + 15, 64 * h + 32, 16), 1024.0, Op.is_ge)
+        cp(t("KI", c, c + 4), t("Sc", 64 * h + 15, 64 * h + 64, 16))
+
+    def pick(h):
+        c = 4 * h
+        ts(t("KJ", c, c + 4), t("KI", c, c + 4), 511, AND)
+        cp(t("koff", c, c + 4), t("KJ", c, c + 4))
+
+    def pairs(r, h, late):
+        c, last = 32 * h, r + 1 == RO
+        act(t("OO", 2 * c, 2 * c + 64), ind(t("eye"), t("koff", 4 * h, 4 * h + 4)))
+        if late:
+            ts(t("Eb", c, c + 32), t("Em", 32, 64), -2048.0, Op.add)
         else:
-            for b in range(4):
-                s = 16 * ORD[b]
-                ts(t("ylf", s, s + 16), t("L16", 16 * b, 16 * b + 16), 2048.0, Op.add)
-            dma("Y", "d_out", outside(T.yl[:, :]), t("ylf"))
-            for lo, b in ((0, 0), (96, 1), (112, 2), (80, 3)):
-                s = 16 * ORD[b]
-                act(t("yzf", s, s + 16), t(lb, lo, lo + 16), Act.Copy)
-            dma("S", "d_out", outside(T.yz[:, :]), t("yzf"))
-            ts(t("Wc"), t(lb, 16, 80), 8388608.0 - 1024.0, Op.add)
-            ts(t("Wd"), t("Wc"), 5, SH, 4095, AND)
-            for b in range(4):
-                s = 16 * ORD[b]
-                cp(t("yaf", s, s + 16), t("Wd", 16 * b, 16 * b + 16))
-            dma("Y", "d_out", outside(T.ya[:, :]), t("yaf", p0=0, p1=128, ps=16))
+            ts(t("Eb", c, c + 32), ind(t("E", 512 * h, 512 * h + 512), t("koff", 4 * h + 2, 4 * h + 4)), -2048.0, Op.add)
+        ts(field("ST", r, h, 0), t("Em", 0, 32) if late else t("EtU", c, c + 32), 0.0 if last else -2048.0, Op.add)
+        tt(t("Q", c, c + 32), t("Eb", c, c + 32), t("OO", 2 * c, 2 * c + 32), Op.mult)
+        if last:
+            mm(t("pV", 0, 32), t("oneh", p1=1), t("c2k", p1=1), True, False)
+        mm(t("pV", 0, 32), t("BD"), t("Q", c, c + 32), not last, True)
+        act(field("ST", r, h, 3), t("OO", 2 * c + 32, 2 * c + 64), scale=-1.0, bias=1.0)
+        tt(field("ST", r, h, 4), t("pV", 0, 32), t("OO", 2 * c + 32, 2 * c + 64), Op.mult)
+
+    def best(h, split):
+        c, m = 32 * h, 512 * h
+        for lo in range(0, 32, split):
+            act(t("G", 16 * lo, 16 * (lo + split)), ind(t("tab", 0, 4096), t("EtU", c + lo, c + lo + split)), scale=0.5)
+        for lo in range(0, 512, 256):
+            segmax(t("Ms", m + lo, m + lo + 256), t("G", lo, lo + 256))
+        mm(t("pU", 0, 32), turn(0), t("dm"), True, False)
+        mm(t("pU", 0, 32), turn(0), t("dm1"), False, False)
+        tt(t("Y16", c, c + 32), t("Ms", m + 15, m + 512, 16), t("zh", c, c + 32), Op.add)
+        mm(t("pU", 0, 32), t("WU"), t("Y16", c, c + 32), False, True)
+
+    def places(h):
+        c = 32 * h
+        segmax(t("ws", c, c + 32), t("pU", 0, 32))
+        ts(t("wr", 2 * h, 2 * h + 2), t("ws", c + 15, c + 32, 16), MAGIC, Op.add, MAGIC, Op.subtract)
+
+    def woff(out, h, b, c0, n):
+        c = 32 * h + 16 * b + 15
+        ts(out, t("tc", c0 + b, c0 + 2 * n, 2), t("ws", c, c + 1), Op.add, t("wr", 2 * h + b, 2 * h + b + 1), Op.subtract)
+
+    def turned(h, n):
+        for k in range(n):
+            mm(t("pY", 32 * k, 32 * k + 32), turn(-k), t("Y16", 32 * h, 32 * h + 32))
+
+    def anchors(r, h):
+        c, m = 32 * h, 512 * h
+        mm(t("pV", 32, 64), t("WU"), t("Y16", c, c + 32))
+        mm(t("pV", 64, 96), turn(0), t("Ms", m + 15, m + 512, 16), True, False)
+        mm(t("pV", 64, 96), t("In"), t("zr", c, c + 32), False, True)
+        cp(t("si", c, c + 32), t("pV", 32, 64))
+        act(field("ST", r, h, 1), t("pV", 64, 96), Act.Abs, scale=2.0)
+        ts(t("ui", c, c + 32), t("si", c, c + 32), 4095, AND)
+        ts(t("u1", c, c + 32), t("ui", c, c + 32), -2048.0, Op.add)
+        ts(t("u2", c, c + 32), t("ui", c, c + 32), 3232.0, Op.add)
+        tt(t("Wc", c, c + 32), t("u1", c, c + 32), t("u2", c, c + 32), Op.mult)
+        ts(t("Wd", c, c + 32), t("Wc", c, c + 32), 0x1FFE0, AND)
+        ts(field("ST", r, h, 2), t("Wd", c, c + 32), t("kA") if h else CC, Op.add)
+
+    def landed(r, h):
+        c = 32 * h
+        for j in range(2):
+            act(t("C2", 2 * c + 32 * j, 2 * c + 32 * j + 32), field("LA", r, h, 2))
+        act(t("zr", c, c + 32), field("LA", r, h, 1))
+        mm(t("pZ", 0, 32), turn(8), t("zr", c, c + 32))
+        act(t("zh", c, c + 32), t("zr", c, c + 32), scale=0.5, bias=1023.75)
+        act(t("zr", 128 + c, 128 + c + 32), t("pZ", 0, 32))
+
+    def receive(r, h):
+        c = 32 * h
+        tt(t("tm", c, c + 32), field("LA", r, h, 0), field("LA", r, h, 3), Op.mult)
+        if r + 1 < RO:
+            s = fork(landed, r, h)
+            tt(t("L16", c, c + 32), t("tm", c, c + 32), field("LA", r, h, 4), Op.add)
+            names(h, s)
+            if h:
+                offsets(1, NT)
+                open_half(1, NT)
+            return
+        lo, pr = 384 * r + LANES[h][1], 384 * r + PAIRS[h][1]
+        ts(t("Wc", c, c + 32), field("LA", r, h, 2), 1 / 32, Op.mult, -32.0 if h else t("LB", 4 * r, 4 * r + 1), Op.add)
+        for q, s, n in RUNS[2 * h:2 * h + 2]:
+            j = q - c
+            tt(t("ylf", s, s + n), t("tm", q, q + n), t("LA", pr + 2 * j + 1, pr + 2 * (j + n), 2), Op.add)
+            act(t("yzf", s, s + n), t("LA", lo + 3 * j + 1, lo + 3 * (j + n), 3))
+        ts(t("Wd", c, c + 32), t("Wc", c, c + 32), 4095, AND)
+        if h:
+            dma("Y", "d_o2", outside(T.yl[:, :]), t("ylf"))
+            dma("S", "d_o2", outside(T.yz[:, :]), t("yzf"))
+        for q, s, n in RUNS[2 * h:2 * h + 2]:
+            cp(t("yaf", s, s + n), t("Wd", q, q + n))
+        if h:
+            dma("Y", "d_o2", outside(T.ya[:, :]), t("yaf", p0=0, p1=128, ps=16))
+
+    got = {}
+
+    def tail0(r):
+        last = r + 1 == RO
+        compare(0, 0, 4, "V")
+        choose(0)
+        pick(0)
+        if r:
+            ts(t("Ei"), ind(t("E", 0, 512), t("koff", 0, 4)), t("LB", 4 * r - 4, 4 * r - 3), Op.add)
+            ts(t("Em"), t("Ei"), 4095, AND)
+            cp(t("EtU", 0, 32), t("Em", 0, 32))
+        else:
+            cp(t("EtU", 0, 32), ind(t("E", 0, 512), t("koff", 0, 2)))
+        s = fork(pairs, r, 0, r > 0)
+        best(0, 16)
+        join(s)
+        anchors(r, 0)
+        send("ST", "LA", 320 * r, 384 * r, MSG[0], "ra%d" % r)
+        if not last:
+            got[r] = fork(receive, r, 0)
+        turned(0, 1 if last else NT)
+        places(0)
+        act(t("Yr1", 256, 288), t("pY", 0, 32), bias=-1024.0)
+        for b in range(2):
+            woff(t("wo1", 16 + b, 17 + b), 0, b, 0, 1)
+        if last:
+            cp(ind(t("spare"), t("wo1", 16, 18)), t("Yr1", 256, 288))
+            for lo in (0, 3072):
+                dma("Y", "d_o1", outside(T.yx[:, lo:lo + 1024]), t("spare", lo, lo + 1024))
+            return
+        act(t("Yr0", 0, 224), t("pY", 32, 256), bias=-1024.0)
+        act(t("Yr0", 224, 240), t("pY", 0, 256, 16), bias=-1024.0)
+        for b in range(2):
+            woff(t("wo0", b, 14, 2), 0, b, 32, 7)
+        ts(t("w6"), t("si", 0, 1), 63, AND)
+        ts(t("wo0", 14, 15), t("w6"), t("pev"), Op.mult, t("padb"), Op.add)
+
+    def thresholds():
+        cp(t("Ai"), t("pC", 64, 65))
+        ts(t("Aj"), t("Ai"), 31, AND)
+        ts(t("ncol"), t("Aj"), -1.0, Op.mult, t("nT"), Op.add)
+        ts(t("thr"), t("gm"), t("ncol"), Op.mult, 0.0625, Op.mult)
+
+    def rest1(r):
+        pairs(r, 1, False)
+        lo = 320 * r + PAIRS[1][0] + 32
+        at = 384 * r + PAIRS[1][1] + 32
+        act(t("LA", at, at + 32), t("ST", lo, lo + 32))
+
+    def tail1(r, first):
+        last = r + 1 == RO
+        compare(1, 3, 4, "S")
+        join(first)
+        if r == 0:
+            for k in range(NT):
+                act(t("tab", TW * k + 4096, TW * k + TW), t("tab", TW * k, TW * k + 64))
+        choose(1)
+        for b in range(4):
+            mm(t("pC", 64, 65), t("BD"), t("hot", b, b + 1), b == 0, b == 3)
+        pick(1)
+        act(t("SA", 4 * r, 4 * r + 1), t("pC", 64, 65), bias=-32.0 if last else 0.0)
+        send("SA", "LB", 4 * r, 4 * r, ((0, 0, 1, 1),), "rc%d" % r)
+        cp(t("EtU", 32, 64), ind(t("E", 512, 1024), t("koff", 4, 6)))
+        act(t("kA"), t("pC", 64, 65), scale=32.0, bias=CC)
+        if not last:
+            cp(ind(t("tab", 4096), t("wo0", 0, 15)), t("Yr0"))
+            th = fork(thresholds)
+        s = fork(rest1, r, at=1)
+        best(1, 16)
+        turned(1, 1 if last else NT)
+        if last:
+            a = fork(anchors, r, 1)
+            places(1)
+            act(t("Yr1", 0, 32), t("pY", 0, 32), bias=-1024.0)
+            for b in range(2):
+                woff(t("wo1", b, b + 1), 1, b, 16, 1)
+            cp(ind(t("tab", 0, 4096), t("wo1", 0, 2)), t("Yr1", 0, 32))
+            dma("Y", "d_o2", outside(T.yx[:, 1024:3072]), t("tab", 1024, 3072))
+            join(s)
+            join(a)
+            send("ST", "LA", 320 * r, 384 * r, MSG[1], "rb%d" % r)
+            receive(r, 0)
+            receive(r, 1)
+            return
+        a = fork(lambda: (anchors(r, 1), join(s), send("ST", "LA", 320 * r, 384 * r, MSG[1], "rb%d" % r), fork(receive, r, 1)), at=1)
+        places(1)
+        act(t("Yr1", 0, 256), t("pY", 0, 256), bias=-1024.0)
+        for b in range(2):
+            woff(t("wo1", b, 16, 2), 1, b, 16, NT)
+        cp(ind(t("tab"), t("wo1")), t("Yr1"))
+        if r + 2 == RO:
+            for lo in (0, 3072):
+                dma("Y", "d_sp", t("spare", lo, lo + 1024), t("tab", lo, lo + 1024))
+        if EARLY:
+            join(a)
+        join(got[r])
+        offsets(0, NT, t("LB", 4 * r, 4 * r + 1))
+        join(th)
+        call(lambda: begin(r + 1))
+        open_half(0, NT)
+
+    def begin(r):
+        for h in range(2):
+            chunks.extend([((h, n, l), 2 * r + h if r else 1, NT if r else 4) for n in range(4) for l in range(16)
+                           if r or h or n not in raw])
+        keep = {}
+
+        def end0():
+            keep[0] = stream(tail0, r)
+            streams.append(keep[0])
+        after[(0, "pD0")] = end0
+        after[(1, "pD1")] = lambda: streams.append(stream(lambda: (join(keep[0]), compare(1, 0, 3, "V"))))
+        after[(1, "pD0")] = lambda: streams.insert(0, stream(lambda: ([join(s) for s in list(streams) if s is not got.get(r)],
+                                                                      tail1(r, keep[0]))))
+
+    for q, s, n in RUNS:
+        ts(t("L16", q, q + n), t("lsi", s, s + n), -2048.0, Op.add)
+    for q, s, n in RUNS:
+        cp(t("anf", q, q + n, p1=8), t("ani", s, s + n, p1=8))
+    cp(t("anf", 64, 65, p1=8), t("thi", p1=8))
+    for c in range(4):
+        mm(t("pU", 32 * c, 32 * c + 32), t("sel", p1=8), t("anf", 32 * (c // 2), 32 * (c // 2) + 32, p1=8))
+    mm(t("pU", 128, 129), t("sel", p1=8), t("anf", 64, 65, p1=8))
+    act(t("C2"), t("pU", 0, 128), scale=32.0, bias=1024.0 - 8388608.0)
+    for q, s, n in RUNS:
+        act(t("zr", q, q + n), t("zi", s, s + n))
+    names(0)
+    for j in range(1, 4):
+        mm(t("pZ", 64 * j, 64 * j + 64), turn(4 * j), t("zr", 0, 64))
+    act(t("zr", 64, 256), t("pZ", 64, 256))
+    act(t("zh"), t("zr", 0, 64), scale=0.5, bias=1023.75)
+    act(t("zn"), t("zr", 0, 32), scale=-1.0)
+    cp(t("off", 0, 128), t("E", 0, 128))
+    cp(t("off", 128, 512), t("E", 128, 512))
+    raw = [2 * (c % 256 // 128) + c // 256 for lo, hi in RAW for c in range(lo, hi, 128)]
+
+    def raw_gathers():
+        for lo in [c for lo, hi in RAW for c in range(lo, hi, 64)]:
+            act(t("rx", 16 * lo, 16 * lo + 1024), ind(t("tab", 0, 4096), t("off", lo, lo + 64)))
+
+    def raw_sums():
+        late_constants()
+        spread("pY", t("zr", 0, 32), True)
+        mm(t("pD0"), t("oneh"), t("thr"), True, False)
+        for n in range(4):
+            lo = 256 * (n % 2) + 128 * (n // 2)
+            if n in raw:
+                mm(t("pD0", 128 * n, 128 * n + 128), t("oneh"), t("zm", 128 * n, 128 * n + 128), False, False)
+            else:
+                for b in range(4):
+                    ts(t("off", lo + b, lo + 128, 4), t("E", lo + b, lo + 128, 4), float(TW * (3 - b)), Op.add)
+        left[(0, "pD0")] = 128
+        names(1)
+        offsets(1, 4)
+        tail_constants()
+        join(rg)
+        open_half(1, 4)
+        for lo, hi in RAW:
+            for i in range(16):
+                tt(t("rm", 16 * lo + i, 16 * hi, 16), t("rx", 16 * lo + i, 16 * hi, 16), t("pY", lo, hi), Op.max)
+
+            def sums(lo=lo, hi=hi):
+                for j in range(lo // 8, hi // 8):
+                    c = (0, 2 * (j % 32 // 16) + j // 32, j % 16)
+                    dist(c, "rx", 128 * j, (16, 1))
+                    dist(c, "rm", 128 * j, (8, 1))
+            call(sums)
 
     begin(0)
-    late_constants()
-    for j in range(NV[0]):
-        q = NH[0] + j
-        ts(t("vd", 128 * j, 128 * j + 64), ind(t("tab", 0, 4 * 4096), off_r(0, 8 * q, 8 * q + 4)), t("zb", q, q + 1), Op.subtract)
-    for r in range(RO):
-        gathers(r)
-        tail(r)
-        receive(r)
+    rg = stream(raw_gathers)
+    streams.extend([rg, stream(raw_sums)])
+    run()
     for s in sorted(total):
         g.wait_ge(T.sem[s], total[s])

@@ -7,10 +7,13 @@ NT = 8
 TW = 4160
 RUNS = ((0, 0, 16), (16, 48, 16), (32, 16, 32))
 SLOT0 = (0, 48, 16, 32)
-FIX, CYC, GAT, SCA, LAT, FAR = 0.05, 0.00083, 0.00125, 0.003, 0.1, 3.6
+FIX, CYC, GAT, SCA, LAT, FAR, FAR_A = 0.05, 0.00083, 0.00125, 0.003, 0.2, 4.0, 3.2
+OVER = 0.01
 T_SMALL, T_X, T_TAB = 2.4, 5.2, 3.2
 WAIT, SLACK = 0.03, 0.12
 EARLY = False
+TURN = ()
+PEND_S, PEND_V, END = 2, 4, 0.3
 RAW = ((0, 256), (256, 384))
 
 SCRATCH = {
@@ -19,23 +22,23 @@ SCRATCH = {
     "vd": ("sbuf", [128, 48 * 128], "bfloat16"),
     "vr": ("sbuf", [128, 48 * 128], "bfloat16"),
     "rx": ("sbuf", [128, 8192], "bfloat16"), "rm": ("sbuf", [128, 8192], "bfloat16"),
-    "W": ("sbuf", [128, 512], "int32"), "E": ("sbuf", [128, 1024], "int32"), "off": ("sbuf", [128, 1024], "uint16"),
+    "W": ("sbuf", [128, 1024], "int32"), "E": ("sbuf", [128, 1024], "int32"), "off": ("sbuf", [128, 1024], "uint16"),
     "L16": ("sbuf", [128, 64], "float16"), "B2": ("sbuf", [128, 128], "float32"), "C2": ("sbuf", [128, 128], "float32"),
     "zr": ("sbuf", [128, 256], "bfloat16"), "zh": ("sbuf", [128, 64], "float32"), "zn": ("sbuf", [128, 32], "bfloat16"),
-    "zi": ("sbuf", [128, 64], "bfloat16"), "zm": ("sbuf", [128, 512], "bfloat16"),
-    "thr": ("sbuf", [128, 512], "float16"), "nT": ("sbuf", [128, 1], "float32"), "ncol": ("sbuf", [128, 1], "float32"),
+    "zi": ("sbuf", [128, 64], "bfloat16"), "zm": ("sbuf", [128, 384], "bfloat16"),
+    "thr": ("sbuf", [128, 384], "float16"), "nT": ("sbuf", [128, 1], "float32"), "ncol": ("sbuf", [128, 1], "float32"),
     "kA": ("sbuf", [128, 1], "float32"), "Ai": ("sbuf", [128, 1], "int32"), "Aj": ("sbuf", [128, 1], "int32"),
     "cmp": ("sbuf", [128, 1024], "bfloat16"), "Sc": ("sbuf", [128, 128], "float32"), "hot": ("sbuf", [128, 4], "bfloat16"),
-    "KI": ("sbuf", [128, 8], "int32"), "KJ": ("sbuf", [128, 8], "int32"), "koff": ("sbuf", [128, 8], "uint16"),
+    "KR": ("sbuf", [128, 8], "float32"), "koff": ("sbuf", [128, 8], "uint16"),
     "Ei": ("sbuf", [128, 64], "int32"), "Em": ("sbuf", [128, 64], "int32"),
     "EtU": ("sbuf", [128, 64], "uint16"), "OO": ("sbuf", [128, 128], "bfloat16"),
     "Eb": ("sbuf", [128, 64], "float32"), "Q": ("sbuf", [128, 64], "float16"),
     "G": ("sbuf", [128, 512], "bfloat16"), "Ms": ("sbuf", [128, 1024], "bfloat16"),
-    "Y16": ("sbuf", [128, 64], "float16"), "Yr0": ("sbuf", [128, 240], "bfloat16"), "Yr1": ("sbuf", [128, 288], "bfloat16"),
+    "Y16": ("sbuf", [128, 64], "float16"), "Yr": ("sbuf", [128, 528], "bfloat16"),
     "si": ("sbuf", [128, 64], "int32"), "ui": ("sbuf", [128, 64], "int32"), "u1": ("sbuf", [128, 64], "float32"),
     "u2": ("sbuf", [128, 64], "float32"), "Wc": ("sbuf", [128, 64], "int32"), "Wd": ("sbuf", [128, 64], "int32"),
     "w6": ("sbuf", [128, 1], "int32"), "ws": ("sbuf", [128, 64], "float32"), "wr": ("sbuf", [128, 4], "float32"),
-    "wo0": ("sbuf", [128, 16], "uint16"), "wo1": ("sbuf", [128, 18], "uint16"),
+    "wo": ("sbuf", [128, 34], "uint16"),
     "tm": ("sbuf", [128, 64], "float32"),
     "ST": ("sbuf", [128, RO * 320], "float32"), "LA": ("sbuf", [128, RO * 384], "float32"),
     "SA": ("sbuf", [128, RO * 4], "float32"), "LB": ("sbuf", [128, RO * 4], "float32"),
@@ -49,26 +52,26 @@ SCRATCH = {
     "pad1": ("sbuf", [128, 1], "float32"), "padb": ("sbuf", [128, 1], "float32"),
     "PH": ("sbuf", [128, 16 * 128], "float16"),
     "BD": ("sbuf", [128, 128], "float16"), "WU": ("sbuf", [128, 128], "float16"), "In": ("sbuf", [128, 128], "float16"),
-    "o8": ("sbuf", [128, 56], "bfloat16"), "sel": ("sbuf", [128, 128], "float32"),
+    "o8": ("sbuf", [128, 56], "bfloat16"), "sel": ("sbuf", [128, 128], "float16"),
     "oneh": ("sbuf", [128, 128], "bfloat16"), "c16": ("sbuf", [128, 512], "bfloat16"), "c2k": ("sbuf", [128, 32], "bfloat16"),
-    "gmi": ("sbuf", [128, 512], "bfloat16"), "gm": ("sbuf", [128, 512], "float16"),
+    "gmi": ("sbuf", [128, 384], "bfloat16"), "gm": ("sbuf", [128, 384], "float16"),
     "kmi": ("sbuf", [128, 64], "int32"), "Km": ("sbuf", [128, 64], "float16"),
     "cfi": ("sbuf", [128, 32], "int32"), "coff": ("sbuf", [128, 32], "uint16"),
     "rmask": ("sbuf", [128, 256], "bfloat16"), "rmi": ("sbuf", [128, 256], "bfloat16"), "dm": ("sbuf", [128, 32], "bfloat16"), "dm1": ("sbuf", [128, 32], "bfloat16"),
     "eyi": ("sbuf", [128, 512], "bfloat16"), "eye": ("sbuf", [128, 512], "bfloat16"),
-    "tci": ("sbuf", [128, 48], "int32"), "tc": ("sbuf", [128, 48], "float32"),
+    "tci": ("sbuf", [128, 32], "float32"), "tc": ("sbuf", [128, 32], "float32"), "pad0": ("sbuf", [128, 1], "float32"),
     "lsi": ("sbuf", [128, 64], "int32"), "ani": ("sbuf", [128, 64], "int32"), "thi": ("sbuf", [128, 1], "int32"),
-    "anf": ("sbuf", [128, 65], "float32"),
+    "anf": ("sbuf", [128, 65], "float16"),
     "ylf": ("sbuf", [128, 64], "float32"), "yaf": ("sbuf", [128, 64], "float32"), "yzf": ("sbuf", [128, 64], "bfloat16"),
 }
 PS = ["pA", "pZ", "pD0", "pD1", "pC", "pV", "pU", "pY"]
 for _n in PS:
     SCRATCH[_n] = ("psum", [128, 512], "float32")
 DM = ["d_ls", "d_an", "d_z", "d_th", "d_x", "d_sp", "d_o1", "d_o2"] + ["d_t%d" % k for k in range(1, NT)]
-SEMAPHORES = ["sV", "sS", "sP", "sG", "lo"] + DM + ["r%s%d" % (a, r) for a in "abc" for r in range(RO)]
-MSG = (((0, 0, 96, 1), (64, 96, 96, 2)), ((128, 192, 80, 2), (208, 272, 80, 3)))
-LANES = ((0, 0), (160, 224))
-PAIRS = ((96, 128), (256, 320))
+SEMAPHORES = ["sV", "sS", "sP", "sG", "lo"] + DM + ["r%s%d" % (a, r) for a in "abcde" for r in range(RO)]
+MSG = ((((0, 0, 64, 1), (32, 64, 64, 2)), ((96, 128, 64, 1),)),
+       (((128, 192, 48, 2), (176, 240, 48, 3)), ((256, 320, 32, 2), (288, 352, 32, 3))))
+AT = (((0, 0), (32, 64), (96, 128)), ((160, 224), (192, 256), (256, 320)))
 MAGIC = 1.5 * 2 ** 29
 CC = 65536.0 + 1024.0 - 8388608.0
 
@@ -106,7 +109,7 @@ def rank_program(g, core, T, topo):
             for a, b, sem, val, w, s2 in acc.get(name, []):
                 over = a < hi and lo < b and (lo - a) % math.gcd(st, s2) == 0
                 if sem == own:
-                    hit = over and w and not isw
+                    hit = over and w and (not isw or name == "tab")
                 elif ps:
                     hit = True
                 else:
@@ -168,20 +171,21 @@ def rank_program(g, core, T, topo):
     def op(q, fn, out, ins, *rest, **kw):
         aps = [a for a in ins if isinstance(a, tuple)]
         reads = [r for a in aps for r in a[1]]
-        if isinstance(kw.get("bias"), tuple):
-            reads = reads + kw["bias"][1]
-            kw["bias"] = kw["bias"][0]
+        for k in ("bias", "scale"):
+            if isinstance(kw.get(k), tuple):
+                reads = reads + kw[k][1]
+                kw[k] = kw[k][0]
         wr = out[1]
         if out[4]:
             reads, wr, c = reads + wr[1:], wr[:1], FIX + SCA * out[2]
         elif q == "P":
-            c = 0.0005 * max(64, out[2])
+            c = CYC * max(64, out[2])
         elif aps and aps[0][4]:
             c = (FIX if q == "V" else 0.065) + GAT * out[2]
         elif q == "G":
             c = 0.13 + 2 * CYC * out[2]
         else:
-            c = FIX + CYC * out[2] * (0.5 if q == "V" and all(a[3] or a[2] == 1 for a in aps + [out]) else 1)
+            c = OVER + CYC * max(64, out[2] * (0.5 if q == "V" and all(a[3] or a[2] == 1 for a in aps + [out]) else 1))
 
         def go():
             prepare(q, reads, wr)
@@ -221,7 +225,7 @@ def rank_program(g, core, T, topo):
             finish(q, i, sem, 16, a[1], out[1], clk[q] + when)
         put((q if q == "S" else "Y", a[1], [] if fresh else out[1], 0.05, go))
 
-    def send(src, land, c0, l0, msg, sem):
+    def send(src, land, c0, l0, msg, sem, far):
         def go():
             prepare("G", [(src, c0 + lo, c0 + lo + w, 1) for lo, at, w, d in msg], [])
             tr = []
@@ -238,7 +242,7 @@ def rank_program(g, core, T, topo):
                 total["lo"] = total.get("lo", 0) + n
                 total[sem] = total.get(sem, 0) + n
             g.remote_dma_fused(tr, local_sem=T.sem.lo)
-            plan[(sem, total[sem])] = clk["G"] + FAR
+            plan[(sem, total[sem])] = clk["G"] + far
             clk["G"] += 0.6
             note([(land, l0 + at, l0 + at + w, 1) for lo, at, w, d in msg], sem, total[sem], True)
         put(("G", [], [], 0, go))
@@ -248,12 +252,10 @@ def rank_program(g, core, T, topo):
     dma("S", "d_th", t("thi", p1=8), outside(T.th[:, 0:1]), T_SMALL)
     dma("Y", "d_z", t("zi"), outside(T.z[:, :]), T_SMALL)
     dma("Y", "d_x", t("tab", 0, 4096), outside(T.x[:, :]), T_X)
-    for k in range(1, NT):
-        lo, hi, when = TW * k, TW * k + 4096, T_X + T_TAB * k
-        for gg in range(8):
-            dma("Y", "d_t%d" % k, t("tab", lo, hi, p0=16 * gg + k, p1=16 * gg + 16), outside(T.x[16 * gg:16 * gg + 16 - k, :]), when, True)
-        for f in range(k):
-            dma("Y", "d_t%d" % k, t("tab", lo, hi, p0=f, p1=128, ps=16), outside(T.x[16 + f - k::16, :]), when, True)
+    for j, k in enumerate([k for k in range(1, NT) if k not in TURN]):
+        lo, hi, when = TW * k, TW * k + 4096, T_X + T_TAB * (j + 1)
+        for f in range(16):
+            dma("Y", "d_t%d" % k, t("tab", lo, hi, p0=f, p1=128, ps=16), outside(T.x[(f - k) % 16::16, :]), when, True)
 
     def iota(out, pattern, base, cm, **kw):
         op("G", g.iota, out, [], pattern, base, cm, **kw)
@@ -263,15 +265,24 @@ def rank_program(g, core, T, topo):
     iota(t("J"), [[-1, 16]], 16, 1)
     iota(t("mh"), [[1, 128]], 0, 0, **SM)
     iota(t("ms"), [[1, 8], [0, 16]], 0, 0, **SM)
-    iota(t("gmi"), [[0, 4], [16, 8], [0, 16]], 0, 0, **SM)
+    iota(t("lm"), [[0, 2], [1, 16]], 0, 0, **SM)
+    iota(t("rmi"), [[0, 16], [32767, 16]], -16384, 0, **SM)
+    for h in range(2):
+        step, base = 64 * (SLOT0[2 * h + 1] - SLOT0[2 * h]), 64 * SLOT0[2 * h]
+        if h:
+            iota(t("tci", 0, 16), [[TW, NT], [step, 2]], base, 0, **SM)
+        else:
+            iota(t("tci", 16, 18), [[step, 2]], base, 0, **SM)
+            iota(t("tci", 18, 32), [[TW, NT - 1], [step, 2]], base + TW - 4096, 0, **SM)
+    iota(t("gmi"), [[0, 3], [16, 8], [0, 16]], 0, 0, **SM)
     iota(t("cfi"), [[16, 2], [0, 16]], 0, 0)
+    for k in range(NT):
+        w = 64 + 16 * (k == NT - 1)
+        iota(t("tab", TW * k + 4096, TW * k + 4096 + w), [[0, w]], 0, 0, **SM)
+    iota(t("c2k"), [[0, 32]], 2048, 0, **SM)
     for s in range(2):
         iota(t("kmi", 32 * s, 32 * s + 32), [[128, 2], [256, 2], [1, 8]], 0, 0)
-    iota(t("lm"), [[0, 2], [1, 16]], 0, 0, **SM)
     iota(t("eyi"), [[-8, 2], [0, 32], [-1, 8]], 15, 0, **SM)
-    iota(t("rmi"), [[0, 16], [32767, 16]], -16384, 0, **SM)
-    for c, h, base in ((0, 0, 0), (16, 1, 0), (32, 0, TW - 4096)):
-        iota(t("tci", c, c + 16), [[TW, NT], [64 * (SLOT0[2 * h + 1] - SLOT0[2 * h]), 2]], base + 64 * SLOT0[2 * h], 0)
     SH, AND = Op.arith_shift_right, Op.bitwise_and
     op("V", g.vector.memset, t("oneh"), [], 1.0)
     op("V", g.vector.memset, t("c16", p1=32), [], 2016.0)
@@ -284,61 +295,64 @@ def rank_program(g, core, T, topo):
     ts(t("tg"), t("J2"), t("pbf"), Op.add)
     cp(t("pff"), t("pj"))
     cp(t("pgf"), t("pk"))
+    ts(t("pm"), t("pi"), 1, AND)
+    ts(t("o8", 0, 8), t("mh", 0, 8), t("pgf"), Op.is_equal)
+    cp(t("podd"), t("pm"))
     for k in range(16):
         ts(t("PH", 128 * k, 128 * k + 128), t("mh"), t("tg", k, k + 1), Op.is_equal)
     ts(t("sel", p1=8), t("ms", p1=8), t("pif", p1=8), Op.is_equal)
+    for c, w in enumerate((2.0, -1.0, -512.0, 512.0, -1024.0, 1024.0)):
+        act(t("o8", 8 * c + 8, 8 * c + 16), t("o8", 0, 8), scale=w)
+    act(t("p8f"), t("pff"), scale=8.0, bias=-255.5)
+    act(t("p64"), t("pff"), scale=64.0, bias=31.5)
+    act(t("pwf"), t("pff"), scale=2.0, bias=1.0)
+    act(t("pad0"), t("pff"), scale=-TW / 2 + 0.5, bias=NT * TW - 4096 - 0.5)
+    act(t("pev"), t("podd"), scale=-1.0, bias=1.0)
+    act(t("dm1"), t("lm"), scale=0.0, bias=-31.5)
+    act(t("pad1"), t("pad0"), Act.Identity, scale=t("podd"))
+    act(t("rmask"), t("rmi"), scale=32.0)
+    act(t("padb"), t("pff"), Act.Identity, scale=TW / 2, bias=t("pad1"))
+    act(t("tc"), t("tci"), Act.Identity, bias=t("p64"))
 
     def turn(k):
         return t("PH", 128 * (k % 16), 128 * (k % 16) + 128)
 
     def late_constants():
-        for k in range(NT):
-            op("V", g.vector.memset, t("tab", TW * k + 4096, TW * k + TW + 16 * (k == NT - 1)), [], 0.0)
-        op("V", g.vector.memset, t("c2k"), [], 2048.0)
-        for c, w in enumerate((1.0, 2.0, -1.0, -512.0, 512.0, -1024.0, 1024.0)):
-            ts(t("o8", 8 * c, 8 * c + 8), t("mh", 0, 8), t("pgf"), Op.is_equal, w, Op.mult)
         ts(t("gm"), t("gmi"), t("pbf"), Op.is_equal)
         ts(t("coff"), t("cfi"), t("pff"), Op.add)
-        ts(t("nT"), t("pU", 128, 129), -1.0, Op.mult, 1785.0, Op.add)
         ts(t("thr"), t("gm"), t("nT"), Op.mult, 0.0625, Op.mult)
-        tt(t("zm"), ind(t("zn"), t("coff")), t("gm"), Op.mult)
+        tt(t("zm"), ind(t("zn"), t("coff", 0, 24)), t("gm"), Op.mult)
 
     def tail_constants():
-        ts(t("rmask"), t("rmi"), 32.0, Op.mult)
-        ts(t("p8f"), t("pff"), 8.0, Op.mult)
-        ts(t("p64"), t("pff"), 64.0, Op.mult, 31.5, Op.add)
-        ts(t("pwf"), t("pff"), 2.0, Op.mult, 1.0, Op.add)
-        ts(t("pm"), t("pi"), 1, AND)
         ts(t("In"), t("mh"), t("pif"), Op.is_equal, -0.5, Op.mult)
         ts(t("BD"), t("ms"), t("pgf"), Op.is_equal)
         ts(t("Km"), t("kmi"), t("p8f"), Op.add)
-        cp(t("podd"), t("pm"))
         ts(t("WU"), t("ms"), t("pgf"), Op.is_equal, t("pwf"), Op.mult)
-        ts(t("tc"), t("tci"), t("p64"), Op.add)
         ts(t("dm"), t("lm"), t("pff"), Op.not_equal, -524288.0, Op.mult)
-        ts(t("dm1"), t("lm"), 0.0, Op.mult, -31.5, Op.add)
         ts(t("eye"), t("eyi"), t("pff"), Op.is_equal)
-        ts(t("pev"), t("podd"), -1.0, Op.mult, 1.0, Op.add)
-        ts(t("pad1"), t("pff"), -TW / 2 + 0.5, Op.mult, NT * TW - 4096 - 0.5, Op.add)
-        ts(t("pad1"), t("pad1"), t("podd"), Op.mult)
-        ts(t("padb"), t("pff"), TW / 2, Op.mult, t("pad1"), Op.add)
 
     def spread(bank, src, first):
         for k in range(16):
             a, b = (15 - k) // 8, (15 - k) % 8
             mm(t(bank, 256 * a + b, 256 * a + 256, 8), turn(k), src, first, first or k == 15)
 
-    def names(h, s=None):
-        mm(t("pA"), t("oneh", p1=1), t("c16", p1=1), True, False)
-        spread("pA", t("L16", 32 * h, 32 * h + 32), False)
+    def names_start(h):
+        mm(t(("pA", "pZ")[h]), t("oneh", p1=1), t("c16", p1=1), True, False)
+
+    def names(h):
+        pa = ("pA", "pZ")[h]
+        spread(pa, t("L16", 32 * h, 32 * h + 32), False)
         double_b(h)
         for b in range(8):
-            tt(t("pA", b, 512, 8), t("pA", b, 512, 8), t("B2", 64 * h, 64 * h + 64), Op.mult)
-        if s is not None:
-            join(s)
+            tt(t(pa, b, 512, 8), t(pa, b, 512, 8), t("B2", 64 * h, 64 * h + 64), Op.mult)
+
+    def names_end(h, cut=0):
+        pa, c = ("pA", "pZ")[h], 512 * h
         for b in range(8):
-            tt(t("W", b, 512, 8), t("pA", b, 512, 8), t("C2", 64 * h, 64 * h + 64), Op.add)
-        ts(t("E", 512 * h, 512 * h + 512), t("W"), 5, SH, 4095, AND)
+            tt(t("W", c + b, c + 512, 8), t(pa, b, 512, 8), t("C2", 64 * h, 64 * h + 64), Op.add)
+        for lo, hi in ((0, cut), (cut, 512)):
+            if hi > lo:
+                ts(t("E", c + lo, c + hi), t("W", c + lo, c + hi), 5, SH, 4095, AND)
 
     def offsets(h, n, A=None):
         for b in range(n):
@@ -352,17 +366,26 @@ def rank_program(g, core, T, topo):
         for c in range(2):
             ts(t("B2", 64 * h + 32 * c, 64 * h + 32 * c + 32), t("L16", 32 * h, 32 * h + 32), 2080.0, Op.add)
 
-    streams, chunks, gate = [], [], [0]
+    streams, chunks, gate, marks, must = [], [], [0], [], []
     seen = {"pD0": True, "pD1": False}
     ring, pend, left, after = {"S": 0, "V": 0}, {"S": [], "V": []}, {}, {}
 
     def place(h, n):
-        return ("pD0", 128 * n) if h == 0 else ("pD1", 128 * n) if n < 3 else ("pD0", 0)
+        return ("pD0", 128 * n) if n < 3 else ("pD1", 0)
 
     def dist(c, src, lo, w):
         h, n, l = c
         bank, col = place(h, n)
         key = (h, bank)
+        if left.get(key, 0) == 0:
+            for s in must:
+                while s:
+                    s.pop(0)[4]()
+            n_col = 128 if n == 3 else 384
+            assert not seen[bank]
+            left[key] = n_col // 4
+            seen[bank] = True
+            mm(t(bank, 0, n_col), t("oneh"), t("thr", 0, n_col), True, False)
         left[key] -= w[1]
         mm(t(bank, col + l, col + l + 113, 16), t(src, lo, lo + 128), t("o8", w[0], w[0] + 8), False, left[key] == 0)
         if left[key] == 0:
@@ -385,12 +408,6 @@ def rank_program(g, core, T, topo):
         h, n, l = c
         q, a = 16 * (n // 2) + l, n % 2
         bank, col = place(h, n)
-        if (h, bank) not in left or left[(h, bank)] == 0:
-            w = 128 if (h, n) == (1, 3) else 512 - 128 * h
-            assert not seen[bank]
-            left[(h, bank)] = w // 4
-            seen[bank] = True
-            mm(t(bank, 0, w), t("oneh"), t("thr", 0, w), True, False)
         if e == "V" and ring[e] == 48:
             flush(e)
         ring[e] %= 64 if e == "S" else 48
@@ -407,12 +424,14 @@ def rank_program(g, core, T, topo):
                 ts(t("vd", lo + w * s, lo + w * s + w), src, t("zr", zc, zc + 1), Op.subtract)
         pend[e].append((c, lo))
         rest = len([1 for x in chunks if place(*x[0][:2])[0] == bank and x[0][0] == h])
+        if rest and seen[bank] and left.get((h, bank), 0) == 0:
+            return
         if rest == 0:
             flush("V")
             flush("S")
-        elif e == "S" and len(pend[e]) >= (2 if rest <= 8 else 4):
+        elif e == "S" and len(pend[e]) >= (2 if rest <= 8 else PEND_S):
             flush(e)
-        elif e == "V" and len(pend[e]) >= (4 if rest <= 16 else 9):
+        elif e == "V" and len(pend[e]) >= (4 if rest <= 16 else PEND_V):
             flush(e, 1)
 
     def ready(step):
@@ -421,10 +440,12 @@ def rank_program(g, core, T, topo):
     def run():
         while chunks or any(streams):
             streams[:] = [s for s in streams if s]
-            s = next((s for s in streams if s[0][0] not in ("S", "V")), None)
+            s = next((s for s in streams if s[0][0] not in ("S", "V") and (s[0][0] != "W" or s[0][4] in marks)), None)
             if s is not None:
                 step = s.pop(0)
-                if step[0] != "J":
+                if step[0] == "W":
+                    pass
+                elif step[0] != "J":
                     step[4]()
                 elif step[4] is not s:
                     s[:0] = step[4]
@@ -433,15 +454,17 @@ def rank_program(g, core, T, topo):
             open_ = [c for c in chunks if c[1] <= gate[0]]
             can = []
             for j, s in enumerate(streams):
+                if s[0][0] == "W":
+                    continue
                 e, at = s[0][0], max(ready(s[0]), clk[s[0][0]])
                 if j and streams[0][0][0] == e and at + s[0][3] > ready(streams[0][0]) + SLACK:
                     continue
                 can.append((max(at - WAIT, clk[e]), j, s))
             if open_:
-                per = 0.23 * (1.3 if open_[0][2] == 4 else 1)
+                per = 0.065 * NT / open_[0][2] + 128 * GAT
                 for e in "SV":
                     at = max(there(e, open_[0]), clk[e])
-                    if e == "S" or at + per + 0.3 < clk["S"] + per * len(chunks):
+                    if e == "S" or at + per + END < clk["S"] + per * len(chunks):
                         can.append((at, 99, e))
             at, j, s = min(can, key=lambda c: c[:2])
             if j == 99:
@@ -469,6 +492,12 @@ def rank_program(g, core, T, topo):
     def join(s):
         put(("J", [], [], 0, s))
 
+    def mark(key):
+        call(lambda: marks.append(key))
+
+    def until(key):
+        put(("W", [], [], 0, key))
+
     def compare(h, n0, n1, e):
         bank, col = place(h, n0)
         o, d = t("cmp", 512 * h + 128 * n0, 512 * h + 128 * n1), t(bank, col, col + 128 * (n1 - n0))
@@ -487,25 +516,28 @@ def rank_program(g, core, T, topo):
                    False, n == 3 and s == 1)
 
     def field(name, r, h, f):
-        base, st = (LANES, 3) if f < 3 else (PAIRS, 2)
-        lo = (320 * r + base[h][0] if name == "ST" else 384 * r + base[h][1]) + f % 3
-        return t(name, lo, lo + 32 * st - f % 3, st)
+        lo = (320 * r if name == "ST" else 384 * r) + AT[h][(f + 1) // 2][name == "LA"]
+        return t(name, lo, lo + 32) if f == 0 else t(name, lo + 1 - f % 2, lo + 64, 2)
+
+    def post(r, h, j):
+        send("ST", "LA", 320 * r, 384 * r, MSG[h][j], "r%s%d" % ("abde"[2 * h + j], r), FAR)
 
     def choose(h):
         c = 4 * h
         segmax(t("Sc", 64 * h, 64 * h + 64), t("pC", 0, 64))
-        ts(t("hot", 2 * h, 2 * h + 2), t("Sc", 64 * h + 15, 64 * h + 32, 16), 1024.0, Op.is_ge)
-        cp(t("KI", c, c + 4), t("Sc", 64 * h + 15, 64 * h + 64, 16))
+        ts(t("hot", 2 * h, 2 * h + 2), t("Sc", 64 * h + 15, 64 * h + 32, 16), 512.0, Op.is_ge)
+        ts(t("KR", c, c + 4), t("Sc", 64 * h + 15, 64 * h + 64, 16), 16 * MAGIC, Op.add, 16 * MAGIC, Op.subtract)
 
-    def pick(h):
-        c = 4 * h
-        ts(t("KJ", c, c + 4), t("KI", c, c + 4), 511, AND)
-        cp(t("koff", c, c + 4), t("KJ", c, c + 4))
+    def pick(h, j0, j1):
+        for j in range(4 * h + j0, 4 * h + j1):
+            ts(t("koff", j, j + 1), t("Sc", 16 * j + 15, 16 * j + 16), t("KR", j, j + 1), Op.subtract, 255.5, Op.add)
 
     def pairs(r, h, late):
         c, last = 32 * h, r + 1 == RO
         act(t("OO", 2 * c, 2 * c + 64), ind(t("eye"), t("koff", 4 * h, 4 * h + 4)))
         if late:
+            ts(t("Ei"), ind(t("E", 0, 512), t("koff", 0, 4)), t("LB", 4 * r - 4, 4 * r - 3), Op.add)
+            ts(t("Em"), t("Ei"), 4095, AND)
             ts(t("Eb", c, c + 32), t("Em", 32, 64), -2048.0, Op.add)
         else:
             ts(t("Eb", c, c + 32), ind(t("E", 512 * h, 512 * h + 512), t("koff", 4 * h + 2, 4 * h + 4)), -2048.0, Op.add)
@@ -514,17 +546,23 @@ def rank_program(g, core, T, topo):
         if last:
             mm(t("pV", 0, 32), t("oneh", p1=1), t("c2k", p1=1), True, False)
         mm(t("pV", 0, 32), t("BD"), t("Q", c, c + 32), not last, True)
-        act(field("ST", r, h, 3), t("OO", 2 * c + 32, 2 * c + 64), scale=-1.0, bias=1.0)
-        tt(field("ST", r, h, 4), t("pV", 0, 32), t("OO", 2 * c + 32, 2 * c + 64), Op.mult)
+        act(field("ST", r, h, 1), t("OO", 2 * c + 32, 2 * c + 64), scale=-1.0, bias=1.0)
+        tt(field("ST", r, h, 2), t("pV", 0, 32), t("OO", 2 * c + 32, 2 * c + 64), Op.mult)
+        post(r, h, 0)
+        if h:
+            lo, at = 320 * r + AT[1][1][0] + 32, 384 * r + AT[1][1][1] + 32
+            act(t("LA", at, at + 32), t("ST", lo, lo + 32))
+        got[(r, h)] = fork(merge, r, h)
 
-    def best(h, split):
+    def best(h):
         c, m = 32 * h, 512 * h
-        for lo in range(0, 32, split):
-            act(t("G", 16 * lo, 16 * (lo + split)), ind(t("tab", 0, 4096), t("EtU", c + lo, c + lo + split)), scale=0.5)
-        for lo in range(0, 512, 256):
-            segmax(t("Ms", m + lo, m + lo + 256), t("G", lo, lo + 256))
+        win = t("tab", 0, 4096 if h else TW)
         mm(t("pU", 0, 32), turn(0), t("dm"), True, False)
         mm(t("pU", 0, 32), turn(0), t("dm1"), False, False)
+        act(t("G", 0, 256), ind(win, t("EtU", c, c + 16)), scale=0.5)
+        ts(t("G", 256, 512), ind(win, t("EtU", c + 16, c + 32)), 0.5, Op.mult)
+        for lo in range(0, 512, 256):
+            segmax(t("Ms", m + lo, m + lo + 256), t("G", lo, lo + 256))
         tt(t("Y16", c, c + 32), t("Ms", m + 15, m + 512, 16), t("zh", c, c + 32), Op.add)
         mm(t("pU", 0, 32), t("WU"), t("Y16", c, c + 32), False, True)
 
@@ -533,9 +571,9 @@ def rank_program(g, core, T, topo):
         segmax(t("ws", c, c + 32), t("pU", 0, 32))
         ts(t("wr", 2 * h, 2 * h + 2), t("ws", c + 15, c + 32, 16), MAGIC, Op.add, MAGIC, Op.subtract)
 
-    def woff(out, h, b, c0, n):
-        c = 32 * h + 16 * b + 15
-        ts(out, t("tc", c0 + b, c0 + 2 * n, 2), t("ws", c, c + 1), Op.add, t("wr", 2 * h + b, 2 * h + b + 1), Op.subtract)
+    def woff(h, b, n):
+        c, lo = 32 * h + 16 * b + 15, 16 - 16 * h
+        ts(t("wo", lo + b, lo + 2 * n, 2), t("tc", lo + b, lo + 2 * n, 2), t("ws", c, c + 1), Op.add, t("wr", 2 * h + b, 2 * h + b + 1), Op.subtract)
 
     def turned(h, n):
         for k in range(n):
@@ -547,97 +585,105 @@ def rank_program(g, core, T, topo):
         mm(t("pV", 64, 96), turn(0), t("Ms", m + 15, m + 512, 16), True, False)
         mm(t("pV", 64, 96), t("In"), t("zr", c, c + 32), False, True)
         cp(t("si", c, c + 32), t("pV", 32, 64))
-        act(field("ST", r, h, 1), t("pV", 64, 96), Act.Abs, scale=2.0)
+        act(field("ST", r, h, 3), t("pV", 64, 96), Act.Abs, scale=2.0)
         ts(t("ui", c, c + 32), t("si", c, c + 32), 4095, AND)
         ts(t("u1", c, c + 32), t("ui", c, c + 32), -2048.0, Op.add)
         ts(t("u2", c, c + 32), t("ui", c, c + 32), 3232.0, Op.add)
         tt(t("Wc", c, c + 32), t("u1", c, c + 32), t("u2", c, c + 32), Op.mult)
         ts(t("Wd", c, c + 32), t("Wc", c, c + 32), 0x1FFE0, AND)
-        ts(field("ST", r, h, 2), t("Wd", c, c + 32), t("kA") if h else CC, Op.add)
+        ts(field("ST", r, h, 4), t("Wd", c, c + 32), t("kA") if h else CC, Op.add)
+        post(r, h, 1)
 
     def landed(r, h):
         c = 32 * h
         for j in range(2):
-            act(t("C2", 2 * c + 32 * j, 2 * c + 32 * j + 32), field("LA", r, h, 2))
-        act(t("zr", c, c + 32), field("LA", r, h, 1))
-        mm(t("pZ", 0, 32), turn(8), t("zr", c, c + 32))
-        act(t("zh", c, c + 32), t("zr", c, c + 32), scale=0.5, bias=1023.75)
-        act(t("zr", 128 + c, 128 + c + 32), t("pZ", 0, 32))
+            act(t("C2", 2 * c + 32 * j, 2 * c + 32 * j + 32), field("LA", r, h, 4))
+        s = fork(landed_z, r, h)
+        slow.append(s)
+        join(got[(r, h)])
+        names_end(h)
+        join(s)
+        if h:
+            offsets(1, NT)
+            open_half(1, NT)
 
-    def receive(r, h):
+    def landed_z(r, h):
         c = 32 * h
-        tt(t("tm", c, c + 32), field("LA", r, h, 0), field("LA", r, h, 3), Op.mult)
+        act(t("zr", c, c + 32), field("LA", r, h, 3))
+        mm(t("pY", 256 + c, 288 + c), turn(8), t("zr", c, c + 32))
+        act(t("zh", c, c + 32), t("zr", c, c + 32), scale=0.5, bias=1023.75)
+        act(t("zr", 128 + c, 128 + c + 32), t("pY", 256 + c, 288 + c))
+
+    def merge(r, h):
+        c = 32 * h
+        slow.append(rec[0])
         if r + 1 < RO:
-            s = fork(landed, r, h)
-            tt(t("L16", c, c + 32), t("tm", c, c + 32), field("LA", r, h, 4), Op.add)
-            names(h, s)
-            if h:
-                offsets(1, NT)
-                open_half(1, NT)
+            names_start(h)
+        tt(t("tm", c, c + 32), field("LA", r, h, 0), field("LA", r, h, 1), Op.mult)
+        if r + 1 < RO:
+            tt(t("L16", c, c + 32), t("tm", c, c + 32), field("LA", r, h, 2), Op.add)
+            names(h)
             return
-        lo, pr = 384 * r + LANES[h][1], 384 * r + PAIRS[h][1]
-        ts(t("Wc", c, c + 32), field("LA", r, h, 2), 1 / 32, Op.mult, -32.0 if h else t("LB", 4 * r, 4 * r + 1), Op.add)
+        pr = 384 * r + AT[h][1][1]
         for q, s, n in RUNS[2 * h:2 * h + 2]:
             j = q - c
             tt(t("ylf", s, s + n), t("tm", q, q + n), t("LA", pr + 2 * j + 1, pr + 2 * (j + n), 2), Op.add)
-            act(t("yzf", s, s + n), t("LA", lo + 3 * j + 1, lo + 3 * (j + n), 3))
+
+    def out_rest(r, h):
+        c, lo = 32 * h, 384 * r + AT[h][2][1]
+        ts(t("Wc", c, c + 32), field("LA", r, h, 4), 1 / 32, Op.mult, -32.0 if h else t("LB", 4 * r, 4 * r + 1), Op.add)
+        for q, s, n in RUNS[2 * h:2 * h + 2]:
+            act(t("yzf", s, s + n), t("LA", lo + 2 * (q - c), lo + 2 * (q - c + n), 2))
         ts(t("Wd", c, c + 32), t("Wc", c, c + 32), 4095, AND)
         if h:
-            dma("Y", "d_o2", outside(T.yl[:, :]), t("ylf"))
             dma("S", "d_o2", outside(T.yz[:, :]), t("yzf"))
         for q, s, n in RUNS[2 * h:2 * h + 2]:
             cp(t("yaf", s, s + n), t("Wd", q, q + n))
         if h:
             dma("Y", "d_o2", outside(T.ya[:, :]), t("yaf", p0=0, p1=128, ps=16))
 
-    got = {}
+    got, named, slow = {}, {}, []
 
     def tail0(r):
         last = r + 1 == RO
-        compare(0, 0, 4, "V")
+        until(("counted", r))
+        compare(0, 3, 4, "V")
         choose(0)
-        pick(0)
-        if r:
-            ts(t("Ei"), ind(t("E", 0, 512), t("koff", 0, 4)), t("LB", 4 * r - 4, 4 * r - 3), Op.add)
-            ts(t("Em"), t("Ei"), 4095, AND)
-            cp(t("EtU", 0, 32), t("Em", 0, 32))
-        else:
-            cp(t("EtU", 0, 32), ind(t("E", 0, 512), t("koff", 0, 2)))
+        mark(("chosen", r))
+        pick(0, 0, 4)
+        ts(t("EtU", 0, 32), ind(t("E", 0, 512), t("koff", 0, 2)), t("LB", 4 * r - 4, 4 * r - 3) if r else 0.0, Op.add)
         s = fork(pairs, r, 0, r > 0)
-        best(0, 16)
-        join(s)
+        best(0)
         anchors(r, 0)
-        send("ST", "LA", 320 * r, 384 * r, MSG[0], "ra%d" % r)
+        join(s)
         if not last:
-            got[r] = fork(receive, r, 0)
+            named[r] = fork(landed, r, 0)
+            slow.append(named[r])
         turned(0, 1 if last else NT)
         places(0)
-        act(t("Yr1", 256, 288), t("pY", 0, 32), bias=-1024.0)
+        n = 1 if last else NT
+        act(t("Yr", 256, 256 + 32 * n), t("pY", 0, 32 * n), bias=-1024.0)
         for b in range(2):
-            woff(t("wo1", 16 + b, 17 + b), 0, b, 0, 1)
+            woff(0, b, n)
         if last:
-            cp(ind(t("spare"), t("wo1", 16, 18)), t("Yr1", 256, 288))
+            cp(ind(t("spare"), t("wo", 16, 18)), t("Yr", 256, 288))
             for lo in (0, 3072):
                 dma("Y", "d_o1", outside(T.yx[:, lo:lo + 1024]), t("spare", lo, lo + 1024))
             return
-        act(t("Yr0", 0, 224), t("pY", 32, 256), bias=-1024.0)
-        act(t("Yr0", 224, 240), t("pY", 0, 256, 16), bias=-1024.0)
-        for b in range(2):
-            woff(t("wo0", b, 14, 2), 0, b, 32, 7)
+        act(t("Yr", 512, 528), t("pY", 0, 256, 16), bias=-1024.0)
         ts(t("w6"), t("si", 0, 1), 63, AND)
-        ts(t("wo0", 14, 15), t("w6"), t("pev"), Op.mult, t("padb"), Op.add)
+        ts(t("wo", 32, 33), t("w6"), t("pev"), Op.mult, t("padb"), Op.add)
+
+    def write_first():
+        for lo in range(18, 33, 4):
+            hi = min(lo + 4, 33)
+            cp(ind(t("tab", 4096), t("wo", lo, hi)), t("Yr", 16 * lo, 16 * hi))
 
     def thresholds():
         cp(t("Ai"), t("pC", 64, 65))
         ts(t("Aj"), t("Ai"), 31, AND)
         ts(t("ncol"), t("Aj"), -1.0, Op.mult, t("nT"), Op.add)
         ts(t("thr"), t("gm"), t("ncol"), Op.mult, 0.0625, Op.mult)
-
-    def rest1(r):
-        pairs(r, 1, False)
-        lo = 320 * r + PAIRS[1][0] + 32
-        at = 384 * r + PAIRS[1][1] + 32
-        act(t("LA", at, at + 32), t("ST", lo, lo + 32))
 
     def tail1(r, first):
         last = r + 1 == RO
@@ -646,48 +692,50 @@ def rank_program(g, core, T, topo):
         if r == 0:
             for k in range(NT):
                 act(t("tab", TW * k + 4096, TW * k + TW), t("tab", TW * k, TW * k + 64))
+        if not last:
+            w = fork(write_first)
         choose(1)
         for b in range(4):
             mm(t("pC", 64, 65), t("BD"), t("hot", b, b + 1), b == 0, b == 3)
-        pick(1)
+        pick(1, 0, 4)
         act(t("SA", 4 * r, 4 * r + 1), t("pC", 64, 65), bias=-32.0 if last else 0.0)
-        send("SA", "LB", 4 * r, 4 * r, ((0, 0, 1, 1),), "rc%d" % r)
+        send("SA", "LB", 4 * r, 4 * r, ((0, 0, 1, 1),), "rc%d" % r, FAR_A)
+        if last:
+            o = fork(out_rest, r, 0)
         cp(t("EtU", 32, 64), ind(t("E", 512, 1024), t("koff", 4, 6)))
         act(t("kA"), t("pC", 64, 65), scale=32.0, bias=CC)
         if not last:
-            cp(ind(t("tab", 4096), t("wo0", 0, 15)), t("Yr0"))
-            th = fork(thresholds)
-        s = fork(rest1, r, at=1)
-        best(1, 16)
+            must.append(fork(thresholds))
+        s = fork(pairs, r, 1, False, at=1)
+        best(1)
         turned(1, 1 if last else NT)
         if last:
-            a = fork(anchors, r, 1)
+            a = fork(anchors, r, 1, at=0)
             places(1)
-            act(t("Yr1", 0, 32), t("pY", 0, 32), bias=-1024.0)
+            act(t("Yr", 0, 32), t("pY", 0, 32), bias=-1024.0)
             for b in range(2):
-                woff(t("wo1", b, b + 1), 1, b, 16, 1)
-            cp(ind(t("tab", 0, 4096), t("wo1", 0, 2)), t("Yr1", 0, 32))
+                woff(1, b, 1)
+            cp(ind(t("tab", 0, 4096), t("wo", 0, 2)), t("Yr", 0, 32))
             dma("Y", "d_o2", outside(T.yx[:, 1024:3072]), t("tab", 1024, 3072))
-            join(s)
-            join(a)
-            send("ST", "LA", 320 * r, 384 * r, MSG[1], "rb%d" % r)
-            receive(r, 0)
-            receive(r, 1)
+            for x in (s, a, o, got[(r, 0)], got[(r, 1)]):
+                join(x)
+            dma("Y", "d_o2", outside(T.yl[:, :]), t("ylf"))
+            out_rest(r, 1)
             return
-        a = fork(lambda: (anchors(r, 1), join(s), send("ST", "LA", 320 * r, 384 * r, MSG[1], "rb%d" % r), fork(receive, r, 1)), at=1)
+        a = fork(lambda: (anchors(r, 1), join(s), fork(landed, r, 1)), at=1)
         places(1)
-        act(t("Yr1", 0, 256), t("pY", 0, 256), bias=-1024.0)
+        act(t("Yr", 0, 256), t("pY", 0, 256), bias=-1024.0)
         for b in range(2):
-            woff(t("wo1", b, 16, 2), 1, b, 16, NT)
-        cp(ind(t("tab"), t("wo1")), t("Yr1"))
+            woff(1, b, NT)
+        cp(ind(t("tab"), t("wo", 0, 18)), t("Yr", 0, 288))
         if r + 2 == RO:
             for lo in (0, 3072):
                 dma("Y", "d_sp", t("spare", lo, lo + 1024), t("tab", lo, lo + 1024))
         if EARLY:
             join(a)
-        join(got[r])
+        join(w)
+        join(named[r])
         offsets(0, NT, t("LB", 4 * r, 4 * r + 1))
-        join(th)
         call(lambda: begin(r + 1))
         open_half(0, NT)
 
@@ -700,40 +748,70 @@ def rank_program(g, core, T, topo):
         def end0():
             keep[0] = stream(tail0, r)
             streams.append(keep[0])
-        after[(0, "pD0")] = end0
-        after[(1, "pD1")] = lambda: streams.append(stream(lambda: (join(keep[0]), compare(1, 0, 3, "V"))))
-        after[(1, "pD0")] = lambda: streams.insert(0, stream(lambda: ([join(s) for s in list(streams) if s is not got.get(r)],
+        after[(0, "pD0")] = lambda: streams.insert(0, stream(lambda: (compare(0, 0, 3, "V"), mark(("counted", r)))))
+        after[(0, "pD1")] = end0
+        after[(1, "pD0")] = lambda: streams.append(stream(lambda: (until(("chosen", r)), compare(1, 0, 3, "V"))))
+        after[(1, "pD1")] = lambda: streams.insert(0, stream(lambda: ([join(s) for s in list(streams) if not any(s is x for x in slow)],
                                                                       tail1(r, keep[0]))))
 
+    names_start(0)
     for q, s, n in RUNS:
         ts(t("L16", q, q + n), t("lsi", s, s + n), -2048.0, Op.add)
     for q, s, n in RUNS:
-        cp(t("anf", q, q + n, p1=8), t("ani", s, s + n, p1=8))
-    cp(t("anf", 64, 65, p1=8), t("thi", p1=8))
-    for c in range(4):
-        mm(t("pU", 32 * c, 32 * c + 32), t("sel", p1=8), t("anf", 32 * (c // 2), 32 * (c // 2) + 32, p1=8))
-    mm(t("pU", 128, 129), t("sel", p1=8), t("anf", 64, 65, p1=8))
-    act(t("C2"), t("pU", 0, 128), scale=32.0, bias=1024.0 - 8388608.0)
+        ts(t("anf", q, q + n, p1=8), t("ani", s, s + n, p1=8), -2048.0, Op.add)
+    ts(t("anf", 64, 65, p1=8), t("thi", p1=8), -2048.0, Op.add)
     for q, s, n in RUNS:
         act(t("zr", q, q + n), t("zi", s, s + n))
     names(0)
+    for c in range(4):
+        mm(t("pU", 32 * c, 32 * c + 32), t("sel", p1=8), t("anf", 32 * (c // 2), 32 * (c // 2) + 32, p1=8))
+    mm(t("pU", 128, 129), t("sel", p1=8), t("anf", 64, 65, p1=8))
+    act(t("C2"), t("pU", 0, 128), scale=32.0, bias=CC)
+    act(t("nT"), t("pU", 128, 129), scale=-1.0, bias=1785.0 - 2048.0)
     for j in range(1, 4):
         mm(t("pZ", 64 * j, 64 * j + 64), turn(4 * j), t("zr", 0, 64))
-    act(t("zr", 64, 256), t("pZ", 64, 256))
-    act(t("zh"), t("zr", 0, 64), scale=0.5, bias=1023.75)
     act(t("zn"), t("zr", 0, 32), scale=-1.0)
-    cp(t("off", 0, 128), t("E", 0, 128))
-    cp(t("off", 128, 512), t("E", 128, 512))
+    act(t("zh"), t("zr", 0, 64), scale=0.5, bias=1023.75)
+    act(t("zr", 64, 256), t("pZ", 64, 256))
+    spread("pY", t("zr", 0, 32), True)
+    names_start(1)
+    names_end(0, 64)
+    cp(t("off", 0, 64), t("E", 0, 64))
+    cp(t("off", 64, 512), t("E", 64, 512))
     raw = [2 * (c % 256 // 128) + c // 256 for lo, hi in RAW for c in range(lo, hi, 128)]
 
+    def sums(src, w, lo, hi):
+        def go():
+            for j in range(lo // 8, hi // 8):
+                dist((0, 2 * (j % 32 // 16) + j // 32, j % 16), src, 128 * j, (w, 1))
+        call(go)
+
     def raw_gathers():
-        for lo in [c for lo, hi in RAW for c in range(lo, hi, 64)]:
+        todo = [c for lo, hi in RAW for c in range(lo, hi, 64)]
+        for j, lo in enumerate(todo):
             act(t("rx", 16 * lo, 16 * lo + 1024), ind(t("tab", 0, 4096), t("off", lo, lo + 64)))
+            mark(("raw", lo))
+            if j:
+                until("first")
+                sums("rx", 16, todo[j - 1], todo[j - 1] + 64)
+        sums("rx", 16, lo, lo + 64)
+        for k in TURN:
+            for j in range(8):
+                bank = ("pD1", "pV")[j % 2]
+                mm(t(bank), turn(-k), t("tab", 512 * j, 512 * j + 512))
+                act(t("tab", TW * k + 512 * j, TW * k + 512 * j + 512), t(bank))
+        mark("turned")
 
     def raw_sums():
+        for lo, hi in RAW:
+            until(("raw", hi - 64))
+            for i in range(16):
+                tt(t("rm", 16 * lo + i, 16 * hi, 16), t("rx", 16 * lo + i, 16 * hi, 16), t("pY", lo, hi), Op.max)
+            sums("rm", 8, lo, hi)
+
+    def first_sums():
         late_constants()
-        spread("pY", t("zr", 0, 32), True)
-        mm(t("pD0"), t("oneh"), t("thr"), True, False)
+        mm(t("pD0", 0, 384), t("oneh"), t("thr"), True, False)
         for n in range(4):
             lo = 256 * (n % 2) + 128 * (n // 2)
             if n in raw:
@@ -741,26 +819,19 @@ def rank_program(g, core, T, topo):
             else:
                 for b in range(4):
                     ts(t("off", lo + b, lo + 128, 4), t("E", lo + b, lo + 128, 4), float(TW * (3 - b)), Op.add)
-        left[(0, "pD0")] = 128
-        names(1)
-        offsets(1, 4)
-        tail_constants()
-        join(rg)
-        open_half(1, 4)
-        for lo, hi in RAW:
-            for i in range(16):
-                tt(t("rm", 16 * lo + i, 16 * hi, 16), t("rx", 16 * lo + i, 16 * hi, 16), t("pY", lo, hi), Op.max)
+        left[(0, "pD0")] = 96
+        mark("first")
 
-            def sums(lo=lo, hi=hi):
-                for j in range(lo // 8, hi // 8):
-                    c = (0, 2 * (j % 32 // 16) + j // 32, j % 16)
-                    dist(c, "rx", 128 * j, (16, 1))
-                    dist(c, "rm", 128 * j, (8, 1))
-            call(sums)
+    def second_names():
+        names(1)
+        names_end(1)
+        offsets(1, 4)
+        until("turned")
+        open_half(1, 4)
+        tail_constants()
 
     begin(0)
-    rg = stream(raw_gathers)
-    streams.extend([rg, stream(raw_sums)])
+    streams.extend([stream(raw_sums), stream(first_sums), stream(raw_gathers), stream(second_names)])
     run()
     for s in sorted(total):
         g.wait_ge(T.sem[s], total[s])

@@ -7,20 +7,22 @@ NT = 8
 TW = 4160
 RUNS = ((0, 0, 16), (16, 48, 16), (32, 16, 32))
 SLOT0 = (0, 48, 16, 32)
-FIX, CYC, GAT, SCA, LAT, FAR, FAR_A = 0.05, 0.00083, 0.00125, 0.003, 0.2, 4.0, 3.2
-OVER = 0.01
-T_SMALL, T_X, T_TAB = 2.4, 5.2, 3.2
+FIX, CYC, GAT, SCA, LAT, FAR, FAR_A = 0.05, 0.00083, 0.00125, 0.003, 0.2, 4.0, 3.0
+OVER = 0.0
+T_SMALL, T_X, T_TAB = 2.4, 4.6, 1.8
 WAIT, SLACK = 0.03, 0.12
-EARLY = False
-TURN = ()
-PEND_S, PEND_V, END = 2, 4, 0.3
-RAW = ((0, 256), (256, 384))
+HALVES, BEST_S = 5, (16, 32)
+STRETCH, LONG, PAIR_AT, TAIL_AT = 0.1, 3, 99, 99
+LATER = (0.0, 0.0)
+LEAVE, LAT_P, NEAR = 3, 0.2, 2
+PEND_S, PEND_V, END = 2, 3, 0.3
+COPIES = (1, 1, 1, 4, 4, 8, 8, 8)
 
 SCRATCH = {
     "tab": ("sbuf", [128, NT * TW + 16], "bfloat16"), "spare": ("sbuf", [128, 4096], "bfloat16"),
     "sd": ("sbuf", [128, 64 * 128], "bfloat16"),
     "vd": ("sbuf", [128, 48 * 128], "bfloat16"),
-    "vr": ("sbuf", [128, 48 * 128], "bfloat16"),
+    "vr": ("sbuf", [128, 48 * 128], "float16"), "zq": ("sbuf", [128, 256], "bfloat16"),
     "rx": ("sbuf", [128, 8192], "bfloat16"), "rm": ("sbuf", [128, 8192], "bfloat16"),
     "W": ("sbuf", [128, 1024], "int32"), "E": ("sbuf", [128, 1024], "int32"), "off": ("sbuf", [128, 1024], "uint16"),
     "L16": ("sbuf", [128, 64], "float16"), "B2": ("sbuf", [128, 128], "float32"), "C2": ("sbuf", [128, 128], "float32"),
@@ -32,15 +34,15 @@ SCRATCH = {
     "KR": ("sbuf", [128, 8], "float32"), "koff": ("sbuf", [128, 8], "uint16"),
     "Ei": ("sbuf", [128, 64], "int32"), "Em": ("sbuf", [128, 64], "int32"),
     "EtU": ("sbuf", [128, 64], "uint16"), "OO": ("sbuf", [128, 128], "bfloat16"),
-    "Eb": ("sbuf", [128, 64], "float32"), "Q": ("sbuf", [128, 64], "float16"),
+    "BD32": ("sbuf", [128, 128], "float32"), "Q": ("sbuf", [128, 64], "float32"),
     "G": ("sbuf", [128, 512], "bfloat16"), "Ms": ("sbuf", [128, 1024], "bfloat16"),
     "Y16": ("sbuf", [128, 64], "float16"), "Yr": ("sbuf", [128, 528], "bfloat16"),
     "si": ("sbuf", [128, 64], "int32"), "ui": ("sbuf", [128, 64], "int32"), "u1": ("sbuf", [128, 64], "float32"),
-    "u2": ("sbuf", [128, 64], "float32"), "Wc": ("sbuf", [128, 64], "int32"), "Wd": ("sbuf", [128, 64], "int32"),
+    "Wc": ("sbuf", [128, 64], "int32"), "Wd": ("sbuf", [128, 64], "int32"),
     "w6": ("sbuf", [128, 1], "int32"), "ws": ("sbuf", [128, 64], "float32"), "wr": ("sbuf", [128, 4], "float32"),
     "wo": ("sbuf", [128, 34], "uint16"),
     "tm": ("sbuf", [128, 64], "float32"),
-    "ST": ("sbuf", [128, RO * 320], "float32"), "LA": ("sbuf", [128, RO * 384], "float32"),
+    "ST": ("sbuf", [128, RO * 352], "float32"), "LA": ("sbuf", [128, RO * 416], "float32"),
     "SA": ("sbuf", [128, RO * 4], "float32"), "LB": ("sbuf", [128, RO * 4], "float32"),
     "J": ("sbuf", [128, 16], "int32"), "J2": ("sbuf", [128, 16], "int32"), "tg": ("sbuf", [128, 16], "float32"),
     "mh": ("sbuf", [128, 128], "bfloat16"), "ms": ("sbuf", [128, 128], "bfloat16"), "lm": ("sbuf", [128, 32], "bfloat16"),
@@ -59,7 +61,7 @@ SCRATCH = {
     "cfi": ("sbuf", [128, 32], "int32"), "coff": ("sbuf", [128, 32], "uint16"),
     "rmask": ("sbuf", [128, 256], "bfloat16"), "rmi": ("sbuf", [128, 256], "bfloat16"), "dm": ("sbuf", [128, 32], "bfloat16"), "dm1": ("sbuf", [128, 32], "bfloat16"),
     "eyi": ("sbuf", [128, 512], "bfloat16"), "eye": ("sbuf", [128, 512], "bfloat16"),
-    "tci": ("sbuf", [128, 32], "float32"), "tc": ("sbuf", [128, 32], "float32"), "pad0": ("sbuf", [128, 1], "float32"),
+    "tci": ("sbuf", [128, 34], "float32"), "tc": ("sbuf", [128, 34], "float32"), "pad0": ("sbuf", [128, 1], "float32"),
     "lsi": ("sbuf", [128, 64], "int32"), "ani": ("sbuf", [128, 64], "int32"), "thi": ("sbuf", [128, 1], "int32"),
     "anf": ("sbuf", [128, 65], "float16"),
     "ylf": ("sbuf", [128, 64], "float32"), "yaf": ("sbuf", [128, 64], "float32"), "yzf": ("sbuf", [128, 64], "bfloat16"),
@@ -69,11 +71,12 @@ for _n in PS:
     SCRATCH[_n] = ("psum", [128, 512], "float32")
 DM = ["d_ls", "d_an", "d_z", "d_th", "d_x", "d_sp", "d_o1", "d_o2"] + ["d_t%d" % k for k in range(1, NT)]
 SEMAPHORES = ["sV", "sS", "sP", "sG", "lo"] + DM + ["r%s%d" % (a, r) for a in "abcde" for r in range(RO)]
-MSG = ((((0, 0, 64, 1), (32, 64, 64, 2)), ((96, 128, 64, 1),)),
-       (((128, 192, 48, 2), (176, 240, 48, 3)), ((256, 320, 32, 2), (288, 352, 32, 3))))
-AT = (((0, 0), (32, 64), (96, 128)), ((160, 224), (192, 256), (256, 320)))
+MSG = ((((0, 0, 64, 1), (32, 64, 64, 2)), ((96, 128, 96, 1),)),
+       (((160, 224, 48, 2), (208, 272, 48, 3)), ((288, 352, 32, 2), (320, 384, 32, 3))))
+WS, WL = 352, 416
+AT = (((0, 0), (32, 64), (96, 128)), ((192, 256), (224, 288), (288, 352)))
 MAGIC = 1.5 * 2 ** 29
-CC = 65536.0 + 1024.0 - 8388608.0
+CC = 1024.0 - 8388608.0
 
 
 def rank_program(g, core, T, topo):
@@ -108,8 +111,10 @@ def rank_program(g, core, T, topo):
             ps = name in PS
             for a, b, sem, val, w, s2 in acc.get(name, []):
                 over = a < hi and lo < b and (lo - a) % math.gcd(st, s2) == 0
+                if over and min(hi - lo, b - a) < max(st, s2):
+                    over = bool(set(range(lo, hi, st)) & set(range(a, b, s2)))
                 if sem == own:
-                    hit = over and w and (not isw or name == "tab")
+                    hit = over and w and (not isw or q != "P")
                 elif ps:
                     hit = True
                 else:
@@ -179,7 +184,7 @@ def rank_program(g, core, T, topo):
         if out[4]:
             reads, wr, c = reads + wr[1:], wr[:1], FIX + SCA * out[2]
         elif q == "P":
-            c = CYC * max(64, out[2])
+            c = CYC * max(64, out[2]) * (1 if aps[0][3] else 4)
         elif aps and aps[0][4]:
             c = (FIX if q == "V" else 0.065) + GAT * out[2]
         elif q == "G":
@@ -191,7 +196,7 @@ def rank_program(g, core, T, topo):
             prepare(q, reads, wr)
             i = fn(out[0], *([a[0] if isinstance(a, tuple) else a for a in ins] + list(rest)), **kw)
             clk[q] += c
-            finish(q, i, "s" + q, 1, reads, wr, clk[q] + LAT)
+            finish(q, i, "s" + q, 1, reads, wr, clk[q] + (LAT_P if q == "P" else LAT))
         put((q, reads, wr, c, go))
 
     def call(fn):
@@ -252,8 +257,8 @@ def rank_program(g, core, T, topo):
     dma("S", "d_th", t("thi", p1=8), outside(T.th[:, 0:1]), T_SMALL)
     dma("Y", "d_z", t("zi"), outside(T.z[:, :]), T_SMALL)
     dma("Y", "d_x", t("tab", 0, 4096), outside(T.x[:, :]), T_X)
-    for j, k in enumerate([k for k in range(1, NT) if k not in TURN]):
-        lo, hi, when = TW * k, TW * k + 4096, T_X + T_TAB * (j + 1)
+    for k in range(1, NT):
+        lo, hi, when = TW * k, TW * k + 4096, T_X + T_TAB * k
         for f in range(16):
             dma("Y", "d_t%d" % k, t("tab", lo, hi, p0=f, p1=128, ps=16), outside(T.x[(f - k) % 16::16, :]), when, True)
 
@@ -270,34 +275,34 @@ def rank_program(g, core, T, topo):
     for h in range(2):
         step, base = 64 * (SLOT0[2 * h + 1] - SLOT0[2 * h]), 64 * SLOT0[2 * h]
         if h:
-            iota(t("tci", 0, 16), [[TW, NT], [step, 2]], base, 0, **SM)
+            iota(t("tci", 0, 16), [[0, 2], [TW, NT // 2], [step, 2]], base, 0, **SM)
         else:
             iota(t("tci", 16, 18), [[step, 2]], base, 0, **SM)
-            iota(t("tci", 18, 32), [[TW, NT - 1], [step, 2]], base + TW - 4096, 0, **SM)
+            iota(t("tci", 18, 34), [[0, NT // 2], [TW, 2], [step, 2]], base, 0, **SM)
     iota(t("gmi"), [[0, 3], [16, 8], [0, 16]], 0, 0, **SM)
     iota(t("cfi"), [[16, 2], [0, 16]], 0, 0)
     for k in range(NT):
         w = 64 + 16 * (k == NT - 1)
         iota(t("tab", TW * k + 4096, TW * k + 4096 + w), [[0, w]], 0, 0, **SM)
-    iota(t("c2k"), [[0, 32]], 2048, 0, **SM)
+    iota(t("c2k"), [[0, 32]], -2048, 0, **SM)
     for s in range(2):
         iota(t("kmi", 32 * s, 32 * s + 32), [[128, 2], [256, 2], [1, 8]], 0, 0)
     iota(t("eyi"), [[-8, 2], [0, 32], [-1, 8]], 15, 0, **SM)
     SH, AND = Op.arith_shift_right, Op.bitwise_and
     op("V", g.vector.memset, t("oneh"), [], 1.0)
     op("V", g.vector.memset, t("c16", p1=32), [], 2016.0)
-    ts(t("pj"), t("pi"), 15, AND)
     ts(t("pl"), t("pi"), 112, AND)
+    ts(t("pj"), t("pi"), 15, AND)
     ts(t("pk"), t("pi"), 4, SH)
+    ts(t("pm"), t("pi"), 1, AND)
     ts(t("J2"), t("J"), 15, AND)
     cp(t("pbf"), t("pl"))
     cp(t("pif"), t("pi"))
-    ts(t("tg"), t("J2"), t("pbf"), Op.add)
     cp(t("pff"), t("pj"))
     cp(t("pgf"), t("pk"))
-    ts(t("pm"), t("pi"), 1, AND)
-    ts(t("o8", 0, 8), t("mh", 0, 8), t("pgf"), Op.is_equal)
     cp(t("podd"), t("pm"))
+    ts(t("tg"), t("J2"), t("pbf"), Op.add)
+    ts(t("o8", 0, 8), t("mh", 0, 8), t("pgf"), Op.is_equal)
     for k in range(16):
         ts(t("PH", 128 * k, 128 * k + 128), t("mh"), t("tg", k, k + 1), Op.is_equal)
     ts(t("sel", p1=8), t("ms", p1=8), t("pif", p1=8), Op.is_equal)
@@ -326,6 +331,7 @@ def rank_program(g, core, T, topo):
     def tail_constants():
         ts(t("In"), t("mh"), t("pif"), Op.is_equal, -0.5, Op.mult)
         ts(t("BD"), t("ms"), t("pgf"), Op.is_equal)
+        ts(t("BD32"), t("ms"), t("pgf"), Op.is_equal)
         ts(t("Km"), t("kmi"), t("p8f"), Op.add)
         ts(t("WU"), t("ms"), t("pgf"), Op.is_equal, t("pwf"), Op.mult)
         ts(t("dm"), t("lm"), t("pff"), Op.not_equal, -524288.0, Op.mult)
@@ -346,16 +352,16 @@ def rank_program(g, core, T, topo):
         for b in range(8):
             tt(t(pa, b, 512, 8), t(pa, b, 512, 8), t("B2", 64 * h, 64 * h + 64), Op.mult)
 
-    def names_end(h, cut=0):
+    def names_end(h, c2, cut=0):
         pa, c = ("pA", "pZ")[h], 512 * h
         for b in range(8):
-            tt(t("W", c + b, c + 512, 8), t(pa, b, 512, 8), t("C2", 64 * h, 64 * h + 64), Op.add)
+            tt(t("W", c + b, c + 512, 8), t(pa, b, 512, 8), c2, Op.add)
         for lo, hi in ((0, cut), (cut, 512)):
             if hi > lo:
                 ts(t("E", c + lo, c + hi), t("W", c + lo, c + hi), 5, SH, 4095, AND)
 
-    def offsets(h, n, A=None):
-        for b in range(n):
+    def offsets(h, n, A=None, bs=None):
+        for b in bs or range(n):
             o, e = t("off", 512 * h + b, 512 * h + 512, n), t("E", 512 * h + b, 512 * h + 512, n)
             if A is None:
                 ts(o, e, float(TW * (n - 1 - b)), Op.add)
@@ -366,9 +372,9 @@ def rank_program(g, core, T, topo):
         for c in range(2):
             ts(t("B2", 64 * h + 32 * c, 64 * h + 32 * c + 32), t("L16", 32 * h, 32 * h + 32), 2080.0, Op.add)
 
-    streams, chunks, gate, marks, must = [], [], [0], [], []
+    streams, chunks, gate, marks, must, free = [], [], [0], [], [], [False]
     seen = {"pD0": True, "pD1": False}
-    ring, pend, left, after = {"S": 0, "V": 0}, {"S": [], "V": []}, {}, {}
+    ring, pend, left, after, begun = {"S": 0, "V": 0}, {"S": [], "V": []}, {}, {}, {}
 
     def place(h, n):
         return ("pD0", 128 * n) if n < 3 else ("pD1", 0)
@@ -394,45 +400,57 @@ def rank_program(g, core, T, topo):
     def flush(e, keep=0):
         now = pend[e][:len(pend[e]) - keep]
         del pend[e][:len(now)]
-        if e == "V" and now:
-            a, b = now[0][1], now[-1][1] + 128
-            ts(t("vr", a, b), t("vd", a, b), 0.0, Op.max)
-        for c, lo in reversed(now):
-            if e == "S":
-                dist(c, "sd", lo, (0, 2))
-            else:
-                dist(c, "vr", lo, (8, 1))
+        if e == "V":
+            for c, lo, n_t in now:
                 dist(c, "vd", lo, (16, 1))
+            for c, lo, n_t in now:
+                for s in range(8 // n_t):
+                    a, zc = lo + 16 * n_t * s, z_at(c, n_t, s)
+                    ts(t("vr", a, a + 16 * n_t), t("vd", a, a + 16 * n_t), t("zr", zc, zc + 1), Op.max, t("zq", zc, zc + 1), Op.subtract)
+        for c, lo, n_t in now if e == "V" else reversed(now):
+            dist(c, "vr" if e == "V" else "sd", lo, (8, 1) if e == "V" else (0, 2))
 
-    def gather(e, c, n_t):
+    def z_at(c, n_t, s):
         h, n, l = c
-        q, a = 16 * (n // 2) + l, n % 2
+        return 64 * ((15 - 8 * (n % 2) - n_t * s) // n_t * n_t // 4) + 32 * h + 16 * (n // 2) + l
+
+    def gather(e, c, n_t, m):
+        h, n, l = c
+        o = 512 * h + 256 * (n % 2) + 128 * (n // 2) + 8 * l
         bank, col = place(h, n)
-        if e == "V" and ring[e] == 48:
+        if e == "V" and ring[e] + m > 48:
             flush(e)
-        ring[e] %= 64 if e == "S" else 48
-        lo = 128 * ring[e]
-        ring[e] += 1
-        for s in range(8 // n_t):
-            o = 512 * h + 256 * a + 8 * q + n_t * s
-            src = ind(t("tab", 0, n_t * TW), t("off", o, o + n_t))
-            zc = 64 * ((15 - 8 * a - n_t * s) // n_t * n_t // 4) + 32 * h + q
-            w = 16 * n_t
-            if e == "S":
-                act(t("sd", lo + w * s, lo + w * s + w), src, Act.Abs, bias=t("zr", zc, zc + 1), scale=-1.0)
-            else:
-                ts(t("vd", lo + w * s, lo + w * s + w), src, t("zr", zc, zc + 1), Op.subtract)
-        pend[e].append((c, lo))
+            ring[e] = 0
+        if c in begun:
+            lo = begun.pop(c)
+            act(t("sd", lo, lo + 64), ind(t("tab", 0, NT * TW), t("off", o, o + 4)), Act.Abs, bias=t("zr", 128 + l, 129 + l), scale=-1.0)
+        else:
+            ring[e] %= 64
+            lo = 128 * ring[e]
+            ring[e] += m
+            if e == "V":
+                cp(t("vd", lo, lo + 128 * m), ind(t("tab", 0, n_t * TW), t("off", o, o + 8 * m)))
+            for s in range(8 // n_t if e == "S" else 0):
+                zc, w = z_at(c, n_t, s), 16 * n_t
+                act(t("sd", lo + w * s, lo + w * s + w), ind(t("tab", 0, n_t * TW), t("off", o + n_t * s, o + n_t * s + n_t)), Act.Abs,
+                    bias=t("zr", zc, zc + 1), scale=-1.0)
+        pend[e].extend([((h, n, l + j), lo + 128 * j, n_t) for j in range(m)])
         rest = len([1 for x in chunks if place(*x[0][:2])[0] == bank and x[0][0] == h])
         if rest and seen[bank] and left.get((h, bank), 0) == 0:
             return
         if rest == 0:
             flush("V")
             flush("S")
-        elif e == "S" and len(pend[e]) >= (2 if rest <= 8 else PEND_S):
+        elif e == "S" and len(pend[e]) >= PEND_S:
             flush(e)
-        elif e == "V" and len(pend[e]) >= (4 if rest <= 16 else PEND_V):
-            flush(e, 1)
+
+    def early():
+        for l in range(HALVES):
+            ring["S"] %= 64
+            lo = begun[(0, 0, l)] = 128 * ring["S"]
+            ring["S"] += 1
+            act(t("sd", lo + 64, lo + 128), ind(t("tab", 0, 4 * TW), t("off", 8 * l + 4, 8 * l + 8)), Act.Abs,
+                bias=t("zr", 128 + l, 129 + l), scale=-1.0)
 
     def ready(step):
         return max([0.0] + [plan[e] for e in waits(step[0], step[1], step[2]).items()])
@@ -440,7 +458,11 @@ def rank_program(g, core, T, topo):
     def run():
         while chunks or any(streams):
             streams[:] = [s for s in streams if s]
-            s = next((s for s in streams if s[0][0] not in ("S", "V") and (s[0][0] != "W" or s[0][4] in marks)), None)
+            if len(chunks) > NEAR:
+                free[0] = False
+            near = len(chunks) <= NEAR and not free[0]
+            s = next((s for s in streams if s[0][0] not in ("S", "V") and (s[0][0] != "W" or s[0][4] in marks)
+                      and not (near and s[0][0] == "P" and any(s is x for x in slow))), None)
             if s is not None:
                 step = s.pop(0)
                 if step[0] == "W":
@@ -454,7 +476,7 @@ def rank_program(g, core, T, topo):
             open_ = [c for c in chunks if c[1] <= gate[0]]
             can = []
             for j, s in enumerate(streams):
-                if s[0][0] == "W":
+                if s[0][0] in "WP":
                     continue
                 e, at = s[0][0], max(ready(s[0]), clk[s[0][0]])
                 if j and streams[0][0][0] == e and at + s[0][3] > ready(streams[0][0]) + SLACK:
@@ -468,16 +490,34 @@ def rank_program(g, core, T, topo):
                         can.append((at, 99, e))
             at, j, s = min(can, key=lambda c: c[:2])
             if j == 99:
-                take(s, open_[0])
+                take(s, open_)
             else:
                 s.pop(0)[4]()
 
     def there(e, c):
         return ready((e, t("tab", 0, c[2] * TW)[1] + t("off", 512 * c[0][0], 512 * c[0][0] + 512)[1], []))
 
-    def take(e, c):
-        chunks.remove(c)
-        gather(e, c[0], c[2])
+    def take(e, open_):
+        c, m = open_[0], 1
+        if e == "V":
+            open_ = [x for x in open_ if x[0] not in begun]
+            c = open_[0]
+            key = (c[0][0], place(*c[0][:2])[0])
+            later = [x for x in open_ if (x[0][0], place(*x[0][:2])[0]) != key]
+            close = len(open_) - len(later) <= LEAVE
+            fresh = len([1 for x in pend[e] if ready((e, t("vd", x[1], x[1] + 128)[1], [])) > clk[e] + WAIT])
+            shut = [1 for x in pend[e] if seen[place(*x[0][:2])[0]] and left.get((x[0][0], place(*x[0][:2])[0]), 0) == 0]
+            if len(pend[e]) - fresh >= (1 if close else PEND_V) and not shut:
+                flush(e, max(fresh, len(pend[e]) - 4))
+                return
+            if close and later and not seen[place(*later[0][0][:2])[0]]:
+                c, close = later[0], False
+            due = min([9.0] + [ready(s[0]) - clk[e] if s[0][0] == e else 0.3 for s in streams if s[0][0] != "W"])
+            room = len([1 for x in open_ if x[0][:2] == c[0][:2]]) if not close else 1
+            m = max(1, min(int((due + STRETCH) / (128 * GAT)), LONG, room, (len(chunks) - 4) // 3))
+        j = chunks.index(c)
+        del chunks[j:j + m]
+        gather(e, c[0], c[2], m)
 
     def open_half(h, n_t):
         def go():
@@ -516,17 +556,20 @@ def rank_program(g, core, T, topo):
                    False, n == 3 and s == 1)
 
     def field(name, r, h, f):
-        lo = (320 * r if name == "ST" else 384 * r) + AT[h][(f + 1) // 2][name == "LA"]
+        lo = (WS * r if name == "ST" else WL * r) + AT[h][min(f + 1, 4) // 2][name == "LA"]
+        if h == 0 and f >= 3:
+            lo += 32 * ((f - 4) % 3)
+            return t(name, lo, lo + 32)
         return t(name, lo, lo + 32) if f == 0 else t(name, lo + 1 - f % 2, lo + 64, 2)
 
     def post(r, h, j):
-        send("ST", "LA", 320 * r, 384 * r, MSG[h][j], "r%s%d" % ("abde"[2 * h + j], r), FAR)
+        send("ST", "LA", WS * r, WL * r, MSG[h][j], "r%s%d" % ("abde"[2 * h + j], r), FAR + (LATER[j] if h and r + 1 < RO else 0))
 
     def choose(h):
         c = 4 * h
         segmax(t("Sc", 64 * h, 64 * h + 64), t("pC", 0, 64))
-        ts(t("hot", 2 * h, 2 * h + 2), t("Sc", 64 * h + 15, 64 * h + 32, 16), 512.0, Op.is_ge)
         ts(t("KR", c, c + 4), t("Sc", 64 * h + 15, 64 * h + 64, 16), 16 * MAGIC, Op.add, 16 * MAGIC, Op.subtract)
+        ts(t("hot", 2 * h, 2 * h + 2), t("Sc", 64 * h + 15, 64 * h + 32, 16), 512.0, Op.is_ge)
 
     def pick(h, j0, j1):
         for j in range(4 * h + j0, 4 * h + j1):
@@ -538,33 +581,35 @@ def rank_program(g, core, T, topo):
         if late:
             ts(t("Ei"), ind(t("E", 0, 512), t("koff", 0, 4)), t("LB", 4 * r - 4, 4 * r - 3), Op.add)
             ts(t("Em"), t("Ei"), 4095, AND)
-            ts(t("Eb", c, c + 32), t("Em", 32, 64), -2048.0, Op.add)
-        else:
-            ts(t("Eb", c, c + 32), ind(t("E", 512 * h, 512 * h + 512), t("koff", 4 * h + 2, 4 * h + 4)), -2048.0, Op.add)
-        ts(field("ST", r, h, 0), t("Em", 0, 32) if late else t("EtU", c, c + 32), 0.0 if last else -2048.0, Op.add)
-        tt(t("Q", c, c + 32), t("Eb", c, c + 32), t("OO", 2 * c, 2 * c + 32), Op.mult)
-        if last:
+        row = t("Em", 32, 64) if late else ind(t("E", 512 * h, 512 * h + 512), t("koff", 4 * h + 2, 4 * h + 4))
+        tt(t("Q", c, c + 32), row, t("OO", 2 * c, 2 * c + 32), Op.mult)
+        if not last:
             mm(t("pV", 0, 32), t("oneh", p1=1), t("c2k", p1=1), True, False)
-        mm(t("pV", 0, 32), t("BD"), t("Q", c, c + 32), not last, True)
+        mm(t("pV", 0, 32), t("BD32"), t("Q", c, c + 32), last, True)
+        ts(field("ST", r, h, 0), t("Em", 0, 32) if late else t("EtU", c, c + 32), 0.0 if last else -2048.0, Op.add)
         act(field("ST", r, h, 1), t("OO", 2 * c + 32, 2 * c + 64), scale=-1.0, bias=1.0)
         tt(field("ST", r, h, 2), t("pV", 0, 32), t("OO", 2 * c + 32, 2 * c + 64), Op.mult)
         post(r, h, 0)
         if h:
-            lo, at = 320 * r + AT[1][1][0] + 32, 384 * r + AT[1][1][1] + 32
+            lo, at = WS * r + AT[1][1][0] + 32, WL * r + AT[1][1][1] + 32
             act(t("LA", at, at + 32), t("ST", lo, lo + 32))
         got[(r, h)] = fork(merge, r, h)
 
-    def best(h):
+    def best(h, n):
         c, m = 32 * h, 512 * h
         win = t("tab", 0, 4096 if h else TW)
         mm(t("pU", 0, 32), turn(0), t("dm"), True, False)
         mm(t("pU", 0, 32), turn(0), t("dm1"), False, False)
-        act(t("G", 0, 256), ind(win, t("EtU", c, c + 16)), scale=0.5)
-        ts(t("G", 256, 512), ind(win, t("EtU", c + 16, c + 32)), 0.5, Op.mult)
+        for lo in range(0, n, 16):
+            act(t("G", 16 * lo, 16 * min(lo + 16, n)), ind(win, t("EtU", c + lo, c + min(lo + 16, n))), scale=0.5)
+        if n < 32:
+            ts(t("G", 16 * n, 512), ind(win, t("EtU", c + n, c + 32)), 0.5, Op.mult)
         for lo in range(0, 512, 256):
             segmax(t("Ms", m + lo, m + lo + 256), t("G", lo, lo + 256))
         tt(t("Y16", c, c + 32), t("Ms", m + 15, m + 512, 16), t("zh", c, c + 32), Op.add)
-        mm(t("pU", 0, 32), t("WU"), t("Y16", c, c + 32), False, True)
+
+    def weigh(h):
+        mm(t("pU", 0, 32), t("WU"), t("Y16", 32 * h, 32 * h + 32), False, True)
 
     def places(h):
         c = 32 * h
@@ -577,7 +622,8 @@ def rank_program(g, core, T, topo):
 
     def turned(h, n):
         for k in range(n):
-            mm(t("pY", 32 * k, 32 * k + 32), turn(-k), t("Y16", 32 * h, 32 * h + 32))
+            j = (k + 4) % NT if h and n > 1 else k
+            mm(t("pD0" if h and k >= 4 else "pY", 32 * j, 32 * j + 32), turn(-k), t("Y16", 32 * h, 32 * h + 32))
 
     def anchors(r, h):
         c, m = 32 * h, 512 * h
@@ -587,21 +633,21 @@ def rank_program(g, core, T, topo):
         cp(t("si", c, c + 32), t("pV", 32, 64))
         act(field("ST", r, h, 3), t("pV", 64, 96), Act.Abs, scale=2.0)
         ts(t("ui", c, c + 32), t("si", c, c + 32), 4095, AND)
-        ts(t("u1", c, c + 32), t("ui", c, c + 32), -2048.0, Op.add)
-        ts(t("u2", c, c + 32), t("ui", c, c + 32), 3232.0, Op.add)
-        tt(t("Wc", c, c + 32), t("u1", c, c + 32), t("u2", c, c + 32), Op.mult)
+        tt(t("Wc", c, c + 32), t("ui", c, c + 32), t("ui", c, c + 32), Op.mult)
+        ts(t("u1", c, c + 32), t("ui", c, c + 32), 1184.0, Op.mult, t("kA") if h else CC, Op.add)
         ts(t("Wd", c, c + 32), t("Wc", c, c + 32), 0x1FFE0, AND)
-        ts(field("ST", r, h, 4), t("Wd", c, c + 32), t("kA") if h else CC, Op.add)
+        for f in range(4, 6 - h):
+            tt(field("ST", r, h, f), t("Wd", c, c + 32), t("u1", c, c + 32), Op.add)
         post(r, h, 1)
 
     def landed(r, h):
         c = 32 * h
-        for j in range(2):
+        for j in range(2 * h):
             act(t("C2", 2 * c + 32 * j, 2 * c + 32 * j + 32), field("LA", r, h, 4))
         s = fork(landed_z, r, h)
         slow.append(s)
         join(got[(r, h)])
-        names_end(h)
+        names_end(h, t("C2", 64, 128) if h else t("LA", WL * r + AT[0][2][1], WL * r + AT[0][2][1] + 64))
         join(s)
         if h:
             offsets(1, NT)
@@ -611,8 +657,10 @@ def rank_program(g, core, T, topo):
         c = 32 * h
         act(t("zr", c, c + 32), field("LA", r, h, 3))
         mm(t("pY", 256 + c, 288 + c), turn(8), t("zr", c, c + 32))
-        act(t("zh", c, c + 32), t("zr", c, c + 32), scale=0.5, bias=1023.75)
+        act(t("zh", c, c + 32), field("LA", r, h, 3), scale=0.5, bias=1023.75)
+        act(t("zq", c, c + 32), field("LA", r, h, 3), scale=0.5)
         act(t("zr", 128 + c, 128 + c + 32), t("pY", 256 + c, 288 + c))
+        act(t("zq", 128 + c, 128 + c + 32), t("pY", 256 + c, 288 + c), scale=0.5)
 
     def merge(r, h):
         c = 32 * h
@@ -624,16 +672,16 @@ def rank_program(g, core, T, topo):
             tt(t("L16", c, c + 32), t("tm", c, c + 32), field("LA", r, h, 2), Op.add)
             names(h)
             return
-        pr = 384 * r + AT[h][1][1]
+        pr = WL * r + AT[h][1][1]
         for q, s, n in RUNS[2 * h:2 * h + 2]:
             j = q - c
             tt(t("ylf", s, s + n), t("tm", q, q + n), t("LA", pr + 2 * j + 1, pr + 2 * (j + n), 2), Op.add)
 
     def out_rest(r, h):
-        c, lo = 32 * h, 384 * r + AT[h][2][1]
+        c, lo, st = 32 * h, WL * r + AT[h][2][1] + 64 - 64 * h, 1 + h
         ts(t("Wc", c, c + 32), field("LA", r, h, 4), 1 / 32, Op.mult, -32.0 if h else t("LB", 4 * r, 4 * r + 1), Op.add)
         for q, s, n in RUNS[2 * h:2 * h + 2]:
-            act(t("yzf", s, s + n), t("LA", lo + 2 * (q - c), lo + 2 * (q - c + n), 2))
+            act(t("yzf", s, s + n), t("LA", lo + st * (q - c), lo + st * (q - c + n), st))
         ts(t("Wd", c, c + 32), t("Wc", c, c + 32), 4095, AND)
         if h:
             dma("S", "d_o2", outside(T.yz[:, :]), t("yzf"))
@@ -642,7 +690,7 @@ def rank_program(g, core, T, topo):
         if h:
             dma("Y", "d_o2", outside(T.ya[:, :]), t("yaf", p0=0, p1=128, ps=16))
 
-    got, named, slow = {}, {}, []
+    got, named, items, slow = {}, {}, {}, []
 
     def tail0(r):
         last = r + 1 == RO
@@ -652,16 +700,23 @@ def rank_program(g, core, T, topo):
         mark(("chosen", r))
         pick(0, 0, 4)
         ts(t("EtU", 0, 32), ind(t("E", 0, 512), t("koff", 0, 2)), t("LB", 4 * r - 4, 4 * r - 3) if r else 0.0, Op.add)
-        s = fork(pairs, r, 0, r > 0)
-        best(0)
+        s = fork(pairs, r, 0, r > 0, at=PAIR_AT)
+        best(0, BEST_S[0])
         anchors(r, 0)
+        weigh(0)
         join(s)
         if not last:
             named[r] = fork(landed, r, 0)
             slow.append(named[r])
-        turned(0, 1 if last else NT)
         places(0)
+        mark(("placed", r))
+        items[r] = fork(first_items, r)
+        slow.append(items[r])
+
+    def first_items(r):
+        last = r + 1 == RO
         n = 1 if last else NT
+        turned(0, n)
         act(t("Yr", 256, 256 + 32 * n), t("pY", 0, 32 * n), bias=-1024.0)
         for b in range(2):
             woff(0, b, n)
@@ -671,13 +726,16 @@ def rank_program(g, core, T, topo):
                 dma("Y", "d_o1", outside(T.yx[:, lo:lo + 1024]), t("spare", lo, lo + 1024))
             return
         act(t("Yr", 512, 528), t("pY", 0, 256, 16), bias=-1024.0)
+        mark(("read", r))
         ts(t("w6"), t("si", 0, 1), 63, AND)
         ts(t("wo", 32, 33), t("w6"), t("pev"), Op.mult, t("padb"), Op.add)
 
-    def write_first():
-        for lo in range(18, 33, 4):
-            hi = min(lo + 4, 33)
-            cp(ind(t("tab", 4096), t("wo", lo, hi)), t("Yr", 16 * lo, 16 * hi))
+    def write_first(r):
+        join(items[r])
+        cp(ind(t("tab", 4096), t("wo", 32, 33)), t("Yr", 512, 528))
+        for k in range(1, NT, 2):
+            lo, hi = 16 + 2 * k, min(20 + 2 * k, 32)
+            cp(ind(t("tab", TW * k, TW * min(k + 2, NT)), t("wo", lo, hi)), t("Yr", 16 * lo, 16 * hi))
 
     def thresholds():
         cp(t("Ai"), t("pC", 64, 65))
@@ -688,12 +746,13 @@ def rank_program(g, core, T, topo):
     def tail1(r, first):
         last = r + 1 == RO
         compare(1, 3, 4, "S")
+        call(lambda: free.insert(0, True))
         join(first)
         if r == 0:
             for k in range(NT):
                 act(t("tab", TW * k + 4096, TW * k + TW), t("tab", TW * k, TW * k + 64))
         if not last:
-            w = fork(write_first)
+            w = fork(write_first, r)
         choose(1)
         for b in range(4):
             mm(t("pC", 64, 65), t("BD"), t("hot", b, b + 1), b == 0, b == 3)
@@ -707,50 +766,62 @@ def rank_program(g, core, T, topo):
         if not last:
             must.append(fork(thresholds))
         s = fork(pairs, r, 1, False, at=1)
-        best(1)
-        turned(1, 1 if last else NT)
+        best(1, 16 if last else BEST_S[1])
         if last:
             a = fork(anchors, r, 1, at=0)
+            join(items[r])
+            weigh(1)
+            turned(1, 1)
             places(1)
             act(t("Yr", 0, 32), t("pY", 0, 32), bias=-1024.0)
             for b in range(2):
                 woff(1, b, 1)
             cp(ind(t("tab", 0, 4096), t("wo", 0, 2)), t("Yr", 0, 32))
-            dma("Y", "d_o2", outside(T.yx[:, 1024:3072]), t("tab", 1024, 3072))
-            for x in (s, a, o, got[(r, 0)], got[(r, 1)]):
+            for x in (s, a):
                 join(x)
-            dma("Y", "d_o2", outside(T.yl[:, :]), t("ylf"))
+            call(lambda: ENG["Y"].wait_ge(T.sem.lo, total["lo"]))
+            dma("Y", "d_o2", outside(T.yx[:, 1024:3072]), t("tab", 1024, 3072))
+            for x in (o, got[(r, 0)], got[(r, 1)]):
+                join(x)
+            dma("S", "d_o2", outside(T.yl[:, :]), t("ylf"))
             out_rest(r, 1)
             return
+        weigh(1)
+        join(items[r])
+        until(("read", r))
+        turned(1, NT)
         a = fork(lambda: (anchors(r, 1), join(s), fork(landed, r, 1)), at=1)
+        o = fork(lambda: (join(named[r]), offsets(0, NT, t("LB", 4 * r, 4 * r + 1), range(4, 8))), at=1)
         places(1)
-        act(t("Yr", 0, 256), t("pY", 0, 256), bias=-1024.0)
         for b in range(2):
             woff(1, b, NT)
-        cp(ind(t("tab"), t("wo", 0, 18)), t("Yr", 0, 288))
+        for lo, bank in ((128, "pY"), (0, "pD0")):
+            act(t("Yr", lo, lo + 128), t(bank, lo, lo + 128), bias=-1024.0)
+        join(w)
+        cp(ind(t("tab", 0, 4 * TW), t("wo", 8, 18)), t("Yr", 128, 288))
         if r + 2 == RO:
             for lo in (0, 3072):
                 dma("Y", "d_sp", t("spare", lo, lo + 1024), t("tab", lo, lo + 1024))
-        if EARLY:
-            join(a)
-        join(w)
-        join(named[r])
-        offsets(0, NT, t("LB", 4 * r, 4 * r + 1))
+        join(o)
+        e = fork(early)
+        cp(ind(t("tab", 4 * TW, NT * TW), t("wo", 0, 8)), t("Yr", 0, 128))
+        offsets(0, NT, t("LB", 4 * r, 4 * r + 1), range(4))
+        join(e)
         call(lambda: begin(r + 1))
         open_half(0, NT)
 
     def begin(r):
         for h in range(2):
-            chunks.extend([((h, n, l), 2 * r + h if r else 1, NT if r else 4) for n in range(4) for l in range(16)
+            chunks.extend([((h, n, l), 2 * r + h + 1, NT if r else COPIES[4 * h + n]) for n in range(4) for l in range(16)
                            if r or h or n not in raw])
         keep = {}
 
         def end0():
             keep[0] = stream(tail0, r)
-            streams.append(keep[0])
-        after[(0, "pD0")] = lambda: streams.insert(0, stream(lambda: (compare(0, 0, 3, "V"), mark(("counted", r)))))
+            streams.insert(TAIL_AT, keep[0])
+        after[(0, "pD0")] = lambda: streams.insert(0, stream(lambda: (until("constants"), compare(0, 0, 3, "V"), mark(("counted", r)))))
         after[(0, "pD1")] = end0
-        after[(1, "pD0")] = lambda: streams.append(stream(lambda: (until(("chosen", r)), compare(1, 0, 3, "V"))))
+        after[(1, "pD0")] = lambda: streams.insert(0, stream(lambda: (until(("chosen", r)), compare(1, 0, 3, "V"))))
         after[(1, "pD1")] = lambda: streams.insert(0, stream(lambda: ([join(s) for s in list(streams) if not any(s is x for x in slow)],
                                                                       tail1(r, keep[0]))))
 
@@ -766,19 +837,22 @@ def rank_program(g, core, T, topo):
     for c in range(4):
         mm(t("pU", 32 * c, 32 * c + 32), t("sel", p1=8), t("anf", 32 * (c // 2), 32 * (c // 2) + 32, p1=8))
     mm(t("pU", 128, 129), t("sel", p1=8), t("anf", 64, 65, p1=8))
-    act(t("C2"), t("pU", 0, 128), scale=32.0, bias=CC)
+    act(t("C2"), t("pU", 0, 128), scale=32.0, bias=CC + 65536.0)
     act(t("nT"), t("pU", 128, 129), scale=-1.0, bias=1785.0 - 2048.0)
     for j in range(1, 4):
         mm(t("pZ", 64 * j, 64 * j + 64), turn(4 * j), t("zr", 0, 64))
     act(t("zn"), t("zr", 0, 32), scale=-1.0)
     act(t("zh"), t("zr", 0, 64), scale=0.5, bias=1023.75)
+    act(t("zq", 0, 64), t("zr", 0, 64), scale=0.5)
     act(t("zr", 64, 256), t("pZ", 64, 256))
+    act(t("zq", 64, 256), t("pZ", 64, 256), scale=0.5)
     spread("pY", t("zr", 0, 32), True)
     names_start(1)
-    names_end(0, 64)
+    names_end(0, t("C2", 0, 64), 64)
     cp(t("off", 0, 64), t("E", 0, 64))
-    cp(t("off", 64, 512), t("E", 64, 512))
-    raw = [2 * (c % 256 // 128) + c // 256 for lo, hi in RAW for c in range(lo, hi, 128)]
+    raw = [n for n in (0, 2, 1) if COPIES[n] == 1]
+    RAW = [(256 * (n % 2) + 128 * (n // 2), 256 * (n % 2) + 128 * (n // 2) + 128) for n in raw]
+    cp(t("off", 64, RAW[-1][1]), t("E", 64, RAW[-1][1]))
 
     def sums(src, w, lo, hi):
         def go():
@@ -795,16 +869,11 @@ def rank_program(g, core, T, topo):
                 until("first")
                 sums("rx", 16, todo[j - 1], todo[j - 1] + 64)
         sums("rx", 16, lo, lo + 64)
-        for k in TURN:
-            for j in range(8):
-                bank = ("pD1", "pV")[j % 2]
-                mm(t(bank), turn(-k), t("tab", 512 * j, 512 * j + 512))
-                act(t("tab", TW * k + 512 * j, TW * k + 512 * j + 512), t(bank))
-        mark("turned")
 
     def raw_sums():
         for lo, hi in RAW:
-            until(("raw", hi - 64))
+            for c in range(lo, hi, 64):
+                until(("raw", c))
             for i in range(16):
                 tt(t("rm", 16 * lo + i, 16 * hi, 16), t("rx", 16 * lo + i, 16 * hi, 16), t("pY", lo, hi), Op.max)
             sums("rm", 8, lo, hi)
@@ -812,23 +881,30 @@ def rank_program(g, core, T, topo):
     def first_sums():
         late_constants()
         mm(t("pD0", 0, 384), t("oneh"), t("thr"), True, False)
-        for n in range(4):
-            lo = 256 * (n % 2) + 128 * (n // 2)
-            if n in raw:
-                mm(t("pD0", 128 * n, 128 * n + 128), t("oneh"), t("zm", 128 * n, 128 * n + 128), False, False)
-            else:
-                for b in range(4):
-                    ts(t("off", lo + b, lo + 128, 4), t("E", lo + b, lo + 128, 4), float(TW * (3 - b)), Op.add)
+        for n in raw:
+            mm(t("pD0", 128 * n, 128 * n + 128), t("oneh"), t("zm", 128 * n, 128 * n + 128), False, False)
         left[(0, "pD0")] = 96
         mark("first")
+        first_offsets(0)
+        open_half(0, 4)
+        mark("open")
+
+    def first_offsets(h):
+        if h:
+            offsets(1, COPIES[7])
+        for n in range(4):
+            lo, k = 512 * h + 256 * (n % 2) + 128 * (n // 2), COPIES[4 * h + n]
+            for b in range(k if k != COPIES[7 * h] else 0):
+                ts(t("off", lo + b, lo + 128, k), t("E", lo + b, lo + 128, k), float(TW * (k - 1 - b)), Op.add)
 
     def second_names():
         names(1)
-        names_end(1)
-        offsets(1, 4)
-        until("turned")
-        open_half(1, 4)
+        names_end(1, t("C2", 64, 128))
+        first_offsets(1)
         tail_constants()
+        mark("constants")
+        until("open")
+        open_half(1, 4)
 
     begin(0)
     streams.extend([stream(raw_sums), stream(first_sums), stream(raw_gathers), stream(second_names)])

import math
from concourse.bass import DstId, RemoteDMATransfer
from concourse.mybir import AluOpType as Op, ActivationFunctionType as Act

RO = 4
NT = 8
TW = 4160
RUNS = ((0, 0, 16), (16, 48, 16), (32, 16, 32))
SLOT0 = (0, 48, 16, 32)
FIX, CYC, GAT, SCA, LAT, FAR, FAR_A = 0.05, 0.00083, 0.00125, 0.003, 0.2, 4.0, 3.0
OVER = 0.0
T_SMALL, T_X, T_TAB = 2.4, 4.6, 1.8
WAIT, SLACK = 0.03, 0.12
HALVES, BEST_S = 5, (16, 32)
STRETCH, LONG, PAIR_AT, TAIL_AT = 0.1, 3, 99, 99
LATER = (0.0, 0.0)
LEAVE, LAT_P, NEAR = 3, 0.2, 2
PEND_S, PEND_V, END = 2, 3, 0.3
COPIES = (1, 1, 1, 4, 4, 8, 8, 8)

SCRATCH = {
    "tab": ("sbuf", [128, NT * TW + 16], "bfloat16"), "spare": ("sbuf", [128, 4096], "bfloat16"),
    "sd": ("sbuf", [128, 64 * 128], "bfloat16"),
    "vd": ("sbuf", [128, 48 * 128], "bfloat16"),
    "vr": ("sbuf", [128, 48 * 128], "float16"), "zq": ("sbuf", [128, 256], "bfloat16"),
    "rx": ("sbuf", [128, 8192], "bfloat16"), "rm": ("sbuf", [128, 8192], "bfloat16"),
    "W": ("sbuf", [128, 1024], "int32"), "E": ("sbuf", [128, 1024], "int32"), "off": ("sbuf", [128, 1024], "uint16"),
    "L16": ("sbuf", [128, 64], "float16"), "B2": ("sbuf", [128, 128], "float32"), "C2": ("sbuf", [128, 128], "float32"),
    "zr": ("sbuf", [128, 256], "bfloat16"), "zh": ("sbuf", [128, 64], "float32"), "zn": ("sbuf", [128, 32], "bfloat16"),
    "zi": ("sbuf", [128, 64], "bfloat16"), "zm": ("sbuf", [128, 384], "bfloat16"),
    "thr": ("sbuf", [128, 384], "float16"), "nT": ("sbuf", [128, 1], "float32"), "ncol": ("sbuf", [128, 1], "float32"),
    "kA": ("sbuf", [128, 1], "float32"), "Ai": ("sbuf", [128, 1], "int32"), "Aj": ("sbuf", [128, 1], "int32"),
    "cmp": ("sbuf", [128, 1024], "bfloat16"), "Sc": ("sbuf", [128, 128], "float32"), "hot": ("sbuf", [128, 4], "bfloat16"),
    "KR": ("sbuf", [128, 8], "float32"), "koff": ("sbuf", [128, 8], "uint16"),
    "Ei": ("sbuf", [128, 64], "int32"), "Em": ("sbuf", [128, 64], "int32"),
    "EtU": ("sbuf", [128, 64], "uint16"), "OO": ("sbuf", [128, 128], "bfloat16"),
    "BD32": ("sbuf", [128, 128], "float32"), "Q": ("sbuf", [128, 64], "float32"),
    "G": ("sbuf", [128, 512], "bfloat16"), "Ms": ("sbuf", [128, 1024], "bfloat16"),
    "Y16": ("sbuf", [128, 64], "float16"), "Yr": ("sbuf", [128, 528], "bfloat16"),
    "si": ("sbuf", [128, 64], "int32"), "ui": ("sbuf", [128, 64], "int32"), "u1": ("sbuf", [128, 64], "float32"),
    "Wc": ("sbuf", [128, 64], "int32"), "Wd": ("sbuf", [128, 64], "int32"),
    "w6": ("sbuf", [128, 1], "int32"), "ws": ("sbuf", [128, 64], "float32"), "wr": ("sbuf", [128, 4], "float32"),
    "wo": ("sbuf", [128, 34], "uint16"),
    "tm": ("sbuf", [128, 64], "float32"),
    "ST": ("sbuf", [128, RO * 352], "float32"), "LA": ("sbuf", [128, RO * 416], "float32"),
    "SA": ("sbuf", [128, RO * 4], "float32"), "LB": ("sbuf", [128, RO * 4], "float32"),
    "J": ("sbuf", [128, 16], "int32"), "J2": ("sbuf", [128, 16], "int32"), "tg": ("sbuf", [128, 16], "float32"),
    "mh": ("sbuf", [128, 128], "bfloat16"), "ms": ("sbuf", [128, 128], "bfloat16"), "lm": ("sbuf", [128, 32], "bfloat16"),
    "pi": ("sbuf", [128, 1], "int32"), "pj": ("sbuf", [128, 1], "int32"), "pk": ("sbuf", [128, 1], "int32"),
    "pl": ("sbuf", [128, 1], "int32"), "pm": ("sbuf", [128, 1], "int32"),
    "pif": ("sbuf", [128, 1], "float32"), "pgf": ("sbuf", [128, 1], "float32"), "pff": ("sbuf", [128, 1], "float32"),
    "pbf": ("sbuf", [128, 1], "float32"), "pwf": ("sbuf", [128, 1], "float32"), "p8f": ("sbuf", [128, 1], "float32"),
    "p64": ("sbuf", [128, 1], "float32"), "podd": ("sbuf", [128, 1], "float32"), "pev": ("sbuf", [128, 1], "float32"),
    "pad1": ("sbuf", [128, 1], "float32"), "padb": ("sbuf", [128, 1], "float32"),
    "PH": ("sbuf", [128, 16 * 128], "float16"),
    "BD": ("sbuf", [128, 128], "float16"), "WU": ("sbuf", [128, 128], "float16"), "In": ("sbuf", [128, 128], "float16"),
    "o8": ("sbuf", [128, 56], "bfloat16"), "sel": ("sbuf", [128, 128], "float16"),
    "oneh": ("sbuf", [128, 128], "bfloat16"), "c16": ("sbuf", [128, 512], "bfloat16"), "c2k": ("sbuf", [128, 32], "bfloat16"),
    "gmi": ("sbuf", [128, 384], "bfloat16"), "gm": ("sbuf", [128, 384], "float16"),
    "kmi": ("sbuf", [128, 64], "int32"), "Km": ("sbuf", [128, 64], "float16"),
    "cfi": ("sbuf", [128, 32], "int32"), "coff": ("sbuf", [128, 32], "uint16"),
    "rmask": ("sbuf", [128, 256], "bfloat16"), "rmi": ("sbuf", [128, 256], "bfloat16"), "dm": ("sbuf", [128, 32], "bfloat16"), "dm1": ("sbuf", [128, 32], "bfloat16"),
    "eyi": ("sbuf", [128, 512], "bfloat16"), "eye": ("sbuf", [128, 512], "bfloat16"),
    "tci": ("sbuf", [128, 34], "float32"), "tc": ("sbuf", [128, 34], "float32"), "pad0": ("sbuf", [128, 1], "float32"),
    "lsi": ("sbuf", [128, 64], "int32"), "ani": ("sbuf", [128, 64], "int32"), "thi": ("sbuf", [128, 1], "int32"),
    "anf": ("sbuf", [128, 65], "float16"),
    "ylf": ("sbuf", [128, 64], "float32"), "yaf": ("sbuf", [128, 64], "float32"), "yzf": ("sbuf", [128, 64], "bfloat16"),
}
PS = ["pA", "pZ", "pD0", "pD1", "pC", "pV", "pU", "pY"]
for _n in PS:
    SCRATCH[_n] = ("psum", [128, 512], "float32")
DM = ["d_ls", "d_an", "d_z", "d_th", "d_x", "d_sp", "d_o1", "d_o2"] + ["d_t%d" % k for k in range(1, NT)]
SEMAPHORES = ["sV", "sS", "sP", "sG", "lo"] + DM + ["r%s%d" % (a, r) for a in "abcde" for r in range(RO)]
MSG = ((((0, 0, 64, 1), (32, 64, 64, 2)), ((96, 128, 96, 1),)),
       (((160, 224, 48, 2), (208, 272, 48, 3)), ((288, 352, 32, 2), (320, 384, 32, 3))))
WS, WL = 352, 416
AT = (((0, 0), (32, 64), (96, 128)), ((192, 256), (224, 288), (288, 352)))
MAGIC = 1.5 * 2 ** 29
CC = 1024.0 - 8388608.0


def rank_program(g, core, T, topo):
    rank = T.rank_of(core)
    if rank is None:
        return
    ENG = {"V": g.vector, "S": g.scalar, "P": g.tensor, "G": g, "Y": g.sync}
    known = {q: {} for q in ENG}
    clock, total, acc, plan = {}, {}, {}, {}
    clk = {q: 0.0 for q in ENG}

    def t(name, lo=0, hi=None, st=1, p0=0, p1=128, ps=1):
        if hi is None:
            hi = SCRATCH[name][1][1]
        if p0 == 0 and p1 == 128 and ps == 1:
            ap = T[name][:, lo:hi] if st == 1 else T[name][:, lo:hi:st]
        else:
            ap = T[name][p0:p1, lo:hi] if ps == 1 else T[name][p0:p1:ps, lo:hi]
        regs = [(name, lo, hi, st)]
        return (ap, regs, (hi - lo + st - 1) // st, SCRATCH[name][2].endswith("16"), "")

    def ind(win, off):
        return (win[0].indirect(off[0]), win[1] + off[1], 16 * off[2], win[3], "ind")

    def outside(ap):
        return (ap, [], 0, False, "")

    def need(q, regs, isw):
        own = "s" + q
        out = {}
        for name, lo, hi, st in regs:
            ps = name in PS
            for a, b, sem, val, w, s2 in acc.get(name, []):
                over = a < hi and lo < b and (lo - a) % math.gcd(st, s2) == 0
                if over and min(hi - lo, b - a) < max(st, s2):
                    over = bool(set(range(lo, hi, st)) & set(range(a, b, s2)))
                if sem == own:
                    hit = over and w and (not isw or q != "P")
                elif ps:
                    hit = True
                else:
                    hit = over and (w or isw)
                if hit and known[q].get(sem, 0) < val:
                    out[sem] = max(out.get(sem, 0), val)
        return out

    def note(regs, sem, val, isw):
        for name, lo, hi, st in regs:
            lst = [e for e in acc.get(name, []) if not (e[0] >= lo and e[1] <= hi and e[2] == sem and e[4] == isw
                                                        and e[5] % st == 0 and (e[0] - lo) % st == 0)]
            lst.append((lo, hi, sem, val, isw, st))
            acc[name] = lst

    def waits(q, reads, writes):
        w = {}
        for regs, isw in ((reads, False), (writes, True)):
            for s, v in need(q, regs, isw).items():
                w[s] = max(w.get(s, 0), v)
        return w

    def prepare(q, reads, writes):
        w = waits(q, reads, writes)
        clk[q] = max([clk[q]] + [plan[e] for e in w.items()])
        for s in sorted(w):
            if any(o != s and clock.get((o, w[o]), {}).get(s, 0) >= w[s] and known[q].get(o, 0) < w[o] for o in w):
                continue
            if known[q].get(s, 0) >= w[s]:
                continue
            ENG[q].wait_ge(T.sem[s], w[s])
            k = known[q]
            for a, b in clock.get((s, w[s]), {}).items():
                k[a] = max(k.get(a, 0), b)
            k[s] = max(k.get(s, 0), w[s])

    def finish(q, ins, sem, n, reads, writes, when):
        total[sem] = total.get(sem, 0) + n
        ins.then_inc(T.sem[sem], n)
        clock[(sem, total[sem])] = dict(known[q])
        plan[(sem, total[sem])] = when
        note(reads, sem, total[sem], False)
        note(writes, sem, total[sem], True)

    rec = [None]

    def put(step):
        if rec[0] is None:
            step[4]()
        else:
            rec[0].append(step)

    def stream(fn, *a):
        keep, rec[0] = rec[0], []
        fn(*a)
        s, rec[0] = rec[0], keep
        return s

    def op(q, fn, out, ins, *rest, **kw):
        aps = [a for a in ins if isinstance(a, tuple)]
        reads = [r for a in aps for r in a[1]]
        for k in ("bias", "scale"):
            if isinstance(kw.get(k), tuple):
                reads = reads + kw[k][1]
                kw[k] = kw[k][0]
        wr = out[1]
        if out[4]:
            reads, wr, c = reads + wr[1:], wr[:1], FIX + SCA * out[2]
        elif q == "P":
            c = CYC * max(64, out[2]) * (1 if aps[0][3] else 4)
        elif aps and aps[0][4]:
            c = (FIX if q == "V" else 0.065) + GAT * out[2]
        elif q == "G":
            c = 0.13 + 2 * CYC * out[2]
        else:
            c = OVER + CYC * max(64, out[2] * (0.5 if q == "V" and all(a[3] or a[2] == 1 for a in aps + [out]) else 1))

        def go():
            prepare(q, reads, wr)
            i = fn(out[0], *([a[0] if isinstance(a, tuple) else a for a in ins] + list(rest)), **kw)
            clk[q] += c
            finish(q, i, "s" + q, 1, reads, wr, clk[q] + (LAT_P if q == "P" else LAT))
        put((q, reads, wr, c, go))

    def call(fn):
        put(("", [], [], 0, fn))

    def tt(out, a, b, o):
        op("V", g.vector.tensor_tensor, out, [a, b, o])

    def ts(out, a, s1, o1, s2=None, o2=None):
        if o2 is None:
            op("V", g.vector.tensor_scalar, out, [a, s1, None, o1])
        else:
            op("V", g.vector.tensor_scalar, out, [a, s1, s2, o1, o2])

    def cp(out, a):
        op("V", g.vector.tensor_copy, out, [a])

    def segmax(out, a):
        op("V", g.vector.tensor_tensor_scan, out, [t("rmask", 0, out[2]), a, 0.0, Op.min, Op.max])

    def act(out, a, f=Act.Copy, **kw):
        op("S", g.scalar.activation, out, [a, f], **kw)

    def mm(out, l, r, start=True, stop=True):
        op("P", g.tensor.matmul, out, [l, r, start, stop])

    def dma(q, sem, out, a, when=2.0, fresh=False):
        def go():
            prepare(q, a[1], [] if fresh else out[1])
            i = ENG[q].dma_start(out[0], a[0])
            finish(q, i, sem, 16, a[1], out[1], clk[q] + when)
        put((q if q == "S" else "Y", a[1], [] if fresh else out[1], 0.05, go))

    def send(src, land, c0, l0, msg, sem, far):
        def go():
            prepare("G", [(src, c0 + lo, c0 + lo + w, 1) for lo, at, w, d in msg], [])
            tr = []
            for j, (lo, at, w, d) in enumerate(msg):
                dst = T.cores[(rank + d) % 4]
                rid, pid, _ = topo.addr(dst)
                e = topo.engines(core, dst)
                n = len(e) // len(msg)
                m = 0
                for x in e[n * j:n * j + n]:
                    m |= 1 << x
                tr.append(RemoteDMATransfer(dst_ids=[DstId(rid=rid, pnc=pid)], dma_engine_mask=m, remote_sem=T.sem[sem],
                                            src=T[src][:, c0 + lo:c0 + lo + w], dst=T[land][:, l0 + at:l0 + at + w]))
                total["lo"] = total.get("lo", 0) + n
                total[sem] = total.get(sem, 0) + n
            g.remote_dma_fused(tr, local_sem=T.sem.lo)
            plan[(sem, total[sem])] = clk["G"] + far
            clk["G"] += 0.6
            note([(land, l0 + at, l0 + at + w, 1) for lo, at, w, d in msg], sem, total[sem], True)
        put(("G", [], [], 0, go))

    dma("Y", "d_ls", t("lsi"), outside(T.ls[:, :]), T_SMALL)
    dma("S", "d_an", t("ani", p1=8), outside(T.an[:, :]), T_SMALL)
    dma("S", "d_th", t("thi", p1=8), outside(T.th[:, 0:1]), T_SMALL)
    dma("Y", "d_z", t("zi"), outside(T.z[:, :]), T_SMALL)
    dma("Y", "d_x", t("tab", 0, 4096), outside(T.x[:, :]), T_X)
    for k in range(1, NT):
        lo, hi, when = TW * k, TW * k + 4096, T_X + T_TAB * k
        for f in range(16):
            dma("Y", "d_t%d" % k, t("tab", lo, hi, p0=f, p1=128, ps=16), outside(T.x[(f - k) % 16::16, :]), when, True)

    def iota(out, pattern, base, cm, **kw):
        op("G", g.iota, out, [], pattern, base, cm, **kw)

    SM = {"allow_small_or_imprecise_dtypes": True}
    iota(t("pi"), [[0, 1]], 0, 1)
    iota(t("J"), [[-1, 16]], 16, 1)
    iota(t("mh"), [[1, 128]], 0, 0, **SM)
    iota(t("ms"), [[1, 8], [0, 16]], 0, 0, **SM)
    iota(t("lm"), [[0, 2], [1, 16]], 0, 0, **SM)
    iota(t("rmi"), [[0, 16], [32767, 16]], -16384, 0, **SM)
    for h in range(2):
        step, base = 64 * (SLOT0[2 * h + 1] - SLOT0[2 * h]), 64 * SLOT0[2 * h]
        if h:
            iota(t("tci", 0, 16), [[0, 2], [TW, NT // 2], [step, 2]], base, 0, **SM)
        else:
            iota(t("tci", 16, 18), [[step, 2]], base, 0, **SM)
            iota(t("tci", 18, 34), [[0, NT // 2], [TW, 2], [step, 2]], base, 0, **SM)
    iota(t("gmi"), [[0, 3], [16, 8], [0, 16]], 0, 0, **SM)
    iota(t("cfi"), [[16, 2], [0, 16]], 0, 0)
    for k in range(NT):
        w = 64 + 16 * (k == NT - 1)
        iota(t("tab", TW * k + 4096, TW * k + 4096 + w), [[0, w]], 0, 0, **SM)
    iota(t("c2k"), [[0, 32]], -2048, 0, **SM)
    for s in range(2):
        iota(t("kmi", 32 * s, 32 * s + 32), [[128, 2], [256, 2], [1, 8]], 0, 0)
    iota(t("eyi"), [[-8, 2], [0, 32], [-1, 8]], 15, 0, **SM)
    SH, AND = Op.arith_shift_right, Op.bitwise_and
    op("V", g.vector.memset, t("oneh"), [], 1.0)
    op("V", g.vector.memset, t("c16", p1=32), [], 2016.0)
    ts(t("pl"), t("pi"), 112, AND)
    ts(t("pj"), t("pi"), 15, AND)
    ts(t("pk"), t("pi"), 4, SH)
    ts(t("pm"), t("pi"), 1, AND)
    ts(t("J2"), t("J"), 15, AND)
    cp(t("pbf"), t("pl"))
    cp(t("pif"), t("pi"))
    cp(t("pff"), t("pj"))
    cp(t("pgf"), t("pk"))
    cp(t("podd"), t("pm"))
    ts(t("tg"), t("J2"), t("pbf"), Op.add)
    ts(t("o8", 0, 8), t("mh", 0, 8), t("pgf"), Op.is_equal)
    for k in range(16):
        ts(t("PH", 128 * k, 128 * k + 128), t("mh"), t("tg", k, k + 1), Op.is_equal)
    ts(t("sel", p1=8), t("ms", p1=8), t("pif", p1=8), Op.is_equal)
    for c, w in enumerate((2.0, -1.0, -512.0, 512.0, -1024.0, 1024.0)):
        act(t("o8", 8 * c + 8, 8 * c + 16), t("o8", 0, 8), scale=w)
    act(t("p8f"), t("pff"), scale=8.0, bias=-255.5)
    act(t("p64"), t("pff"), scale=64.0, bias=31.5)
    act(t("pwf"), t("pff"), scale=2.0, bias=1.0)
    act(t("pad0"), t("pff"), scale=-TW / 2 + 0.5, bias=NT * TW - 4096 - 0.5)
    act(t("pev"), t("podd"), scale=-1.0, bias=1.0)
    act(t("dm1"), t("lm"), scale=0.0, bias=-31.5)
    act(t("pad1"), t("pad0"), Act.Identity, scale=t("podd"))
    act(t("rmask"), t("rmi"), scale=32.0)
    act(t("padb"), t("pff"), Act.Identity, scale=TW / 2, bias=t("pad1"))
    act(t("tc"), t("tci"), Act.Identity, bias=t("p64"))

    def turn(k):
        return t("PH", 128 * (k % 16), 128 * (k % 16) + 128)

    def late_constants():
        ts(t("gm"), t("gmi"), t("pbf"), Op.is_equal)
        ts(t("coff"), t("cfi"), t("pff"), Op.add)
        ts(t("thr"), t("gm"), t("nT"), Op.mult, 0.0625, Op.mult)
        tt(t("zm"), ind(t("zn"), t("coff", 0, 24)), t("gm"), Op.mult)

    def tail_constants():
        ts(t("In"), t("mh"), t("pif"), Op.is_equal, -0.5, Op.mult)
        ts(t("BD"), t("ms"), t("pgf"), Op.is_equal)
        ts(t("BD32"), t("ms"), t("pgf"), Op.is_equal)
        ts(t("Km"), t("kmi"), t("p8f"), Op.add)
        ts(t("WU"), t("ms"), t("pgf"), Op.is_equal, t("pwf"), Op.mult)
        ts(t("dm"), t("lm"), t("pff"), Op.not_equal, -524288.0, Op.mult)
        ts(t("eye"), t("eyi"), t("pff"), Op.is_equal)

    def spread(bank, src, first):
        for k in range(16):
            a, b = (15 - k) // 8, (15 - k) % 8
            mm(t(bank, 256 * a + b, 256 * a + 256, 8), turn(k), src, first, first or k == 15)

    def names_start(h):
        mm(t(("pA", "pZ")[h]), t("oneh", p1=1), t("c16", p1=1), True, False)

    def names(h):
        pa = ("pA", "pZ")[h]
        spread(pa, t("L16", 32 * h, 32 * h + 32), False)
        double_b(h)
        for b in range(8):
            tt(t(pa, b, 512, 8), t(pa, b, 512, 8), t("B2", 64 * h, 64 * h + 64), Op.mult)

    def names_end(h, c2, cut=0):
        pa, c = ("pA", "pZ")[h], 512 * h
        for b in range(8):
            tt(t("W", c + b, c + 512, 8), t(pa, b, 512, 8), c2, Op.add)
        for lo, hi in ((0, cut), (cut, 512)):
            if hi > lo:
                ts(t("E", c + lo, c + hi), t("W", c + lo, c + hi), 5, SH, 4095, AND)

    def offsets(h, n, A=None, bs=None):
        for b in bs or range(n):
            o, e = t("off", 512 * h + b, 512 * h + 512, n), t("E", 512 * h + b, 512 * h + 512, n)
            if A is None:
                ts(o, e, float(TW * (n - 1 - b)), Op.add)
            else:
                ts(o, e, A, Op.add, float(TW * (n - 1 - b)), Op.add)

    def double_b(h):
        for c in range(2):
            ts(t("B2", 64 * h + 32 * c, 64 * h + 32 * c + 32), t("L16", 32 * h, 32 * h + 32), 2080.0, Op.add)

    streams, chunks, gate, marks, must, free = [], [], [0], [], [], [False]
    seen = {"pD0": True, "pD1": False}
    ring, pend, left, after, begun = {"S": 0, "V": 0}, {"S": [], "V": []}, {}, {}, {}

    def place(h, n):
        return ("pD0", 128 * n) if n < 3 else ("pD1", 0)

    def dist(c, src, lo, w):
        h, n, l = c
        bank, col = place(h, n)
        key = (h, bank)
        if left.get(key, 0) == 0:
            for s in must:
                while s:
                    s.pop(0)[4]()
            n_col = 128 if n == 3 else 384
            assert not seen[bank]
            left[key] = n_col // 4
            seen[bank] = True
            mm(t(bank, 0, n_col), t("oneh"), t("thr", 0, n_col), True, False)
        left[key] -= w[1]
        mm(t(bank, col + l, col + l + 113, 16), t(src, lo, lo + 128), t("o8", w[0], w[0] + 8), False, left[key] == 0)
        if left[key] == 0:
            after[key]()

    def flush(e, keep=0):
        now = pend[e][:len(pend[e]) - keep]
        del pend[e][:len(now)]
        if e == "V":
            for c, lo, n_t in now:
                dist(c, "vd", lo, (16, 1))
            for c, lo, n_t in now:
                for s in range(8 // n_t):
                    a, zc = lo + 16 * n_t * s, z_at(c, n_t, s)
                    ts(t("vr", a, a + 16 * n_t), t("vd", a, a + 16 * n_t), t("zr", zc, zc + 1), Op.max, t("zq", zc, zc + 1), Op.subtract)
        for c, lo, n_t in now if e == "V" else reversed(now):
            dist(c, "vr" if e == "V" else "sd", lo, (8, 1) if e == "V" else (0, 2))

    def z_at(c, n_t, s):
        h, n, l = c
        return 64 * ((15 - 8 * (n % 2) - n_t * s) // n_t * n_t // 4) + 32 * h + 16 * (n // 2) + l

    def gather(e, c, n_t, m):
        h, n, l = c
        o = 512 * h + 256 * (n % 2) + 128 * (n // 2) + 8 * l
        bank, col = place(h, n)
        if e == "V" and ring[e] + m > 48:
            flush(e)
            ring[e] = 0
        if c in begun:
            lo = begun.pop(c)
            act(t("sd", lo, lo + 64), ind(t("tab", 0, NT * TW), t("off", o, o + 4)), Act.Abs, bias=t("zr", 128 + l, 129 + l), scale=-1.0)
        else:
            ring[e] %= 64
            lo = 128 * ring[e]
            ring[e] += m
            if e == "V":
                cp(t("vd", lo, lo + 128 * m), ind(t("tab", 0, n_t * TW), t("off", o, o + 8 * m)))
            for s in range(8 // n_t if e == "S" else 0):
                zc, w = z_at(c, n_t, s), 16 * n_t
                act(t("sd", lo + w * s, lo + w * s + w), ind(t("tab", 0, n_t * TW), t("off", o + n_t * s, o + n_t * s + n_t)), Act.Abs,
                    bias=t("zr", zc, zc + 1), scale=-1.0)
        pend[e].extend([((h, n, l + j), lo + 128 * j, n_t) for j in range(m)])
        rest = len([1 for x in chunks if place(*x[0][:2])[0] == bank and x[0][0] == h])
        if rest and seen[bank] and left.get((h, bank), 0) == 0:
            return
        if rest == 0:
            flush("V")
            flush("S")
        elif e == "S" and len(pend[e]) >= PEND_S:
            flush(e)

    def early():
        for l in range(HALVES):
            ring["S"] %= 64
            lo = begun[(0, 0, l)] = 128 * ring["S"]
            ring["S"] += 1
            act(t("sd", lo + 64, lo + 128), ind(t("tab", 0, 4 * TW), t("off", 8 * l + 4, 8 * l + 8)), Act.Abs,
                bias=t("zr", 128 + l, 129 + l), scale=-1.0)

    def ready(step):
        return max([0.0] + [plan[e] for e in waits(step[0], step[1], step[2]).items()])

    def run():
        while chunks or any(streams):
            streams[:] = [s for s in streams if s]
            if len(chunks) > NEAR:
                free[0] = False
            near = len(chunks) <= NEAR and not free[0]
            s = next((s for s in streams if s[0][0] not in ("S", "V") and (s[0][0] != "W" or s[0][4] in marks)
                      and not (near and s[0][0] == "P" and any(s is x for x in slow))), None)
            if s is not None:
                step = s.pop(0)
                if step[0] == "W":
                    pass
                elif step[0] != "J":
                    step[4]()
                elif step[4] is not s:
                    s[:0] = step[4]
                    step[4].clear()
                continue
            open_ = [c for c in chunks if c[1] <= gate[0]]
            can = []
            for j, s in enumerate(streams):
                if s[0][0] in "WP":
                    continue
                e, at = s[0][0], max(ready(s[0]), clk[s[0][0]])
                if j and streams[0][0][0] == e and at + s[0][3] > ready(streams[0][0]) + SLACK:
                    continue
                can.append((max(at - WAIT, clk[e]), j, s))
            if open_:
                per = 0.065 * NT / open_[0][2] + 128 * GAT
                for e in "SV":
                    at = max(there(e, open_[0]), clk[e])
                    if e == "S" or at + per + END < clk["S"] + per * len(chunks):
                        can.append((at, 99, e))
            at, j, s = min(can, key=lambda c: c[:2])
            if j == 99:
                take(s, open_)
            else:
                s.pop(0)[4]()

    def there(e, c):
        return ready((e, t("tab", 0, c[2] * TW)[1] + t("off", 512 * c[0][0], 512 * c[0][0] + 512)[1], []))

    def take(e, open_):
        c, m = open_[0], 1
        if e == "V":
            open_ = [x for x in open_ if x[0] not in begun]
            c = open_[0]
            key = (c[0][0], place(*c[0][:2])[0])
            later = [x for x in open_ if (x[0][0], place(*x[0][:2])[0]) != key]
            close = len(open_) - len(later) <= LEAVE
            fresh = len([1 for x in pend[e] if ready((e, t("vd", x[1], x[1] + 128)[1], [])) > clk[e] + WAIT])
            shut = [1 for x in pend[e] if seen[place(*x[0][:2])[0]] and left.get((x[0][0], place(*x[0][:2])[0]), 0) == 0]
            if len(pend[e]) - fresh >= (1 if close else PEND_V) and not shut:
                flush(e, max(fresh, len(pend[e]) - 4))
                return
            if close and later and not seen[place(*later[0][0][:2])[0]]:
                c, close = later[0], False
            due = min([9.0] + [ready(s[0]) - clk[e] if s[0][0] == e else 0.3 for s in streams if s[0][0] != "W"])
            room = len([1 for x in open_ if x[0][:2] == c[0][:2]]) if not close else 1
            m = max(1, min(int((due + STRETCH) / (128 * GAT)), LONG, room, (len(chunks) - 4) // 3))
        j = chunks.index(c)
        del chunks[j:j + m]
        gather(e, c[0], c[2], m)

    def open_half(h, n_t):
        def go():
            gate[0] += 1
        call(go)

    def fork(fn, *a, at=99):
        s = stream(fn, *a)
        call(lambda: streams.insert(at, s))
        return s

    def join(s):
        put(("J", [], [], 0, s))

    def mark(key):
        call(lambda: marks.append(key))

    def until(key):
        put(("W", [], [], 0, key))

    def compare(h, n0, n1, e):
        bank, col = place(h, n0)
        o, d = t("cmp", 512 * h + 128 * n0, 512 * h + 128 * n1), t(bank, col, col + 128 * (n1 - n0))
        if e == "S":
            act(o, d, Act.Sign, bias=-1784.5)
        else:
            ts(o, d, 1785.0, Op.is_ge, 0.5, Op.subtract)
        call(lambda: seen.update({bank: False}))
        if n0 == 0:
            mm(t("pC", 0, 64), turn(0), t("Km"), True, False)
        w = 24 if e == "S" else 40
        for n in range(n0, n1):
            for s in range(2):
                c = 32 * s + 8 * n
                mm(t("pC", c, c + 8), t("cmp", 512 * h + 128 * n, 512 * h + 128 * n + 128), t("o8", w + 8 * s, w + 8 * s + 8),
                   False, n == 3 and s == 1)

    def field(name, r, h, f):
        lo = (WS * r if name == "ST" else WL * r) + AT[h][min(f + 1, 4) // 2][name == "LA"]
        if h == 0 and f >= 3:
            lo += 32 * ((f - 4) % 3)
            return t(name, lo, lo + 32)
        return t(name, lo, lo + 32) if f == 0 else t(name, lo + 1 - f % 2, lo + 64, 2)

    def post(r, h, j):
        send("ST", "LA", WS * r, WL * r, MSG[h][j], "r%s%d" % ("abde"[2 * h + j], r), FAR + (LATER[j] if h and r + 1 < RO else 0))

    def choose(h):
        c = 4 * h
        segmax(t("Sc", 64 * h, 64 * h + 64), t("pC", 0, 64))
        ts(t("KR", c, c + 4), t("Sc", 64 * h + 15, 64 * h + 64, 16), 16 * MAGIC, Op.add, 16 * MAGIC, Op.subtract)
        ts(t("hot", 2 * h, 2 * h + 2), t("Sc", 64 * h + 15, 64 * h + 32, 16), 512.0, Op.is_ge)

    def pick(h, j0, j1):
        for j in range(4 * h + j0, 4 * h + j1):
            ts(t("koff", j, j + 1), t("Sc", 16 * j + 15, 16 * j + 16), t("KR", j, j + 1), Op.subtract, 255.5, Op.add)

    def pairs(r, h, late):
        c, last = 32 * h, r + 1 == RO
        act(t("OO", 2 * c, 2 * c + 64), ind(t("eye"), t("koff", 4 * h, 4 * h + 4)))
        if late:
            ts(t("Ei"), ind(t("E", 0, 512), t("koff", 0, 4)), t("LB", 4 * r - 4, 4 * r - 3), Op.add)
            ts(t("Em"), t("Ei"), 4095, AND)
        row = t("Em", 32, 64) if late else ind(t("E", 512 * h, 512 * h + 512), t("koff", 4 * h + 2, 4 * h + 4))
        tt(t("Q", c, c + 32), row, t("OO", 2 * c, 2 * c + 32), Op.mult)
        if not last:
            mm(t("pV", 0, 32), t("oneh", p1=1), t("c2k", p1=1), True, False)
        mm(t("pV", 0, 32), t("BD32"), t("Q", c, c + 32), last, True)
        ts(field("ST", r, h, 0), t("Em", 0, 32) if late else t("EtU", c, c + 32), 0.0 if last else -2048.0, Op.add)
        act(field("ST", r, h, 1), t("OO", 2 * c + 32, 2 * c + 64), scale=-1.0, bias=1.0)
        tt(field("ST", r, h, 2), t("pV", 0, 32), t("OO", 2 * c + 32, 2 * c + 64), Op.mult)
        post(r, h, 0)
        if h:
            lo, at = WS * r + AT[1][1][0] + 32, WL * r + AT[1][1][1] + 32
            act(t("LA", at, at + 32), t("ST", lo, lo + 32))
        got[(r, h)] = fork(merge, r, h)

    def best(h, n):
        c, m = 32 * h, 512 * h
        win = t("tab", 0, 4096 if h else TW)
        mm(t("pU", 0, 32), turn(0), t("dm"), True, False)
        mm(t("pU", 0, 32), turn(0), t("dm1"), False, False)
        for lo in range(0, n, 16):
            act(t("G", 16 * lo, 16 * min(lo + 16, n)), ind(win, t("EtU", c + lo, c + min(lo + 16, n))), scale=0.5)
        if n < 32:
            ts(t("G", 16 * n, 512), ind(win, t("EtU", c + n, c + 32)), 0.5, Op.mult)
        for lo in range(0, 512, 256):
            segmax(t("Ms", m + lo, m + lo + 256), t("G", lo, lo + 256))
        tt(t("Y16", c, c + 32), t("Ms", m + 15, m + 512, 16), t("zh", c, c + 32), Op.add)

    def weigh(h):
        mm(t("pU", 0, 32), t("WU"), t("Y16", 32 * h, 32 * h + 32), False, True)

    def places(h):
        c = 32 * h
        segmax(t("ws", c, c + 32), t("pU", 0, 32))
        ts(t("wr", 2 * h, 2 * h + 2), t("ws", c + 15, c + 32, 16), MAGIC, Op.add, MAGIC, Op.subtract)

    def woff(h, b, n):
        c, lo = 32 * h + 16 * b + 15, 16 - 16 * h
        ts(t("wo", lo + b, lo + 2 * n, 2), t("tc", lo + b, lo + 2 * n, 2), t("ws", c, c + 1), Op.add, t("wr", 2 * h + b, 2 * h + b + 1), Op.subtract)

    def turned(h, n):
        for k in range(n):
            j = (k + 4) % NT if h and n > 1 else k
            mm(t("pD0" if h and k >= 4 else "pY", 32 * j, 32 * j + 32), turn(-k), t("Y16", 32 * h, 32 * h + 32))

    def anchors(r, h):
        c, m = 32 * h, 512 * h
        mm(t("pV", 32, 64), t("WU"), t("Y16", c, c + 32))
        mm(t("pV", 64, 96), turn(0), t("Ms", m + 15, m + 512, 16), True, False)
        mm(t("pV", 64, 96), t("In"), t("zr", c, c + 32), False, True)
        cp(t("si", c, c + 32), t("pV", 32, 64))
        act(field("ST", r, h, 3), t("pV", 64, 96), Act.Abs, scale=2.0)
        ts(t("ui", c, c + 32), t("si", c, c + 32), 4095, AND)
        tt(t("Wc", c, c + 32), t("ui", c, c + 32), t("ui", c, c + 32), Op.mult)
        ts(t("u1", c, c + 32), t("ui", c, c + 32), 1184.0, Op.mult, t("kA") if h else CC, Op.add)
        ts(t("Wd", c, c + 32), t("Wc", c, c + 32), 0x1FFE0, AND)
        for f in range(4, 6 - h):
            tt(field("ST", r, h, f), t("Wd", c, c + 32), t("u1", c, c + 32), Op.add)
        post(r, h, 1)

    def landed(r, h):
        c = 32 * h
        for j in range(2 * h):
            act(t("C2", 2 * c + 32 * j, 2 * c + 32 * j + 32), field("LA", r, h, 4))
        s = fork(landed_z, r, h)
        slow.append(s)
        join(got[(r, h)])
        names_end(h, t("C2", 64, 128) if h else t("LA", WL * r + AT[0][2][1], WL * r + AT[0][2][1] + 64))
        join(s)
        if h:
            offsets(1, NT)
            open_half(1, NT)

    def landed_z(r, h):
        c = 32 * h
        act(t("zr", c, c + 32), field("LA", r, h, 3))
        mm(t("pY", 256 + c, 288 + c), turn(8), t("zr", c, c + 32))
        act(t("zh", c, c + 32), field("LA", r, h, 3), scale=0.5, bias=1023.75)
        act(t("zq", c, c + 32), field("LA", r, h, 3), scale=0.5)
        act(t("zr", 128 + c, 128 + c + 32), t("pY", 256 + c, 288 + c))
        act(t("zq", 128 + c, 128 + c + 32), t("pY", 256 + c, 288 + c), scale=0.5)

    def merge(r, h):
        c = 32 * h
        slow.append(rec[0])
        if r + 1 < RO:
            names_start(h)
        tt(t("tm", c, c + 32), field("LA", r, h, 0), field("LA", r, h, 1), Op.mult)
        if r + 1 < RO:
            tt(t("L16", c, c + 32), t("tm", c, c + 32), field("LA", r, h, 2), Op.add)
            names(h)
            return
        pr = WL * r + AT[h][1][1]
        for q, s, n in RUNS[2 * h:2 * h + 2]:
            j = q - c
            tt(t("ylf", s, s + n), t("tm", q, q + n), t("LA", pr + 2 * j + 1, pr + 2 * (j + n), 2), Op.add)

    def out_rest(r, h):
        c, lo, st = 32 * h, WL * r + AT[h][2][1] + 64 - 64 * h, 1 + h
        ts(t("Wc", c, c + 32), field("LA", r, h, 4), 1 / 32, Op.mult, -32.0 if h else t("LB", 4 * r, 4 * r + 1), Op.add)
        for q, s, n in RUNS[2 * h:2 * h + 2]:
            act(t("yzf", s, s + n), t("LA", lo + st * (q - c), lo + st * (q - c + n), st))
        ts(t("Wd", c, c + 32), t("Wc", c, c + 32), 4095, AND)
        if h:
            dma("S", "d_o2", outside(T.yz[:, :]), t("yzf"))
        for q, s, n in RUNS[2 * h:2 * h + 2]:
            cp(t("yaf", s, s + n), t("Wd", q, q + n))
        if h:
            dma("Y", "d_o2", outside(T.ya[:, :]), t("yaf", p0=0, p1=128, ps=16))

    got, named, items, slow = {}, {}, {}, []

    def tail0(r):
        last = r + 1 == RO
        until(("counted", r))
        compare(0, 3, 4, "V")
        choose(0)
        mark(("chosen", r))
        pick(0, 0, 4)
        ts(t("EtU", 0, 32), ind(t("E", 0, 512), t("koff", 0, 2)), t("LB", 4 * r - 4, 4 * r - 3) if r else 0.0, Op.add)
        s = fork(pairs, r, 0, r > 0, at=PAIR_AT)
        best(0, BEST_S[0])
        anchors(r, 0)
        weigh(0)
        join(s)
        if not last:
            named[r] = fork(landed, r, 0)
            slow.append(named[r])
        places(0)
        mark(("placed", r))
        items[r] = fork(first_items, r)
        slow.append(items[r])

    def first_items(r):
        last = r + 1 == RO
        n = 1 if last else NT
        turned(0, n)
        act(t("Yr", 256, 256 + 32 * n), t("pY", 0, 32 * n), bias=-1024.0)
        for b in range(2):
            woff(0, b, n)
        if last:
            cp(ind(t("spare"), t("wo", 16, 18)), t("Yr", 256, 288))
            for lo in (0, 3072):
                dma("Y", "d_o1", outside(T.yx[:, lo:lo + 1024]), t("spare", lo, lo + 1024))
            return
        act(t("Yr", 512, 528), t("pY", 0, 256, 16), bias=-1024.0)
        mark(("read", r))
        ts(t("w6"), t("si", 0, 1), 63, AND)
        ts(t("wo", 32, 33), t("w6"), t("pev"), Op.mult, t("padb"), Op.add)

    def write_first(r):
        join(items[r])
        cp(ind(t("tab", 4096), t("wo", 32, 33)), t("Yr", 512, 528))
        for k in range(1, NT, 2):
            lo, hi = 16 + 2 * k, min(20 + 2 * k, 32)
            cp(ind(t("tab", TW * k, TW * min(k + 2, NT)), t("wo", lo, hi)), t("Yr", 16 * lo, 16 * hi))

    def thresholds():
        cp(t("Ai"), t("pC", 64, 65))
        ts(t("Aj"), t("Ai"), 31, AND)
        ts(t("ncol"), t("Aj"), -1.0, Op.mult, t("nT"), Op.add)
        ts(t("thr"), t("gm"), t("ncol"), Op.mult, 0.0625, Op.mult)

    def tail1(r, first):
        last = r + 1 == RO
        compare(1, 3, 4, "S")
        call(lambda: free.insert(0, True))
        join(first)
        if r == 0:
            for k in range(NT):
                act(t("tab", TW * k + 4096, TW * k + TW), t("tab", TW * k, TW * k + 64))
        if not last:
            w = fork(write_first, r)
        choose(1)
        for b in range(4):
            mm(t("pC", 64, 65), t("BD"), t("hot", b, b + 1), b == 0, b == 3)
        pick(1, 0, 4)
        act(t("SA", 4 * r, 4 * r + 1), t("pC", 64, 65), bias=-32.0 if last else 0.0)
        send("SA", "LB", 4 * r, 4 * r, ((0, 0, 1, 1),), "rc%d" % r, FAR_A)
        if last:
            o = fork(out_rest, r, 0)
        cp(t("EtU", 32, 64), ind(t("E", 512, 1024), t("koff", 4, 6)))
        act(t("kA"), t("pC", 64, 65), scale=32.0, bias=CC)
        if not last:
            must.append(fork(thresholds))
        s = fork(pairs, r, 1, False, at=1)
        best(1, 16 if last else BEST_S[1])
        if last:
            a = fork(anchors, r, 1, at=0)
            join(items[r])
            weigh(1)
            turned(1, 1)
            places(1)
            act(t("Yr", 0, 32), t("pY", 0, 32), bias=-1024.0)
            for b in range(2):
                woff(1, b, 1)
            cp(ind(t("tab", 0, 4096), t("wo", 0, 2)), t("Yr", 0, 32))
            for x in (s, a):
                join(x)
            call(lambda: ENG["Y"].wait_ge(T.sem.lo, total["lo"]))
            dma("Y", "d_o2", outside(T.yx[:, 1024:3072]), t("tab", 1024, 3072))
            for x in (o, got[(r, 0)], got[(r, 1)]):
                join(x)
            dma("S", "d_o2", outside(T.yl[:, :]), t("ylf"))
            out_rest(r, 1)
            return
        weigh(1)
        join(items[r])
        until(("read", r))
        turned(1, NT)
        a = fork(lambda: (anchors(r, 1), join(s), fork(landed, r, 1)), at=1)
        o = fork(lambda: (join(named[r]), offsets(0, NT, t("LB", 4 * r, 4 * r + 1), range(4, 8))), at=1)
        places(1)
        for b in range(2):
            woff(1, b, NT)
        for lo, bank in ((128, "pY"), (0, "pD0")):
            act(t("Yr", lo, lo + 128), t(bank, lo, lo + 128), bias=-1024.0)
        join(w)
        cp(ind(t("tab", 0, 4 * TW), t("wo", 8, 18)), t("Yr", 128, 288))
        if r + 2 == RO:
            for lo in (0, 3072):
                dma("Y", "d_sp", t("spare", lo, lo + 1024), t("tab", lo, lo + 1024))
        join(o)
        e = fork(early)
        cp(ind(t("tab", 4 * TW, NT * TW), t("wo", 0, 8)), t("Yr", 0, 128))
        offsets(0, NT, t("LB", 4 * r, 4 * r + 1), range(4))
        join(e)
        call(lambda: begin(r + 1))
        open_half(0, NT)

    def begin(r):
        for h in range(2):
            chunks.extend([((h, n, l), 2 * r + h + 1, NT if r else COPIES[4 * h + n]) for n in range(4) for l in range(16)
                           if r or h or n not in raw])
        keep = {}

        def end0():
            keep[0] = stream(tail0, r)
            streams.insert(TAIL_AT, keep[0])
        after[(0, "pD0")] = lambda: streams.insert(0, stream(lambda: (until("constants"), compare(0, 0, 3, "V"), mark(("counted", r)))))
        after[(0, "pD1")] = end0
        after[(1, "pD0")] = lambda: streams.insert(0, stream(lambda: (until(("chosen", r)), compare(1, 0, 3, "V"))))
        after[(1, "pD1")] = lambda: streams.insert(0, stream(lambda: ([join(s) for s in list(streams) if not any(s is x for x in slow)],
                                                                      tail1(r, keep[0]))))

    names_start(0)
    for q, s, n in RUNS:
        ts(t("L16", q, q + n), t("lsi", s, s + n), -2048.0, Op.add)
    for q, s, n in RUNS:
        ts(t("anf", q, q + n, p1=8), t("ani", s, s + n, p1=8), -2048.0, Op.add)
    ts(t("anf", 64, 65, p1=8), t("thi", p1=8), -2048.0, Op.add)
    for q, s, n in RUNS:
        act(t("zr", q, q + n), t("zi", s, s + n))
    names(0)
    for c in range(4):
        mm(t("pU", 32 * c, 32 * c + 32), t("sel", p1=8), t("anf", 32 * (c // 2), 32 * (c // 2) + 32, p1=8))
    mm(t("pU", 128, 129), t("sel", p1=8), t("anf", 64, 65, p1=8))
    act(t("C2"), t("pU", 0, 128), scale=32.0, bias=CC + 65536.0)
    act(t("nT"), t("pU", 128, 129), scale=-1.0, bias=1785.0 - 2048.0)
    for j in range(1, 4):
        mm(t("pZ", 64 * j, 64 * j + 64), turn(4 * j), t("zr", 0, 64))
    act(t("zn"), t("zr", 0, 32), scale=-1.0)
    act(t("zh"), t("zr", 0, 64), scale=0.5, bias=1023.75)
    act(t("zq", 0, 64), t("zr", 0, 64), scale=0.5)
    act(t("zr", 64, 256), t("pZ", 64, 256))
    act(t("zq", 64, 256), t("pZ", 64, 256), scale=0.5)
    spread("pY", t("zr", 0, 32), True)
    names_start(1)
    names_end(0, t("C2", 0, 64), 64)
    cp(t("off", 0, 64), t("E", 0, 64))
    raw = [n for n in (0, 2, 1) if COPIES[n] == 1]
    RAW = [(256 * (n % 2) + 128 * (n // 2), 256 * (n % 2) + 128 * (n // 2) + 128) for n in raw]
    cp(t("off", 64, RAW[-1][1]), t("E", 64, RAW[-1][1]))

    def sums(src, w, lo, hi):
        def go():
            for j in range(lo // 8, hi // 8):
                dist((0, 2 * (j % 32 // 16) + j // 32, j % 16), src, 128 * j, (w, 1))
        call(go)

    def raw_gathers():
        todo = [c for lo, hi in RAW for c in range(lo, hi, 64)]
        for j, lo in enumerate(todo):
            act(t("rx", 16 * lo, 16 * lo + 1024), ind(t("tab", 0, 4096), t("off", lo, lo + 64)))
            mark(("raw", lo))
            if j:
                until("first")
                sums("rx", 16, todo[j - 1], todo[j - 1] + 64)
        sums("rx", 16, lo, lo + 64)

    def raw_sums():
        for lo, hi in RAW:
            for c in range(lo, hi, 64):
                until(("raw", c))
            for i in range(16):
                tt(t("rm", 16 * lo + i, 16 * hi, 16), t("rx", 16 * lo + i, 16 * hi, 16), t("pY", lo, hi), Op.max)
            sums("rm", 8, lo, hi)

    def first_sums():
        late_constants()
        mm(t("pD0", 0, 384), t("oneh"), t("thr"), True, False)
        for n in raw:
            mm(t("pD0", 128 * n, 128 * n + 128), t("oneh"), t("zm", 128 * n, 128 * n + 128), False, False)
        left[(0, "pD0")] = 96
        mark("first")
        first_offsets(0)
        open_half(0, 4)
        mark("open")

    def first_offsets(h):
        if h:
            offsets(1, COPIES[7])
        for n in range(4):
            lo, k = 512 * h + 256 * (n % 2) + 128 * (n // 2), COPIES[4 * h + n]
            for b in range(k if k != COPIES[7 * h] else 0):
                ts(t("off", lo + b, lo + 128, k), t("E", lo + b, lo + 128, k), float(TW * (k - 1 - b)), Op.add)

    def second_names():
        names(1)
        names_end(1, t("C2", 64, 128))
        first_offsets(1)
        tail_constants()
        mark("constants")
        until("open")
        open_half(1, 4)

    begin(0)
    streams.extend([stream(raw_sums), stream(first_sums), stream(raw_gathers), stream(second_names)])
    run()
    for s in sorted(total):
        g.wait_ge(T.sem[s], total[s])
